import numpy as np, ml_dtypes
CORES = [48,51,52,55]
N = 4
import mx_ref
BF = ml_dtypes.bfloat16
def gcols(t, e):
    v = np.concatenate([t.reshape(8, 16, -1, 4), np.zeros((8, 16, 1, 4), BF)], axis=2)
    return np.ascontiguousarray(np.stack([v[g][:, e[g]] for g in range(8)])).reshape(128, -1)
def cut(t, i, w=512):
    return t[:, w * i:w * i + w]
def pick(q, e):
    c = np.concatenate([q[0].reshape(128, -1, 4), np.zeros((128, 1, 4), np.uint8)], axis=1); s = np.concatenate([q[1], np.ones((16, 1), np.uint8)], axis=1)
    return (np.ascontiguousarray(c[:, e].reshape(128, -1)), np.ascontiguousarray(s[:, e]))
def join(*qs):
    return (np.concatenate([q[0] for q in qs], axis=1), np.concatenate([q[1] for q in qs], axis=1))
def put(q, e, v):
    c, s = q[0].reshape(128, -1, 4).copy(), q[1].copy(); c[:, e] = v[0].reshape(128, -1, 4); s[:, e] = v[1]
    return (c.reshape(128, -1), s)
def pk(c, s):
    return (np.ascontiguousarray(c), mx_ref.live(s))
def emit(q):
    return q[0], q[1]
def packed(v, rng):
    q = [mx_ref.quantize(np.ascontiguousarray(v[r])) for r in range(N)]
    return np.stack([a for a, b in q]), np.stack([mx_ref.plane(b, rng) for a, b in q])
def values_of_codes():
    e, c = np.zeros((128, 128, 4), np.float32), np.zeros((128, 2, 4), np.uint8)
    e[np.arange(128), np.arange(128), 0] = 1
    c[:127, :, 0] = np.arange(256).reshape(2, 128).T[:127]
    return mx_ref.matmul(mx_ref.quantize(e.reshape(128, 512).astype(BF)), (c.reshape(128, 8), np.full((16, 2), 127, np.uint8))).T.reshape(-1).astype(np.float64)
CODE_VALUE, SCALE_VALUE = values_of_codes(), 2.0 ** (np.arange(256) - 127.0)
def decode(q):
    return (CODE_VALUE[q[0]].reshape(16, 8, -1, 4) * SCALE_VALUE[q[1]][:, None, :, None] + 0.0).reshape(128, -1).astype(np.float32)
def f(rng, *shape):
    return mx_ref.flush((rng.standard_normal(shape, dtype=np.float32) * np.exp2(rng.integers(-2, 3, shape[:-1] + (1,)))).astype(BF))
def wide(rng, *shape, cols=0):
    v = rng.standard_normal(shape, dtype=np.float32) * np.exp2(rng.integers(-12, 13, shape)).astype(np.float32)
    if cols: v *= np.repeat(np.exp2(rng.integers(-cols, cols + 1, shape[:-2] + (1, shape[-1] // 4))) * (rng.random(shape[:-2] + (1, shape[-1] // 4)) > 0.0625), 4, axis=-1).astype(np.float32)
    return mx_ref.flush(v.astype(BF))
C, S, L, R = 384, 48, 8, 3
def layer(lay, q, k):
    return np.stack([np.maximum(mx_ref.matmul(w, q), np.float32(0.0)) * np.float32(k) for w in lay], axis=2).reshape(128, -1)
def seams(e):
    e = e.reshape(N, 8, S, L)
    m, back = e[:, 0], []
    for g in range(1, 8):
        w = np.pad(m, ((0, 0), (0, 0), (1, 1)), constant_values=np.inf)
        three = np.stack([w[:, :, :-2], m, w[:, :, 2:]])
        back.append(np.argmin(three, axis=0) + np.arange(L) - 1)
        m = np.maximum(e[:, g], np.min(three, axis=0))
    p = [np.argmin(m, axis=2)]
    for b in back[::-1]: p.insert(0, np.take_along_axis(b, p[0][:, :, None], axis=2)[:, :, 0])
    return np.stack(p, axis=1) + L * np.arange(S), np.min(m, axis=2)
def edited(p, dear):
    key = np.concatenate([np.tile(2 * np.arange(C), (8, 1)), 2 * p + 1], axis=1)
    gone = np.zeros((8, C + S), bool)
    gone[:, C:] = ~dear
    np.put_along_axis(gone, p, gone[:, C:].copy(), axis=1)
    return np.argsort(np.where(gone, 2 * C, key), axis=1, kind="stable")[:, :C + S - 2 * np.count_nonzero(~dear)]
def numbers_of(rng):
    return {"x": np.array(f(rng, N, 128, 4 * C)), "u": np.array(f(rng, N, 128, 512)), "v": np.array(f(rng, N, 128, 512))}
def weights(w, rng):
    c, p = packed(np.stack([w] * N), rng)
    return {"wc": c, "ws": p}
def unit(k, rng, fill=False):
    w = np.zeros((128, 4, 128, 4), np.float32)
    i = np.arange(128)
    for b in range(4): w[i, b, i, b] = k
    if fill:
        h = np.arange(0, 128, 16)
        w[h + 2, 0, h + 2, 0] = 0
        w[h, 0, h + 2, 0] = k
    return weights(w.reshape(128, 2048).astype(BF), rng)
def setup_inputs(rng):
    return {**numbers_of(rng), **weights(f(rng, 128, 2048), rng)}
def setup_inputs_ties(rng):
    d = numbers_of(rng)
    o = rng.permutation(N)
    x = d["x"].reshape(N, 8, 16, C, 4)
    a = x[0, :, :8, :3].copy()
    a[:, :, 2] = 0
    for r in range(N):
        for g in range(8):
            k = np.zeros(C, int) if r == o[0] else np.minimum(rng.permutation(C) % 4, 2)
            x[r, g, :8] = a[g][:, k]
    x[o[1], :, :8] = 0
    u = d["u"].reshape(N, 8, 16, 128, 4)
    w = np.array(f(rng, 128, 2048)).reshape(8, 16, 4, 8, 16, 4)
    for g in range(8):
        a = u[0, g, :8, 16 * g].copy()
        u[:, :, :, 16 * g] = 0
        u[:, g, :8, 16 * g] = a
        a = w[g, :8, :, g, :8].copy()
        w[:, :, :, g, :8] = 0
        w[g, :8, :, g, :8] = a
    return {"x": x.reshape(N, 128, 4 * C), "u": u.reshape(N, 128, 512), "v": d["v"], **weights(w.reshape(128, 2048), rng)}
def setup_inputs_near(rng):
    d = numbers_of(rng)
    x = d["x"].astype(np.float32).reshape(N, 8, 16, C, 4)
    s = rng.integers(0, 256, (N, 8, C))
    g = ((s[..., None] >> np.arange(8)) & 1) * np.exp2(np.arange(8) - 30.0)
    x[:, :, 0] = 0
    x[:, :, 0, :, 0] = 2.0 ** -7
    x[:, :, 1:8] = rng.integers(4, 8, (N, 8, 7, C, 4)) * rng.choice([-1.0, 1.0], (N, 8, 7, C, 4)) * 2.0 ** -9
    x[:, :, 1:3] = 0
    x[:, :, 1, :, 0] = 2.0 ** -16
    x[:, :, 8] = g[..., :4]
    x[:, :, 9] = g[..., 4:]
    x[:, :, 10:] = rng.integers(4, 8, (N, 8, 6, C, 4)) * rng.choice([-1.0, 1.0], (N, 8, 6, C, 4)) * 2.0 ** -27
    k = np.where(np.arange(N) < N // 2 - 1, 1.0, 2.0 ** -30).astype(np.float32).astype(BF)
    j = L * int(rng.integers(S))
    x[int(rng.integers(N // 2 - 1)), :, 0, j:j + L, 0] = 2.0 ** 27
    u = d["u"].reshape(N, 128, 128, 4)
    u[:, :, ::16] = 0
    for h in range(0, 128, 16):
        u[:, h:h + 2, h, 0] = k[:, None]
        u[:, h + 8:h + 10, h] = k[:, None, None]
        u[N // 2 - 1, h + 2, h, 0] = k[N // 2 - 1]
    return {"x": x.reshape(N, 128, 4 * C).astype(BF), "u": u.reshape(N, 128, 512), "v": d["v"], **unit(32, rng, True)}
def setup_inputs_huge(rng):
    d = numbers_of(rng)
    x = 2.0 ** 30 * (0.85 + 0.15 * rng.random((N, 128, C, 4)))
    x[N // 2:] -= 2.0 ** 28
    c = np.stack([rng.permutation(C) % 2 * 2.0 - 1.0 for r in range(N)])
    c[rng.permutation(N) < N // 2] = -1
    x *= c[:, None, :, None]
    s = np.stack([rng.permutation(8) % 2 * 2.0 - 1.0 for r in range(N)])
    u = d["u"].reshape(N, 128, 128, 4)
    u[:, :, ::16] = (2.0 ** 30 * (1 - 0.1 * rng.random((N, 128, 8, 4))) * s[:, None, :, None]).astype(np.float32).astype(BF)
    return {"x": x.astype(np.float32).reshape(N, 128, 4 * C).astype(BF), "u": u.reshape(N, 128, 512), "v": d["v"], **unit(-16, rng)}
def setup_inputs_caps(rng):
    d = numbers_of(rng)
    x = d["x"].astype(np.float32).reshape(N, 8, 16, C, 4)
    e = 1 + rng.random((N, 8, C))
    g = np.arange(8)[:, None]
    for r in range(N):
        k, a = rng.permutation(S) % 4, rng.integers(0, L - 7, S)
        way = np.where(k == 0, a + g, np.where(k == 1, a + 7 - g, np.where(k == 2, 0, L - 1))) + L * np.arange(S)
        np.put_along_axis(e[r], way, 2.0 ** -4, axis=1)
    x[:, :, 0] = 0
    x[:, :, 0, :, 0] = e
    k = np.where(np.arange(N) < N // 2, 2.0 ** -12, 1.0)
    s = np.stack([rng.permutation(8) % 2 * 2.0 - 1.0 for r in range(N)])
    u = d["u"].reshape(N, 128, 128, 4)
    u[:, :, ::16] = 0
    for h in range(0, 128, 16): u[:, h, h, 0] = (k * s[:, h // 16]).astype(np.float32).astype(BF)
    return {"x": mx_ref.flush(x.reshape(N, 128, 4 * C).astype(BF)), "u": u.reshape(N, 128, 512), "v": d["v"], **unit(32, rng)}
def setup_inputs_spread(rng):
    d = setup_inputs(rng)
    d["x"] = wide(rng, N, 128, 4 * C, cols=6)
    return d
def check_inputs(d):
    b = []
    for k in ("x", "u", "v"):
        a = np.abs(d[k].astype(np.float32))
        if not (np.isfinite(a).all() and ((a == 0) | (a >= 2.0 ** -30) & (a <= 2.0 ** 30)).all()): b.append("a value of " + k)
    if (d["wc"] != d["wc"][:1]).any(): b.append("wc differs between ranks")
    s = [mx_ref.live(p) for p in d["ws"]]
    if any((p != s[0]).any() for p in s): b.append("ws differs between ranks")
    if (d["wc"] % 128 == 127).any(): b.append("wc: a code that is no number")
    with np.errstate(over="ignore"):
        a = np.abs(decode(pk(d["wc"][0], d["ws"][0])))
    if not ((a == 0) | (a >= 2.0 ** -30) & (a <= 2.0 ** 30)).all(): b.append("a number of W")
    return b
def reference(x, u, v, wc, ws):
    q = pk(wc[0], ws[0])
    lay = [pick(q, np.arange(128 * b, 128 * b + 128)) for b in range(4)]
    qu = [mx_ref.quantize(u[r]) for r in range(N)]
    now = [x[r] for r in range(N)]
    for t in range(R):
        held, e = [], np.zeros((N, 8, C), np.float32)
        for r in range(N):
            q = mx_ref.quantize(now[r])
            held.append(decode(q).astype(BF))
            e[r] = np.abs(mx_ref.matmul(qu[r], q)[::16])
        p, cost = seams(e)
        dear = np.ones(N * S, bool)
        dear[np.argsort(cost.reshape(-1), kind="stable")[:N * S // 2]] = False
        dear = dear.reshape(N, S)
        row = []
        for r in range(N):
            h = layer(lay, mx_ref.quantize(gcols(held[r], p[r])), 0.03125).astype(BF)
            row.append(gcols(np.concatenate([held[r], h], axis=1), edited(p[r], dear[r])))
        row = np.concatenate(row, axis=1)
        for r in range(N):
            q = mx_ref.quantize(np.ascontiguousarray(cut(row, r, 4 * C)))
            now[r] = (decode(q) + layer(lay, q, 0.015625)).astype(BF)
    y, ol = np.zeros((N, 128, C), np.float32), np.zeros((N, 8, S), np.float32)
    oc, osc = np.zeros((N, 128, 4 * C), np.uint8), np.zeros((N, 16, C), np.uint8)
    for r in range(N):
        q = mx_ref.quantize(now[r])
        y[r] = mx_ref.matmul(mx_ref.quantize(v[r]), q)
        ol[r] = p[r]
        oc[r], osc[r] = emit(q)
    return {"y": y, "ol": ol, "oc": oc, "osc": osc}

@@ -1,0 +1,680 @@
+from concourse.bass import DstId, RemoteDMATransfer
+from concourse.mybir import dt, AluOpType, AxisListType, ActivationFunctionType
+
+ALU = AluOpType
+ACT = ActivationFunctionType
+C, S, L, R, N = 384, 48, 8, 3, 4
+BIG = 1.0e29
+FLOOR = 2.0 ** -100
+MAGIC = 12582912.0
+PW = 432
+XW = 320
+HX = 160
+B0 = 528
+ZC = B0 + 128
+F32, BF, I32, U16, CODE, PLANE = "float32", "bfloat16", "int32", "uint16", "float8_e4m3fn_x4", "uint8"
+WIDTH = {F32: 4, BF: 2, I32: 4, U16: 2, CODE: 4, PLANE: 1}
+
+SCRATCH = {"ps": ("psum", [128, 4096], F32)}
+
+
+def _buf(dtype, **kw):
+    for k, n in kw.items():
+        SCRATCH[k] = ("sbuf", [128, n], dtype)
+
+
+_buf(BF, xin=1536, uin=512, vin=512, xt=1536, fb=4 * PW, fe=4 * XW, zt=4 * ZC, vt=512, ve=512, st=512, eb=2048,
+     mv=512, zer=512, fl32=32, frow=128, fone=128)
+_buf(CODE, tn=384, tq=512, tf=384, uq=128, vq=128, wq=512, eq=512, mq=128, sq=128, vcq=128, veq=128, zq=ZC, gq=384,
+     bq=192, lq0=224, lq1=224, lq2=224)
+_buf(PLANE, tns=384, tqs=512, tfs=384, uqs=128, vqs=128, wqs=512, eqs=512, mqs=128, sqs=128, vcqs=128, veqs=128,
+     zqs=ZC, gqs=384, bqs=192, lq0s=224, lq1s=224, lq2s=224)
+_buf(F32, kc=56, e=80, m=80, t1=80, m3=80, ca=72, cb=72, tau=72, ctau=72, pm=8, mc=12, acc=8, dump=64, msg=4, sp=64,
+     prow=76, oa=192, ox=160, bown=24, bext=16, pin=64, pt=64, pe=64, kt=256, ki=128, inr=256, row=256, cg=32, ct=32,
+     cmp=256, cnt=4, c96=32, z32=32, c98=128, pos=132, t7=68, th=68, cl=204, sums=8, lo=8, dk=96, xr=96,
+     rr=96, mm5=120, tmp=1536, ysb=384, olb=48, o8=48, io1=128, w0=24, w3=8, w4=8, w5=8, w6=8, w7=8, w8=8,
+     thp=4, cl0=16, cl1=16, cl2=16, pl0=8, pl1=8, pl2=8)
+_buf(I32, pi=8)
+_buf(U16, l0=24, lf=24, lb=12, lv=4, lve=2, lz=24, lzx=16, lp=2, lc=2, ls=6, lm=24, lfo=4, lfx=2)
+
+SEMAPHORES = ["cv", "cs", "cp", "cg", "dx", "dx2", "du", "dv", "dw", "dws", "dol", "dy", "doc", "dos"] + [
+    "%s%d" % (k, t) for t in range(R) for k in ("ac", "as", "ak", "ap", "sc", "ss", "sk", "sp")]
+COUNTER = {"v": "cv", "s": "cs", "p": "cp", "g": "cg"}
+CY, GAT, WAKE, PE, HOP, DMA = 1.0, 1.3, 50.0, 0.6, 2500.0, 2000.0
+FINE = ("oa", "ox", "tq", "m", "mc", "cmp", "cnt", "gq", "gqs", "xt", "tmp", "ca", "cb", "tau", "th", "rr", "mm5", "cl",
+        "pe", "fb", "fe")
+AHEAD = {'lz<oa144': 1500, 'lz': 1500, 'oa144': 1500, 'tq192': 2500, 'msg': 3100, 'mc0': 800, 'gqs0<zqsi': 300,
+         'cmp128': 2000, 'kt': 1200, 'vq': -2000, 'lve': 300, 'lf<bown': -300, 'eqlq': 2000, 'xt0': 800, 'vcq': 500,
+         'mm596': -2000, 'eq': -300, 'bext<io1': -2000, 'lzx<ox': 800, 'bq<tqi': 300, 'mq': 500, 'dk': -800,
+         'ctau<ctau': 2000, 'c98': 300, 'z32': 2000, 'm41': 300, 'm3': -300, 'oa48<oa': 300, 'w8<w8': 300,
+         'cmp0': -300, 'lq2s': 800, 'eb': 2000, 'fe320<ps': -800, 'wqve': 2000, 'e': -300, 'oa96': 2000, 'lp': 300,
+         'tmp384<ps': 2000, 'l0': -800, 'fone': 300}
+SPARE = {'zt<fe': 1000, 'zt<fb': 0, 'o8<io1': 0, 'st<sp': 0, 'zt<zer': 300, 'zt<fbi': 0, 'inr<kt': 300,
+         'fe160<zer': -100, 'ox16<ox': -100, 'cg<rowi': -100, 'oa24<oa': 1000, 'sums<sums': 1000, 'sp<sp': -100,
+         'ox80<ox': 1000, 'vt<zer': -100}
+
+
+def A(name, c0=0, c1=None, step=1, p0=0, p1=128, ind=None, cast=None):
+    if c1 is None:
+        c1 = SCRATCH[name][1][1]
+    return (name, c0, c1, step, p0, p1, ind, cast)
+
+
+def col(name, c, p0=0, p1=128):
+    return A(name, c, c + 1, 1, p0, p1)
+
+
+def size(a):
+    return (a[2] - a[1] + a[3] - 1) // a[3]
+
+
+def name(a):
+    return a[0] + (str(a[1]) if a[0] in FINE else "")
+
+
+def clash(a, b):
+    if a[0] == "ps":
+        return a[1] // 512 <= (b[2] - 1) // 512 and b[1] // 512 <= (a[2] - 1) // 512
+    if a[5] <= b[4] or b[5] <= a[4] or a[2] <= b[1] or b[2] <= a[1]:
+        return False
+    return not (a[3] == b[3] and a[3] > 1 and (a[1] - b[1]) % a[3] != 0)
+
+
+def schedule(ops):
+    n = len(ops)
+    after, prio = [[] for o in ops], [0.0] * n
+    for i in range(n - 1, -1, -1):
+        prio[i] = min(ops[i]["cost"].values()) + max(
+            [prio[j] + (0.0 if i in ops[j]["order"] else ops[i]["lat"] + WAKE) for j in after[i]] + [ops[i]["lat"]])
+        for j in ops[i]["deps"]:
+            after[j].append(i)
+    prio = [prio[i] + AHEAD.get(ops[i]["tag"], 0.0) for i in range(n)]
+    left, at = [len(o["deps"]) for o in ops], [0.0] * n
+    ready = [i for i in range(n) if not left[i]]
+    free, done, order = {}, [0.0] * n, []
+    while ready:
+        cand = []
+        for i in ready:
+            pen = SPARE.get(ops[i]["tag"], 100)
+            q = min((max(at[i], free.get(q, 0.0)) + c_ + (pen if q == "v" else 0.0), q) for q, c_ in ops[i]["cost"].items())[1]
+            end = max(at[i], free.get(q, 0.0)) + ops[i]["cost"][q]
+            cand.append((end, q, i, end - ops[i]["cost"][q]))
+        end, q, i, t = min(cand)
+        end, q, i, t = max([x for x in cand if x[1] == q and x[3] < end] + [(end, q, i, t)], key=lambda x: prio[x[2]])
+        free[q], done[i] = end, end + ops[i]["lat"]
+        order.append((i, q))
+        ready.remove(i)
+        for j in after[i]:
+            at[j] = max(at[j], end if i in ops[j]["order"] else done[i] + WAKE)
+            left[j] -= 1
+            if not left[j]:
+                ready.append(j)
+    return order, done
+
+
+def rank_program(g, core, T, topo):
+    r = T.rank_of(core)
+    if r is None:
+        return
+    eng = {"v": g.vector, "s": g.scalar, "p": g.tensor, "g": g, "y": g.sync}
+    ops, touched, last_g = [], {}, []
+
+    def X(a):
+        if not isinstance(a, tuple):
+            return a
+        t = T[a[0]][a[4]:a[5], a[1]:a[2]:a[3]] if a[3] > 1 else T[a[0]][a[4]:a[5], a[1]:a[2]]
+        if a[7] is not None:
+            t = t.bitcast(a[7])
+        if a[6] is not None:
+            t = t.indirect(X(a[6]))
+        return t
+
+    def emit(fns, cost, outs, ins, sem=None, inc=1, chain=True, lat=0.0, soft=(), tag=None):
+        rd = [a for a in ins if isinstance(a, tuple)]
+        rd += [a[6] for a in rd if a[6] is not None]
+        i, hard = len(ops), set()
+        for a, w in [(a, True) for a in outs] + [(a, False) for a in rd]:
+            for j, b, wb in touched.get(a[0], []):
+                if (w or wb or (a[0] == "ps" and (len(fns) > 1 or ops[j]["cost"].keys() != cost.keys()))) and clash(a, b):
+                    hard.add(j)
+        for a, w in [(a, True) for a in outs] + [(a, False) for a in rd]:
+            touched.setdefault(a[0], []).append((i, a, w))
+        soft = set(soft)
+        if "g" in fns:
+            if last_g and ops[last_g[-1]]["sem"] is None:
+                hard.add(last_g[-1])
+            soft |= set(last_g[-1:])
+            last_g.append(i)
+        ops.append({"fns": fns, "cost": cost, "hard": hard, "deps": hard | soft,
+                    "order": set() if "x" in fns else soft - hard, "sem": sem, "inc": inc, "chain": chain,
+                    "lat": lat, "tag": tag or (name(outs[0]) if outs else sem[:2])})
+        return i
+
+    def price(out, in_, k=1.0):
+        if in_[6] is not None:
+            return 55.0 + GAT * size(out)
+        if WIDTH[SCRATCH[out[0]][2]] == 2 and WIDTH[SCRATCH[in_[0]][2]] == 2:
+            k = 0.5
+        return CY * max(64.0, k * size(in_))
+
+    def vec(fn, outs, ins, k=1.0):
+        emit({"v": fn}, {"v": price(outs[0], ins[0], k)}, outs, ins)
+
+    def either(q, fv, fs, out, ins):
+        tag = name(out) + '<' + ins[0][0] + ('i' if ins[0][6] else '')
+        cv, cs = price(out, ins[0]), max(price(out, ins[0]), CY * size(out))
+        fns, cost = {"v": fv, "s": fs}, {"v": cv, "s": cs}
+        emit({k: fns[k] for k in q}, {k: cost[k] for k in q}, [out], ins, tag=tag)
+
+    def ts(out, in0, s1, op0, s2=None, op1=None):
+        if op1 is None:
+            vec(lambda e: e.tensor_scalar(X(out), X(in0), X(s1), None, op0), [out], [in0, s1])
+        else:
+            vec(lambda e: e.tensor_scalar(X(out), X(in0), X(s1), X(s2), op0, op1), [out], [in0, s1, s2])
+
+    def tt(out, a, b, op):
+        vec(lambda e: e.tensor_tensor(X(out), X(a), X(b), op), [out], [a, b], 1.0 if a[0] == "ps" else 2.0)
+
+    def act(out, in_, func, bias=0.0, scale=1.0, accum=None):
+        c_ = {"s": CY * max(64.0, size(in_)) + (20.0 if accum else 0.0)}
+        if accum is None:
+            emit({"s": lambda e: e.activation(X(out), X(in_), func, bias=X(bias), scale=X(scale))}, c_, [out],
+                 [in_, bias, scale])
+        else:
+            emit({"s": lambda e: e.activation(X(out), X(in_), func, bias=X(bias), scale=X(scale), accum_out=X(accum))},
+                 c_, [out, accum], [in_, bias, scale])
+
+    def cp(q, out, in_):
+        either(q, lambda e: e.tensor_copy(X(out), X(in_)), lambda e: e.activation(X(out), X(in_), ACT.Copy), out, [in_])
+
+    def aff(q, out, in_, mul, add):
+        either(q, lambda e: e.tensor_scalar(X(out), X(in_), X(mul), X(add), ALU.mult, ALU.add),
+               lambda e: e.activation(X(out), X(in_), ACT.Identity, bias=X(add), scale=X(mul)), out, [in_, mul, add])
+
+    def relu(q, out, in_, k):
+        either(q, lambda e: e.tensor_scalar(X(out), X(in_), 0.0, k, ALU.max, ALU.mult),
+               lambda e: e.activation(X(out), X(in_), ACT.Relu, scale=k), out, [in_])
+
+    def fill(out, v):
+        emit({"v": lambda e: e.memset(X(out), v)}, {"v": price(out, out)}, [out], [])
+
+    def tr(out, in_):
+        vec(lambda e: e.transpose(X(out), X(in_)), [out], [in_])
+
+    def scan(out, d0, d1, init, op0, op1):
+        vec(lambda e: e.tensor_tensor_scan(X(out), X(d0), X(d1), X(init), op0, op1), [out], [d0, d1, init])
+
+    def red(out, in_, op):
+        vec(lambda e: e.tensor_reduce(X(out), X(in_), AxisListType.X, op), [out], [in_])
+
+    def iota(out, pat, base=0, cm=0):
+        c_ = {"g": 130.0 + 2 * CY * size(out)}
+        if SCRATCH[out[0]][2] == I32:
+            emit({"g": lambda e: e.iota(X(out), pat, base, cm)}, c_, [out], [])
+        else:
+            emit({"g": lambda e: e.iota(X(out), pat, base, cm, allow_small_or_imprecise_dtypes=True)}, c_, [out], [])
+
+    def quant(name_, c0, c1, src, e0):
+        o, s_, i_ = A(name_, c0, c1), A(name_ + "s", c0, c1), A(src, e0, e0 + 4 * (c1 - c0))
+        emit({"v": lambda e: e.quantize_mx(X(o), X(s_), X(i_))}, {"v": 12.0 + 0.27 * size(i_)}, [o, s_], [i_])
+
+    def mm(bank, w, w0, x, x0, n, soft=()):
+        o = A("ps", 512 * bank, 512 * bank + n)
+        a, a_, b, b_ = A(w, w0, w0 + 128), A(w + "s", w0, w0 + 128), A(x, x0, x0 + n), A(x + "s", x0, x0 + n)
+        return emit({"p": lambda e: e.matmul_mx(X(o), X(a), X(a_), X(b), X(b_), True, True)}, {"p": PE * (n + 16)},
+                    [o], [a, a_, b, b_], soft=soft, tag=w + x[:2])
+
+    def pick(dst, d0, n, src, w, lst):
+        cp("v", A(dst, d0, d0 + n, cast=dt.uint32), A(src, 0, w, ind=lst, cast=dt.uint32))
+        cp("s", A(dst + "s", d0, d0 + n), A(src + "s", 0, w, ind=lst))
+
+    def dma(q, out, in_, sem, lat=DMA, more=()):
+        emit({q: lambda e: e.dma_start(X(out), X(in_))}, {q: 60.0}, [a for a in [out] if isinstance(a, tuple)],
+             [in_] + list(more), sem, 16, True, lat)
+
+    def remote(moves, rsem, lsem, lands, inc, hop=HOP):
+        n_ = len(moves)
+        trs, tot = [], 0
+        for i, (src, dst, ranks) in enumerate(moves):
+            es = [x for x in topo.engines(core, T.cores[ranks[0]])
+                  if all(x in topo.engines(core, T.cores[k]) for k in ranks)]
+            es = es[i * len(es) // n_:(i + 1) * len(es) // n_]
+            ids = [DstId(rid=topo.addr(T.cores[k])[0], pnc=topo.addr(T.cores[k])[1]) for k in ranks]
+            trs.append(RemoteDMATransfer(dst_ids=ids, dma_engine_mask=sum(1 << x for x in es), remote_sem=T.sem[rsem],
+                                         srcs=[X(src)], dsts=[X(dst) for k in ranks]))
+            tot += len(es)
+        i = emit({"g": lambda e: e.remote_dma_fused(trs, local_sem=T.sem[lsem])}, {"g": 300.0}, [],
+                 [m_[0] for m_ in moves], lsem, tot, False, hop)
+        emit({"x": None}, {"x": 0.0}, [lands], [], rsem, inc, False, 0.0, [i])
+
+    def share(k):
+        return len(topo.engines(T.cores[k], core)) // (2 if 0 < k < N - 1 else 1)
+
+    def ps(bank, c0, c1, step=1):
+        return A("ps", 512 * bank + c0, 512 * bank + c1, step)
+
+    left, right = (r - 1 if r > 0 else None), (r + 1 if r < N - 1 else None)
+    sent = [8, 12, 12, 8]
+    nL = sent[left] if left is not None else 0
+    nR = sent[right] if right is not None else 0
+    uL, uR = [0, 6, 12, 8][r], [8, 12, 6, 0][r]
+    nx, n = nL + nR, uL + S + uR
+    mir = r >= N // 2
+    sg = -1 if mir else 1
+    n0 = S * (N - 1 - r) - uR if mir else S * r - uL
+    init = -float(S * (N - 1 - r) if mir else S * r)
+    nbs = [k for k in (left, right) if k is not None]
+    others = [k for k in range(N) if k != r]
+    ne = len(nbs)
+    u8 = dt.uint8
+    vs = "vs"
+    K = {}
+
+    def kc(name_):
+        if name_ not in K:
+            K[name_] = len(K)
+        return col("kc", K[name_])
+
+    dma("y", A("xin", 0, 768), T.x[:, 0:768], "dx", 2600.0)
+    dma("s", A("xin", 768, 1536), T.x[:, 768:1536], "dx2", 2800.0)
+    dma("s", A("uin"), T.u[:, :], "du")
+    dma("y", A("wq", cast=u8), T.wc[:, :], "dw", 3000.0, [A("xin")])
+    dma("y", A("wqs"), T.ws[:, :], "dws", DMA, [A("xin")])
+    dma("y", A("vin"), T.v[:, :], "dv", DMA, [A("wq")])
+    iota(col("pi", 0), [[0, 1]], 0, 1)
+    iota(A("w0"), [[1, 8], [128, 3]])
+    iota(A("io1"), [[1, 128]])
+    iota(A("ctau", 0, 70), [[0, 7], [1, 10]], -5)
+    off = [0, 0, 32, 96]
+    iota(A("ki"), [[48, 4], [-sg, 32]])
+    for a in range(4):
+        c_ = [(191 - 32 * d + off[a] if mir else 32 * d + off[a]) for d in (a, (a + 2) % 4)]
+        iota(A("thp", 0, 2, 1, 32 * a, 32 * a + 32), [[c_[1] - c_[0], 2]], c_[0] - 32 * a, -1)
+
+    def iotas_late():
+        for a in range(4):
+            c_ = []
+            for kk in range(2):
+                i = 191 - 32 * a - 16 * kk if mir else 32 * a + 16 * kk
+                s_ = i % S
+                c_.append(128 * int((s_ >= 32) != (a in (1, 2))) + 32 * (i // S) + s_ % 32)
+            iota(A("thp", 2, 4, 1, 32 * a, 32 * a + 32), [[c_[1] - c_[0], 2]], c_[0], 0)
+        iota(A("dk", 0, 24), [[sg * 9, 8], [sg * 128 * (n + 8), 3]])
+        iota(A("dk", 24, 96), [[0, 3], [sg, 8], [sg * 128 * n, 3]])
+
+    fill(A("zer"), 0.0)
+    ts(col("pi", 1), col("pi", 0), 15, ALU.bitwise_and)
+    ts(col("pi", 2), col("pi", 0), 4, ALU.arith_shift_right)
+    ts(col("pi", 3), col("pi", 0), 7, ALU.bitwise_and)
+    ts(col("pi", 4), col("pi", 0), 16, ALU.bitwise_and)
+    ts(col("pi", 5), col("pi", 0), 3, ALU.arith_shift_right, 1, ALU.bitwise_and)
+    ts(col("pi", 6), col("pi", 0), 1, ALU.bitwise_and)
+    ts(col("pi", 7), col("pi", 0), 1, ALU.arith_shift_right)
+    P, Q, G, Q7, H16, QH, ODD, HALF = [kc(k) for k in ("p", "q", "g", "q7", "h16", "qh", "odd", "half")]
+    cp("v", A("kc", 0, 8), A("pi", 0, 8))
+    aff(vs, kc("q8"), Q, 8.0, 0.0)
+    aff(vs, kc("fin"), Q7, 48.0, QH)
+    ts(A("l0"), A("w0"), kc("q8"), ALU.add)
+    quant("tq", 384, 512, "zer", 0)
+    aff(vs, A("bown"), A("io1", 0, 48, 2), 1.0, kc("fin"))
+    cp("v", A("lf"), A("bown"))
+    if ne == 2:
+        cp("v", A("lb", 0, 6), A("bown", 0, 6))
+        cp("v", A("lb", 6, 12), A("bown", 18, 24))
+    ts(kc("eb"), P, 48.0, ALU.is_ge, BIG, ALU.mult)
+    fill(A("m"), BIG)
+    fill(A("e"), BIG)
+    fill(A("t1"), 0.0)
+    fill(A("m3"), 0.0)
+    quant("uq", 0, 128, "uin", 0)
+    quant("tn", 0, 192, "xin", 0)
+    quant("tn", 192, 384, "xin", 768)
+    pick("tq", 0, 384, "tn", 384, A("l0"))
+    quant("vq", 0, 128, "vin", 0)
+    for b in range(4):
+        cp(vs, A("eb", 512 * b, 512 * b + 512), A("zer"))
+        ts(A("eb", 512 * b + b, 512 * b + 512, 4), A("io1"), P, ALU.is_equal)
+        quant("eq", 128 * b, 128 * b + 128, "eb", 512 * b)
+    if ne == 1:
+        for t in range(R):
+            quant("lq%d" % t, 96, 224, "zer", 0)
+    aff(vs, A("ctau", 50, 60), A("ctau", 50, 60), 1.0, 3.5)
+    fill(A("sp"), 0.0)
+    cp(vs, A("mv"), A("zer"))
+    fill(A("sp", 0, 64, 4), 1.0)
+    ts(A("sp", 1, 64, 4), A("io1", 0, 16), Q, ALU.is_equal)
+    aff(vs, A("sp", 2, 32, 4), A("sp", 0, 32, 4), ODD, -1.0)
+    aff(vs, A("sp", 2, 32, 4), A("sp", 2, 32, 4), -1.0, 0.0)
+    aff(vs, A("sp", 34, 64, 4), A("sp", 0, 32, 4), ODD, 0.0)
+    ts(A("mv", 0, 192, 4), A("io1", 0, 48), P, ALU.is_equal)
+    ts(A("mv", 193, 204, 4), A("io1", 0, 3), G, ALU.is_equal)
+    ts(A("mv", 4 * 52 + 2, 4 * 76, 4), A("io1", 0, 24), HALF, ALU.is_equal)
+    quant("mq", 0, 128, "mv", 0)
+    ts(kc("g7"), G, 7.0, ALU.is_equal)
+    cp(vs, A("vt"), A("zer"))
+    cp(vs, A("ve"), A("zer"))
+    cp(vs, A("zt", 4 * B0, 4 * ZC), A("zer"))
+    if 8 * n < B0:
+        fill(A("zt", 32 * n, 4 * B0), 0.0)
+        quant("zq", B0 - 128, B0, "zer", 0)
+    fill(A("z32"), 0.0)
+    aff(vs, kc("al"), kc("g7"), -0.5, -0.5)
+    aff(vs, kc("be"), kc("g7"), -3.5, 3.5)
+    aff(vs, kc("q16"), Q, 1.0, 16.0)
+    aff(vs, kc("q32"), Q, 1.0, 32.0)
+    aff(vs, kc("w2"), Q7, -48.0, 384.0)
+    aff(vs, kc("w2x"), Q7, -1.0, float(HX))
+    aff(vs, kc("mw2"), Q7, 48.0, -384.0)
+    aff(vs, kc("mw2x"), Q7, 1.0, -float(HX))
+    aff(vs, kc("mq7"), Q7, -1.0, 0.0)
+    aff(vs, kc("ev4"), QH, -4.0, 4.0)
+    aff(vs, kc("od4"), QH, 4.0, 0.0)
+    aff(vs, kc("ev"), QH, -1.0, 1.0)
+    aff(vs, A("bext", 0, 16), A("io1", 0, 16), 16.0, Q)
+
+    def consts_c():
+        for d in range(2):
+            ts(A("kt", d, 256, 2), A("ki"), col("thp", d), ALU.is_lt, -2.0 ** -24, ALU.mult)
+        aff(vs, A("kt"), A("kt"), 1.0, 1.0)
+        aff(vs, kc("sq"), Q, float(sg), 0.0)
+        aff(vs, A("w3", 0, 6), A("io1", 0, 96, 16), 1.0, Q)
+        z8 = 47.0 if mir else 0.0
+        ts(kc("up"), P, 64.0, ALU.is_ge)
+        ca_, cb_, da_, db_ = (-4096.0, 1024.0, 4095.0, 1.125) if mir else (-4097.0, 1025.125, 4096.0, 0.0)
+        aff(vs, kc("ta"), kc("up"), da_ - ca_, ca_)
+        aff(vs, kc("tb"), kc("up"), db_ - cb_, cb_)
+        aff(vs, kc("lo"), kc("up"), 0.0 if mir else -0.125, z8)
+        aff(vs, kc("hi"), kc("up"), 0.125 if mir else 0.0, z8 + 1)
+        aff(vs, A("lo", 0, 3), A("w3", 0, 3), float(sg), kc("lo"))
+        aff(vs, A("lo", 4, 7), A("w3", 0, 3), float(sg), kc("hi"))
+        tab = [(n + 8, 1.125, n - 3.5 / 8 - (8 * n - 1 if mir else 0)),
+               (n, 0.125, n - 3.5 / 8 + (-(B0 + n - 1) if mir else B0 - 1)),
+               (n, 0.125, 1.125 * n - 0.5 if mir else n - 0.375), (n, 0.125, 1.125 * n - 0.375 if mir else n - 0.5)]
+        for i, (a_, b_, c_) in enumerate(tab):
+            aff(vs, kc("d%d" % i), Q, float(sg * a_), c_ + (47 * a_ + 7 * b_ if mir else 0.0))
+            aff(vs, A("dk", 24 * i, 24 * i + 24), A("dk", 24 * i, 24 * i + 24), 0.125, kc("d%d" % i))
+        ts(A("lc"), A("thp", 2, 4), kc("sq"), ALU.add)
+        aff(vs, A("w4", 0, 6), A("w3", 0, 6), 1.0 / 3, -1.0 / 3)
+        ts(A("w4", 0, 6), A("w4", 0, 6), MAGIC, ALU.add, MAGIC, ALU.subtract)
+        ts(A("w5", 0, 6), A("w3", 0, 6), 48.0, ALU.is_ge, kc("up"), ALU.not_equal)
+        tt(A("w4", 0, 6), A("w5", 0, 6), A("w4", 0, 6), ALU.subtract)
+        aff(vs, A("w4", 0, 6), A("w4", 0, 6), 3.0, 0.0)
+        tt(A("w4", 0, 6), A("w4", 0, 6), A("w3", 0, 6), ALU.add)
+        cp("v", A("ls"), A("w4", 0, 6))
+        fill(A("c96"), 96.0)
+        fill(A("c98"), 1.125)
+        fill(col("pos", 0), init)
+        fill(A("sums"), 0.0)
+        for b in range(4):
+            cp(vs, A("fe", XW * b + 8 * nx, XW * b + XW), A("zer", 0, XW - 8 * nx))
+        f0 = float(n0 + n - 1 if mir else n0)
+        ts(A("w6", 0, 3), A("w3", 0, 3), 24.0, ALU.is_ge, -23.5, ALU.mult)
+        tt(A("w6", 0, 3), A("w6", 0, 3), A("w3", 0, 3), ALU.add)
+        aff("v", A("lfo", 0, 3), A("w6", 0, 3), 2.0 * sg, f0 + sg * uL)
+        aff(vs, A("w7", 0, 2), A("io1", 0, 2), 0.5, Q)
+        ts(A("w8", 0, 2), A("w7", 0, 2), nL / 2.0, ALU.is_ge)
+        aff(vs, A("w6", 4, 6), A("w8", 0, 2), 24.0, 0.0)
+        tt(A("w6", 4, 6), A("w6", 4, 6), A("w7", 0, 2), ALU.add)
+        aff(vs, A("w6", 4, 6), A("w6", 4, 6), 2.0 * sg, f0 - sg * (nL - uL))
+        ts(A("lfx"), A("w6", 4, 6), 0.0, ALU.max, 127.0, ALU.min)
+        if ne == 2:
+            aff(vs, A("w8", 2, 4), A("w8", 0, 2), 8.0, (16 - nL) / 2.0)
+            tt(A("w8", 2, 4), A("w8", 2, 4), A("w7", 0, 2), ALU.add)
+            ts(A("w8", 2, 4), A("w8", 2, 4), 2.0, ALU.mult, 47.0, ALU.min)
+        else:
+            aff(vs, A("w8", 2, 4), A("w7", 0, 2), 2.0, float(16 - nL if nL else 0))
+            ts(A("w8", 2, 4), A("w8", 2, 4), 15.0, ALU.min)
+        ts(A("lp"), A("w8", 2, 4), H16, ALU.add)
+        if nL:
+            ts(kc("xl"), Q, float(nL - 16), ALU.add, 0.0, ALU.max)
+            aff(vs, kc("xl"), kc("xl"), 8.0, 0.0)
+        if nR:
+            ts(kc("xr"), Q, float(nR - 1), ALU.min, float(nL), ALU.add)
+            aff(vs, kc("xr"), kc("xr"), 8.0, 0.0)
+
+    def slots(buf, p, w, base, stride, w2):
+        a_, b_, c_ = [A(buf, k * w, k * w + w) for k in (3, 4, 5)]
+        act(c_, p, ACT.Sign, bias=kc("mq7"))
+        act(a_, c_, ACT.Relu, scale=stride)
+        act(b_, c_, ACT.Abs)
+        aff(vs, c_, a_, -1.0, stride)
+        aff(vs, b_, b_, w2[1], w2[0])
+        tt(a_, a_, b_, ALU.add)
+        tt(A(buf, 0, w), a_, base, ALU.add)
+        tt(c_, c_, a_, ALU.subtract)
+        aff(vs, A(buf, w, 2 * w), c_, kc("ev4"), 0.0)
+        aff(vs, A(buf, 2 * w, 3 * w), c_, kc("od4"), 0.0)
+
+    def choose(buf, w, lst):
+        tt(A(buf, 6 * w, 8 * w), A("frow", ind=lst), A(buf, w, 3 * w), ALU.mult)
+        tt(A(buf, 6 * w, 7 * w), A(buf, 6 * w, 7 * w), A(buf, 7 * w, 8 * w), ALU.add)
+        tt(A(buf, 6 * w, 7 * w), A(buf, 6 * w, 7 * w), A(buf, 0, w), ALU.add)
+
+    def zgather(b, z0, k, src, w, lst):
+        cp(vs, A("zt", 32 * z0 + b, 32 * (z0 + k), 4), A(src, w * b, w * b + w, ind=lst))
+
+    for t in range(R):
+        lq, cl, pl = "lq%d" % t, "cl%d" % t, "pl%d" % t
+        for l in range(L - 1, -1, -1):
+            mm(l, "tq", 48 * l, "uq", 0, 128)
+        ns = 8 * sent[r]
+        lst = A("lb") if ne == 2 else (A("lf", 20, 24) if r == 0 else A("lf", 0, 4))
+        pick("bq", 0, ns * ne, "tq", 384, lst)
+        for nm, cast, rs, ls_ in (("", u8, "ac", "sc"), ("s", None, "as", "ss")):
+            mv_ = []
+            for i, k in enumerate(nbs):
+                d0 = 0 if k > r or k == 0 else 8 * sent[k - 1]
+                mv_.append((A("bq" + nm, ns * i, ns * i + ns, cast=cast), A(lq + nm, d0, d0 + ns, cast=cast), [k]))
+            remote(mv_, "%s%d" % (rs, t), "%s%d" % (ls_, t), A(lq + nm, 0, 8 * nx), sum(share(k) for k in nbs),
+                   HOP + 600)
+        if t == 0:
+            iotas_late()
+            consts_c()
+
+        def score(out, gr, bias=0.0):
+            act(out, A("ps", 16 * gr, 3585 + 16 * gr, 512), ACT.Abs, bias=bias)
+
+        score(A("m", 1, 9), 0, kc("eb"))
+        score(A("m", 11, 19), 7)
+        for k in range(1, 4):
+            score(A("e", 20 * k + 1, 20 * k + 9), k)
+            score(A("e", 20 * k + 11, 20 * k + 19), 7 - k)
+        score(A("e", 11, 19), 7)
+        ts(A("e", 71, 79), A("e", 71, 79), FLOOR, ALU.max)
+        for b in range(4):
+            mm(b, "eq", 128 * b, "tq", 0, 384)
+        for b in range(4):
+            mm(4 + b, "eq", 128 * b, lq, 0, max(128, 8 * nx))
+        for b in range(4):
+            cp("s", A("fb", PW * b, PW * b + 384), ps(b, 0, 384))
+
+        def least(o, w):
+            tt(A("t1", o + 1, o + 1 + w), A("m", o, o + w), A("m", o + 1, o + 1 + w), ALU.min)
+            tt(A("m3", o + 1, o + 1 + w), A("t1", o + 1, o + 1 + w), A("m", o + 2, o + 2 + w), ALU.min)
+
+        for o in (0, 20, 40):
+            least(o, 18)
+            tt(A("m", o + 21, o + 39), A("m3", o + 1, o + 19), A("e", o + 21, o + 39), ALU.max)
+        least(60, 8)
+        tt(A("mc", 0, 8), A("m3", 61, 69), A("m", 71, 79), ALU.max)
+        red(col("msg", 0, 0, 64), A("mc", 0, 8, 1, 0, 64), ALU.min)
+        red(col("msg", 0, 64, 96), A("mc", 0, 8, 1, 32, 64), ALU.min)
+        red(col("msg", 0, 96, 128), A("mc", 0, 8, 1, 0, 32), ALU.min)
+        remote([(col("msg", 0), col(cl, 4 * r), others)], "ak%d" % t, "sk%d" % t, A(cl),
+               sum(len(topo.engines(T.cores[k], core)) for k in others), HOP + 300)
+        tt(A("m", 11, 19), A("m3", 61, 69), A("e", 71, 79), ALU.max)
+        for o in (10, 30, 50):
+            least(o, 8)
+            tt(A("m", o + 21, o + 29), A("m3", o + 1, o + 9), A("e", 61 - o, 69 - o), ALU.max)
+        scan(A("pm"), A("m", 71, 79), A("m", 71, 79), BIG, ALU.min, ALU.min)
+        for o, w in ((0, 49), (50, 19)):
+            tt(A("ca", o, o + w), A("t1", o, o + w), A("m3", o, o + w), ALU.is_equal)
+            tt(A("cb", o, o + w), A("m", o, o + w), A("m3", o + 1, o + w + 1), ALU.is_equal)
+            tt(A("ca", o, o + w), A("ca", o, o + w), A("ctau", o, o + w), ALU.add)
+            tt(A("tau", o, o + w), A("ca", o, o + w), A("cb", o, o + w), ALU.add)
+        act(A("dump", 56, 64), A("pm"), ACT.Sign, bias=col("pm", 7), scale=-1.0, accum=col("acc", 7))
+        for gr in range(7, 0, -1):
+            o = [0, 20, 40, 60, 10, 30, 50][gr - 1]
+            act(A("dump", 8 * gr - 8, 8 * gr - 1), A("tau", o + 1, o + 8), ACT.Sign, bias=col("acc", gr),
+                scale=1.0 if gr == 7 else 2.0, accum=col("acc", gr - 1))
+        for gr in range(7, -1, -1):
+            aff(vs, A("st", 64 * gr, 64 * gr + 64), A("sp"), col("acc", gr), 0.0)
+        quant("sq", 0, 128, "st", 0)
+        mm(0, "sq", 0, "mq", 0, 128)
+        for b in range(4):
+            cp("s", A("fe", XW * b, XW * b + 8 * nx), ps(4 + b, 0, 8 * nx))
+        aff("v", A("prow", 0, 76), ps(0, 0, 76), kc("al"), kc("be"))
+        mv_ = []
+        if left is not None:
+            mv_.append((col("prow", 48), col(pl, 4), [left]))
+        if right is not None:
+            mv_.append((col("prow", 50), col(pl, 0), [right]))
+        remote(mv_, "ap%d" % t, "sp%d" % t, A(pl), sum(share(k) for k in nbs))
+        for m_, qq in enumerate((Q, kc("q16"), kc("q32"))):
+            aff("v", col("lv", m_), col("prow", 48 + m_), 48.0, qq)
+        for b in range(4):
+            cp(vs, A("vt", b, 192, 4), A("fb", PW * b, PW * b + 384, ind=A("lv", 0, 3)))
+        quant("vcq", 0, 128, "vt", 0)
+        for b in range(4):
+            mm(4 + b, "wq", 128 * b, "vcq", 0, 128)
+        slots("oa", A("prow", 52, 76), 24, A("bown"), 48.0, (kc("w2"), kc("mw2")))
+        for b in range(4):
+            relu("s", A("fb", PW * b + 384, PW * b + 432), ps(4 + b, 0, 48), 0.03125)
+        for b in range(4):
+            cp(vs, A("zt", 4 * (B0 + uL) + b, 4 * (B0 + uL + S), 4), A("fb", PW * b, PW * b + S))
+            if uL:
+                cp(vs, A("zt", 4 * B0 + b, 4 * (B0 + uL), 4), A("fe", XW * b + 8 * (nL - uL), XW * b + 8 * nL, 8))
+            if uR:
+                cp(vs, A("zt", 4 * (B0 + uL + S) + b, 4 * (B0 + n), 4),
+                   A("fe", XW * b + 8 * nL, XW * b + 8 * (nL + uR), 8))
+        quant("zq", B0, ZC, "zt", 4 * B0)
+        if t == R - 1:
+            aff(vs, A("o8"), A("io1", 0, 48), 8.0, 0.0)
+            tt(A("olb"), A("prow", 0, 48), A("o8"), ALU.add)
+            for gr in range(8):
+                dma("y", T.ol[gr:gr + 1, :], A("olb", 0, 48, 1, 16 * gr, 16 * gr + 1), "dol")
+        for k in [r] + others:
+            aff(vs, A("inr", 64 * k, 64 * k + 64), A("kt", 64 * k, 64 * k + 64),
+                col("msg", 0) if k == r else col(cl, 4 * k), 0.0)
+        tr(A("row", 0, 128), A("inr", 0, 256, 2))
+        tr(A("row", 128, 256, 1, 64, 128), A("inr", 1, 256, 2, 0, 64))
+        tr(A("row", 128, 256, 1, 0, 64), A("inr", 1, 256, 2, 64, 128))
+        cp(vs, A("cg"), A("row", ind=A("lc")))
+        tr(A("ct"), A("cg"))
+        key = col("ct", 31 if mir else 0)
+        ts(A("cmp", 0, 128), A("row", 0, 128), key, ALU.is_lt)
+        red(col("cnt", 0), A("cmp", 0, 128), ALU.add)
+        act(A("cmp", 128, 256), A("row", 128, 256), ACT.Sign, bias=key, scale=-1.0)
+        act(A("cmp", 128, 256), A("cmp", 128, 256), ACT.Relu, accum=col("cnt", 2))
+        ts(A("fl32"), A("c96"), col("cnt", 0), ALU.subtract, col("cnt", 2), ALU.is_gt)
+        for a in range(4):
+            tr(A("fone", 32 * a, 32 * a + 32, 1, 0, 32), A("fl32", 0, 32, 1, 32 * a, 32 * a + 32))
+        for a in range(4):
+            aff("v", A("frow", 0, 128, 1, 32 * a, 32 * a + 32), A("fone", 0, 128, 1, 0, 32), 0.25, 0.0)
+        choose("oa", 24, A("lfo", 0, 3))
+        cp("v", A("lz"), A("oa", 144, 168))
+        for b in range(4):
+            if b < 2:
+                zgather(b, uL, S, "fb", PW, A("lz"))
+            else:
+                for h in range(2):
+                    zgather(b, uL + 24 * h, 24, "fb", PW, A("lz", 12 * h, 12 * h + 12))
+        sides = ([(0, kc("xl"))] if nL else []) + ([(4, kc("xr"))] if nR else [])
+        for i, (c_, xb) in enumerate(sides):
+            ts(col("lve", i), col(pl, c_), xb, ALU.add)
+        for b in range(4):
+            cp(vs, A("ve", b, 64 * ne, 4), A("fe", XW * b, XW * b + 8 * nx, ind=A("lve", 0, ne)))
+        quant("veq", 0, 128, "ve", 0)
+        for b in range(4):
+            mm(b, "wq", 128 * b, "veq", 0, 128)
+        v0 = 16 - nL if nL else 0
+        for b in range(4):
+            relu("s", A("fe", XW * b + HX, XW * b + HX + 8 * nx, 8), ps(b, v0, v0 + nx), 0.03125)
+        for i, (c_, xb) in enumerate(sides):
+            aff(vs, A("pin", 32 * i, 32 * i + 32), A("z32"), 1.0, col(pl, c_))
+        tr(A("pt", 0, 32 * ne), A("pin", 0, 32 * ne))
+        cp(vs, A("pe", 0, 32), A("pt", 0, 32 * ne, ind=A("lp")))
+        aff(vs, A("pe", 32, 48), A("pe", 0, 16), kc("ev"), 0.0)
+        aff(vs, A("pe", 48, 64), A("pe", 16, 32), QH, 0.0)
+        tt(A("pe", 32, 48), A("pe", 32, 48), A("pe", 48, 64), ALU.add)
+        slots("ox", A("pe", 32, 48), 16, A("bext"), 1.0, (kc("w2x"), kc("mw2x")))
+        choose("ox", 16, A("lfx"))
+        if uL:
+            cp("v", A("lzx", 0, uL // 2), A("ox", 96 + (nL - uL) // 2, 96 + nL // 2))
+        if uR:
+            cp("v", A("lzx", 8, 8 + uR // 2), A("ox", 96 + nL // 2, 96 + (nL + uR) // 2))
+        for b in range(4):
+            if uL:
+                zgather(b, 0, uL, "fe", XW, A("lzx", 0, uL // 2))
+            if uR:
+                zgather(b, uL + S, uR, "fe", XW, A("lzx", 8, 8 + uR // 2))
+        scan(A("pos", 1, 1 + n0 + n), A("c98", 0, n0 + n), A("frow", 0, n0 + n), init, ALU.add, ALU.subtract)
+        aff(vs, A("t7", 0, n), A("frow", n0, n0 + n), kc("ta"), kc("tb"))
+        tt(A("th", 0, n), A("pos", n0, n0 + n), A("t7", 0, n), ALU.add)
+        aff(vs, col("cnt", 1), col("pos", n0), 8.0, 0.0)
+        for m_ in range(3):
+            ts(A("cl", 68 * m_, 68 * m_ + n), A("th", 0, n), col("lo", m_), ALU.max, col("lo", 4 + m_), ALU.min)
+            red(col("sums", m_), A("cl", 68 * m_, 68 * m_ + n), ALU.add)
+        cp(vs, A("sums", 3, 6, 1, 0, 64), A("sums", 0, 3, 1, 64, 128))
+        cp(vs, A("sums", 3, 6, 1, 64, 128), A("sums", 0, 3, 1, 0, 64))
+        tt(A("xr"), A("sums", ind=A("ls")), A("dk"), ALU.subtract)
+        c1, c4, da, db = [A("rr", 24 * i, 24 * i + 24) for i in range(4)]
+        ts(A("rr", 48, 96), A("xr", 48, 96), 8.0 / 9, ALU.mult, MAGIC, ALU.add)
+        ts(c4, A("xr", 24, 48), MAGIC, ALU.add, -2 * MAGIC, ALU.add)
+        ts(c1, A("xr", 0, 24), MAGIC, ALU.add, col("cnt", 1), ALU.add)
+        x0, x1, x2, x3, x4 = [A("mm5", 24 * i, 24 * i + 24) for i in range(5)]
+        tt(x0, da, db, ALU.subtract)
+        tt(x1, c4, da, ALU.add)
+        if mir:
+            tt(x2, c1, da, ALU.subtract)
+        else:
+            tt(x2, da, c1, ALU.subtract)
+        tt(x3, x0, x1, ALU.mult)
+        tt(x4, x3, x2, ALU.max)
+        cp("v", A("lm"), x4)
+        quant("zq", 128, 8 * n - 128, "zt", 512)
+        quant("zq", 0, 128, "zt", 0)
+        quant("zq", 8 * n - 128, 8 * n, "zt", 32 * n - 512)
+        for h in (1, 0):
+            pick("gq", 192 * h, 192, "zq", ZC, A("lm", 12 * h, 12 * h + 12))
+        for h in (1, 0):
+            for b in range(4):
+                i = mm(b, "wq", 128 * b, "gq", 192 * h, 192, [i] if 1 - h + b else [])
+                i = mm(4 + b, "eq", 128 * b, "gq", 192 * h, 192, [i])
+            for b in range(4):
+                o = 384 * b + 192 * h
+                relu("s", A("tmp", o, o + 192), ps(b, 0, 192), 0.015625)
+                tt(A("xt", 768 * h + b, 768 * h + 768, 4), ps(4 + b, 0, 192), A("tmp", o, o + 192), ALU.add)
+            quant("tq", 192 * h, 192 * h + 192, "xt", 768 * h)
+
+    pick("tf", 0, 384, "tq", 384, A("lf"))
+    for h in range(2):
+        mm(h, "vq", 0, "tf", 192 * h, 192)
+        cp("vs"[h], A("ysb", 192 * h, 192 * h + 192), ps(h, 0, 192))
+    dma("y", T.oc[:, :], A("tf", cast=u8), "doc")
+    for k in range(4):
+        dma("sy"[k % 2], T.osc[4 * k:4 * k + 4, :], A("tfs", 0, 384, 1, 32 * k, 32 * k + 4), "dos")
+    dma("y", T.y[:, :], A("ysb"), "dy")
+
+    count, known, mark = {}, {q: {} for q in eng}, {}
+    for i, q in schedule(ops)[0]:
+        o = ops[i]
+        sem = o["sem"] or COUNTER[q]
+        count[sem] = count.get(sem, 0) + o["inc"]
+        if q == "x":
+            mark[i] = (sem, count[sem], {sem: count[sem]}, len(mark))
+            continue
+        k = known[q]
+        for s_, v_, clock, at in sorted((mark[j] for j in o["hard"]), key=lambda x: -x[3]):
+            if k.get(s_, 0) < v_:
+                eng[q].wait_ge(T.sem[s_], v_)
+                for s2, v2 in clock.items():
+                    k[s2] = max(k.get(s2, 0), v2)
+        call = o["fns"][q](eng[q])
+        if o["chain"]:
+            call.then_inc(T.sem[sem], o["inc"])
+        clock = dict(k)
+        clock[sem] = count[sem]
+        mark[i] = (sem, count[sem], clock, len(mark))
+    for s_, v_ in count.items():
+        g.wait_ge(T.sem[s_], v_)

@@ -29,10 +29,10 @@ _buf(CODE, tn=384, tq=512, tf=384, uq=128, vq=128, wq=512, eq=512, mq=128, sq=12
      bq=192, lq0=224, lq1=224, lq2=224)
 _buf(PLANE, tns=384, tqs=512, tfs=384, uqs=128, vqs=128, wqs=512, eqs=512, mqs=128, sqs=128, vcqs=128, veqs=128,
      zqs=ZC, gqs=384, bqs=192, lq0s=224, lq1s=224, lq2s=224)
-_buf(F32, kc=56, e=80, m=80, t1=80, m3=80, ca=72, cb=72, tau=72, ctau=72, pm=8, mc=12, acc=8, dump=64, msg=4, sp=64,
-     prow=76, oa=192, ox=160, bown=24, bext=16, pin=64, pt=64, pe=64, kt=256, ki=128, inr=256, row=256, cg=32, ct=32,
-     cmp=256, cnt=4, c96=32, z32=32, c98=128, pos=132, t7=68, th=68, cl=204, sums=8, lo=8, dk=96, xr=96,
-     rr=96, mm5=120, tmp=1536, ysb=384, olb=48, o8=48, io1=128, w0=24, w3=8, w4=8, w5=8, w6=8, w7=8, w8=8,
+_buf(F32, kc=56, te=160, mo=160, mz=160, tc=16, ca=72, cb=72, cn=216, cq=144, tau=360, ctau=72, mc=24, acc=8, dump=64,
+     msg=4, sp=64, prow=76, oa=192, ox=416, bown=24, bext=16, pin=64, pt=64, kt=256, ki=128, inr=256, row=256, cg=32,
+     ct=32, cmp=256, cnt=4, c96=32, c5=80, z32=32, c98=128, pos=132, t7=68, th=68, cl=204, sums=8, lo=8, dk=96, xr=96,
+     rr=96, mm5=120, tmp=1536, ysb=384, olb=48, o8=48, io1=128, w0=24, w3=8, w4=8, w5=8, w6=8, w7=8,
      thp=4, cl0=16, cl1=16, cl2=16, pl0=8, pl1=8, pl2=8)
 _buf(I32, pi=8)
 _buf(U16, l0=24, lf=24, lb=12, lv=4, lve=2, lz=24, lzx=16, lp=2, lc=2, ls=6, lm=24, lfo=4, lfx=2)
@@ -40,18 +40,13 @@ _buf(U16, l0=24, lf=24, lb=12, lv=4, lve=2, lz=24, lzx=16, lp=2, lc=2, ls=6, lm=
 SEMAPHORES = ["cv", "cs", "cp", "cg", "dx", "dx2", "du", "dv", "dw", "dws", "dol", "dy", "doc", "dos"] + [
     "%s%d" % (k, t) for t in range(R) for k in ("ac", "as", "ak", "ap", "sc", "ss", "sk", "sp")]
 COUNTER = {"v": "cv", "s": "cs", "p": "cp", "g": "cg"}
-CY, GAT, WAKE, PE, HOP, DMA = 1.0, 1.3, 50.0, 0.6, 2500.0, 2000.0
-FINE = ("oa", "ox", "tq", "m", "mc", "cmp", "cnt", "gq", "gqs", "xt", "tmp", "ca", "cb", "tau", "th", "rr", "mm5", "cl",
-        "pe", "fb", "fe")
-AHEAD = {'lz<oa144': 1500, 'lz': 1500, 'oa144': 1500, 'tq192': 2500, 'msg': 3100, 'mc0': 800, 'gqs0<zqsi': 300,
-         'cmp128': 2000, 'kt': 1200, 'vq': -2000, 'lve': 300, 'lf<bown': -300, 'eqlq': 2000, 'xt0': 800, 'vcq': 500,
-         'mm596': -2000, 'eq': -300, 'bext<io1': -2000, 'lzx<ox': 800, 'bq<tqi': 300, 'mq': 500, 'dk': -800,
-         'ctau<ctau': 2000, 'c98': 300, 'z32': 2000, 'm41': 300, 'm3': -300, 'oa48<oa': 300, 'w8<w8': 300,
-         'cmp0': -300, 'lq2s': 800, 'eb': 2000, 'fe320<ps': -800, 'wqve': 2000, 'e': -300, 'oa96': 2000, 'lp': 300,
-         'tmp384<ps': 2000, 'l0': -800, 'fone': 300}
-SPARE = {'zt<fe': 1000, 'zt<fb': 0, 'o8<io1': 0, 'st<sp': 0, 'zt<zer': 300, 'zt<fbi': 0, 'inr<kt': 300,
-         'fe160<zer': -100, 'ox16<ox': -100, 'cg<rowi': -100, 'oa24<oa': 1000, 'sums<sums': 1000, 'sp<sp': -100,
-         'ox80<ox': 1000, 'vt<zer': -100}
+CY, GAT, WAKE, PE, HOP, DMA = 0.95, 1.3, 200.0, 0.6, 2500.0, 2000.0
+FINE = ("oa", "ox", "tq", "mo", "mz", "te", "cn", "cq", "tc", "cmp", "cnt", "gq", "gqs", "xt", "tmp", "ca", "cb", "tau",
+        "th", "rr", "mm5", "cl", "pe", "fb", "fe")
+AHEAD = {'zt<fbi': 800, 'lz<oa': 800, 'vcq': 500, 'vt<fbi': 500, 'tau93': 300, 'tn': 800, 'ox112': -2000, 'cl2': -2000,
+         'cl0': -2000, 'cl136': -2000, 'kt': -300, 'cn1': -300, 'xr': -2000, 'cq59': 800, 'w5': 300, 'mm548': -800,
+         'eqgq': -800}
+SPARE = {'zt<fe': 0, 've<fei': -100}
 
 
 def A(name, c0=0, c1=None, step=1, p0=0, p1=128, ind=None, cast=None):
@@ -62,6 +57,10 @@ def A(name, c0=0, c1=None, step=1, p0=0, p1=128, ind=None, cast=None):
 
 def col(name, c, p0=0, p1=128):
     return A(name, c, c + 1, 1, p0, p1)
+
+
+def odd(buf, o, w):
+    return A(buf, 2 * o + 1, 2 * (o + w), 2)
 
 
 def size(a):
@@ -322,10 +321,9 @@ def rank_program(g, core, T, topo):
         cp("v", A("lb", 0, 6), A("bown", 0, 6))
         cp("v", A("lb", 6, 12), A("bown", 18, 24))
     ts(kc("eb"), P, 48.0, ALU.is_ge, BIG, ALU.mult)
-    fill(A("m"), BIG)
-    fill(A("e"), BIG)
-    fill(A("t1"), 0.0)
-    fill(A("m3"), 0.0)
+    fill(A("mo"), BIG)
+    fill(A("te"), BIG)
+    fill(A("mz"), 0.0)
     quant("uq", 0, 128, "uin", 0)
     quant("tn", 0, 192, "xin", 0)
     quant("tn", 192, 384, "xin", 768)
@@ -364,12 +362,15 @@ def rank_program(g, core, T, topo):
     aff(vs, kc("q32"), Q, 1.0, 32.0)
     aff(vs, kc("w2"), Q7, -48.0, 384.0)
     aff(vs, kc("w2x"), Q7, -1.0, float(HX))
-    aff(vs, kc("mw2"), Q7, 48.0, -384.0)
-    aff(vs, kc("mw2x"), Q7, 1.0, -float(HX))
-    aff(vs, kc("mq7"), Q7, -1.0, 0.0)
     aff(vs, kc("ev4"), QH, -4.0, 4.0)
     aff(vs, kc("od4"), QH, 4.0, 0.0)
     aff(vs, kc("ev"), QH, -1.0, 1.0)
+    aff(vs, kc("ev8"), QH, 8.0, -8.0)
+    aff(vs, kc("od8"), QH, -8.0, 0.0)
+    aff(vs, kc("wev"), kc("w2x"), kc("ev"), 0.0)
+    aff(vs, kc("wod"), kc("w2x"), QH, 0.0)
+    aff(vs, kc("wev4"), kc("wev"), -4.0, 0.0)
+    aff(vs, kc("wod4"), kc("wod"), -4.0, 0.0)
     aff(vs, A("bext", 0, 16), A("io1", 0, 16), 16.0, Q)
 
     def consts_c():
@@ -402,6 +403,8 @@ def rank_program(g, core, T, topo):
         tt(A("w4", 0, 6), A("w4", 0, 6), A("w3", 0, 6), ALU.add)
         cp("v", A("ls"), A("w4", 0, 6))
         fill(A("c96"), 96.0)
+        fill(A("c5"), 1.0)
+        fill(A("c5", 0, 80, 5), 0.0)
         fill(A("c98"), 1.125)
         fill(col("pos", 0), init)
         fill(A("sums"), 0.0)
@@ -412,19 +415,19 @@ def rank_program(g, core, T, topo):
         tt(A("w6", 0, 3), A("w6", 0, 3), A("w3", 0, 3), ALU.add)
         aff("v", A("lfo", 0, 3), A("w6", 0, 3), 2.0 * sg, f0 + sg * uL)
         aff(vs, A("w7", 0, 2), A("io1", 0, 2), 0.5, Q)
-        ts(A("w8", 0, 2), A("w7", 0, 2), nL / 2.0, ALU.is_ge)
-        aff(vs, A("w6", 4, 6), A("w8", 0, 2), 24.0, 0.0)
+        ts(A("w7", 2, 4), A("w7", 0, 2), nL / 2.0, ALU.is_ge)
+        aff(vs, A("w6", 4, 6), A("w7", 2, 4), 24.0, 0.0)
         tt(A("w6", 4, 6), A("w6", 4, 6), A("w7", 0, 2), ALU.add)
         aff(vs, A("w6", 4, 6), A("w6", 4, 6), 2.0 * sg, f0 - sg * (nL - uL))
         ts(A("lfx"), A("w6", 4, 6), 0.0, ALU.max, 127.0, ALU.min)
         if ne == 2:
-            aff(vs, A("w8", 2, 4), A("w8", 0, 2), 8.0, (16 - nL) / 2.0)
-            tt(A("w8", 2, 4), A("w8", 2, 4), A("w7", 0, 2), ALU.add)
-            ts(A("w8", 2, 4), A("w8", 2, 4), 2.0, ALU.mult, 47.0, ALU.min)
+            aff(vs, A("w7", 4, 6), A("w7", 2, 4), 8.0, (16 - nL) / 2.0)
+            tt(A("w7", 4, 6), A("w7", 4, 6), A("w7", 0, 2), ALU.add)
+            ts(A("w7", 4, 6), A("w7", 4, 6), 2.0, ALU.mult, 47.0, ALU.min)
         else:
-            aff(vs, A("w8", 2, 4), A("w7", 0, 2), 2.0, float(16 - nL if nL else 0))
-            ts(A("w8", 2, 4), A("w8", 2, 4), 15.0, ALU.min)
-        ts(A("lp"), A("w8", 2, 4), H16, ALU.add)
+            aff(vs, A("w7", 4, 6), A("w7", 0, 2), 2.0, float(16 - nL if nL else 0))
+            ts(A("w7", 4, 6), A("w7", 4, 6), 15.0, ALU.min)
+        ts(A("lp"), A("w7", 4, 6), H16, ALU.add)
         if nL:
             ts(kc("xl"), Q, float(nL - 16), ALU.add, 0.0, ALU.max)
             aff(vs, kc("xl"), kc("xl"), 8.0, 0.0)
@@ -434,11 +437,9 @@ def rank_program(g, core, T, topo):
 
     def slots(buf, p, w, base, stride, w2):
         a_, b_, c_ = [A(buf, k * w, k * w + w) for k in (3, 4, 5)]
-        act(c_, p, ACT.Sign, bias=kc("mq7"))
-        act(a_, c_, ACT.Relu, scale=stride)
-        act(b_, c_, ACT.Abs)
-        aff(vs, c_, a_, -1.0, stride)
-        aff(vs, b_, b_, w2[1], w2[0])
+        ts(a_, p, Q7, ALU.is_gt, stride, ALU.mult)
+        ts(b_, p, Q7, ALU.is_equal, w2, ALU.mult)
+        ts(c_, p, Q7, ALU.is_le, stride, ALU.mult)
         tt(a_, a_, b_, ALU.add)
         tt(A(buf, 0, w), a_, base, ALU.add)
         tt(c_, c_, a_, ALU.subtract)
@@ -452,6 +453,16 @@ def rank_program(g, core, T, topo):
 
     def zgather(b, z0, k, src, w, lst):
         cp(vs, A("zt", 32 * z0 + b, 32 * (z0 + k), 4), A(src, w * b, w * b + w, ind=lst))
+
+    def score(out, gr, bias=0.0):
+        act(out, A("ps", 16 * gr, 3585 + 16 * gr, 512), ACT.Abs, bias=bias)
+
+    def level(o, eo, do, w, held=True):
+        tt(A("te", 2 * eo + 2, 2 * (eo + w) + 2, 2), odd("mo", o, w), odd("mo", o + 2, w), ALU.min)
+        if held:
+            cp(vs, odd("mz", o + 1, w), odd("mo", o + 1, w))
+        scan(A("mo", 2 * do + 2, 2 * (do + w) + 2), A("mz", 2 * o + 2, 2 * (o + w) + 2),
+             A("te", 2 * eo + 2, 2 * (eo + w) + 2), 0.0, ALU.min, ALU.max)
 
     for t in range(R):
         lq, cl, pl = "lq%d" % t, "cl%d" % t, "pl%d" % t
@@ -470,53 +481,54 @@ def rank_program(g, core, T, topo):
         if t == 0:
             iotas_late()
             consts_c()
-
-        def score(out, gr, bias=0.0):
-            act(out, A("ps", 16 * gr, 3585 + 16 * gr, 512), ACT.Abs, bias=bias)
-
-        score(A("m", 1, 9), 0, kc("eb"))
-        score(A("m", 11, 19), 7)
+        score(odd("mo", 1, 8), 0, kc("eb"))
+        score(odd("mo", 11, 8), 7)
         for k in range(1, 4):
-            score(A("e", 20 * k + 1, 20 * k + 9), k)
-            score(A("e", 20 * k + 11, 20 * k + 19), 7 - k)
-        score(A("e", 11, 19), 7)
-        ts(A("e", 71, 79), A("e", 71, 79), FLOOR, ALU.max)
+            score(odd("te", 20 * k + 1, 8), k)
+            score(odd("te", 20 * k + 11, 8), 7 - k)
+        score(odd("te", 11, 8), 7)
+        ts(odd("te", 71, 8), odd("te", 71, 8), FLOOR, ALU.max)
         for b in range(4):
             mm(b, "eq", 128 * b, "tq", 0, 384)
         for b in range(4):
             mm(4 + b, "eq", 128 * b, lq, 0, max(128, 8 * nx))
         for b in range(4):
             cp("s", A("fb", PW * b, PW * b + 384), ps(b, 0, 384))
-
-        def least(o, w):
-            tt(A("t1", o + 1, o + 1 + w), A("m", o, o + w), A("m", o + 1, o + 1 + w), ALU.min)
-            tt(A("m3", o + 1, o + 1 + w), A("t1", o + 1, o + 1 + w), A("m", o + 2, o + 2 + w), ALU.min)
-
         for o in (0, 20, 40):
-            least(o, 18)
-            tt(A("m", o + 21, o + 39), A("m3", o + 1, o + 19), A("e", o + 21, o + 39), ALU.max)
-        least(60, 8)
-        tt(A("mc", 0, 8), A("m3", 61, 69), A("m", 71, 79), ALU.max)
-        red(col("msg", 0, 0, 64), A("mc", 0, 8, 1, 0, 64), ALU.min)
-        red(col("msg", 0, 64, 96), A("mc", 0, 8, 1, 32, 64), ALU.min)
-        red(col("msg", 0, 96, 128), A("mc", 0, 8, 1, 0, 32), ALU.min)
+            level(o, o + 20, o + 20, 18)
+        tt(A("tc", 0, 16, 2), odd("mo", 60, 8), odd("mo", 62, 8), ALU.min)
+        cp(vs, odd("tc", 0, 8), odd("mo", 71, 8))
+        cp(vs, odd("mz", 61, 8), odd("mo", 61, 8))
+        scan(A("mc", 0, 16), A("mz", 122, 138), A("tc"), 0.0, ALU.min, ALU.max)
+        red(col("msg", 0, 0, 64), A("mc", 1, 16, 2, 0, 64), ALU.min)
+        red(col("msg", 0, 64, 96), A("mc", 1, 16, 2, 32, 64), ALU.min)
+        red(col("msg", 0, 96, 128), A("mc", 1, 16, 2, 0, 32), ALU.min)
         remote([(col("msg", 0), col(cl, 4 * r), others)], "ak%d" % t, "sk%d" % t, A(cl),
                sum(len(topo.engines(T.cores[k], core)) for k in others), HOP + 300)
-        tt(A("m", 11, 19), A("m3", 61, 69), A("e", 71, 79), ALU.max)
+        level(60, 70, 10, 8, False)
         for o in (10, 30, 50):
-            least(o, 8)
-            tt(A("m", o + 21, o + 29), A("m3", o + 1, o + 9), A("e", 61 - o, 69 - o), ALU.max)
-        scan(A("pm"), A("m", 71, 79), A("m", 71, 79), BIG, ALU.min, ALU.min)
-        for o, w in ((0, 49), (50, 19)):
-            tt(A("ca", o, o + w), A("t1", o, o + w), A("m3", o, o + w), ALU.is_equal)
-            tt(A("cb", o, o + w), A("m", o, o + w), A("m3", o + 1, o + w + 1), ALU.is_equal)
-            tt(A("ca", o, o + w), A("ca", o, o + w), A("ctau", o, o + w), ALU.add)
-            tt(A("tau", o, o + w), A("ca", o, o + w), A("cb", o, o + w), ALU.add)
-        act(A("dump", 56, 64), A("pm"), ACT.Sign, bias=col("pm", 7), scale=-1.0, accum=col("acc", 7))
-        for gr in range(7, 0, -1):
-            o = [0, 20, 40, 60, 10, 30, 50][gr - 1]
-            act(A("dump", 8 * gr - 8, 8 * gr - 1), A("tau", o + 1, o + 8), ACT.Sign, bias=col("acc", gr),
-                scale=1.0 if gr == 7 else 2.0, accum=col("acc", gr - 1))
+            level(o, 60 - o, o + 20, 8)
+        scan(A("mc", 16, 24), odd("mo", 71, 8), odd("mo", 71, 8), BIG, ALU.min, ALU.min)
+        for o, w in ((0, 49), (59, 10), (50, 9)):
+            tt(A("ca", o, o + w), odd("mo", o, w), odd("mo", o + 1, w), ALU.is_le)
+            tt(A("cb", o, o + w), odd("mo", o, w), odd("mo", o + 2, w), ALU.is_le)
+            tt(A("cn", o + 1, o + w), A("cb", o, o + w - 1), A("ca", o + 1, o + w), ALU.max)
+            tt(A("cq", o, o + w), A("ca", o, o + w), A("cb", o, o + w), ALU.mult)
+            tt(A("cq", 72 + o, 72 + o + w), A("cq", o, o + w), A("ctau", o, o + w), ALU.add)
+            tt(A("tau", o + 1, o + w), A("cn", o + 1, o + w), A("cq", 73 + o, 72 + o + w), ALU.add)
+        tt(A("cn", 73, 120), A("cn", 1, 48), A("cq", 1, 48), ALU.max)
+        tt(A("cn", 145, 192), A("cn", 1, 48), A("cq", 1, 48), ALU.mult)
+        for o, w in ((21, 17), (61, 7)):
+            tt(A("tau", 72 + o, 73 + o + w), A("tau", o, o + w + 1), A("tau", o - 1, o + w), ALU.subtract)
+            tt(A("tau", 144 + o, 144 + o + w), A("tau", 72 + o, 72 + o + w), A("cn", 52 + o, 52 + o + w), ALU.mult)
+            tt(A("tau", 216 + o, 216 + o + w), A("tau", 73 + o, 73 + o + w), A("cn", 124 + o, 124 + o + w), ALU.mult)
+            tt(A("tau", 144 + o, 144 + o + w), A("tau", 144 + o, 144 + o + w), A("tau", o - 1, o + w - 1), ALU.add)
+            tt(A("tau", 288 + o, 288 + o + w), A("tau", 144 + o, 144 + o + w), A("tau", 216 + o, 216 + o + w), ALU.add)
+        act(A("dump", 56, 64), A("mc", 16, 24), ACT.Sign, bias=col("mc", 23), scale=-1.0, accum=col("acc", 7))
+        for gr, to in ((7, 6), (6, 4), (6, 5), (4, 2), (4, 3), (2, 0), (2, 1)):
+            o = [0, 20, 40, 60, 10, 30, 50][gr - 1] + (288 if gr - to == 2 else 0)
+            act(A("dump", 8 * to, 8 * to + 7), A("tau", o + 1, o + 8), ACT.Sign, bias=col("acc", gr),
+                scale=1.0 if gr == 7 else 2.0, accum=col("acc", to))
         for gr in range(7, -1, -1):
             aff(vs, A("st", 64 * gr, 64 * gr + 64), A("sp"), col("acc", gr), 0.0)
         quant("sq", 0, 128, "st", 0)
@@ -537,7 +549,7 @@ def rank_program(g, core, T, topo):
         quant("vcq", 0, 128, "vt", 0)
         for b in range(4):
             mm(4 + b, "wq", 128 * b, "vcq", 0, 128)
-        slots("oa", A("prow", 52, 76), 24, A("bown"), 48.0, (kc("w2"), kc("mw2")))
+        slots("oa", A("prow", 52, 76), 24, A("bown"), 48.0, kc("w2"))
         for b in range(4):
             relu("s", A("fb", PW * b + 384, PW * b + 432), ps(4 + b, 0, 48), 0.03125)
         for b in range(4):
@@ -593,16 +605,25 @@ def rank_program(g, core, T, topo):
         for i, (c_, xb) in enumerate(sides):
             aff(vs, A("pin", 32 * i, 32 * i + 32), A("z32"), 1.0, col(pl, c_))
         tr(A("pt", 0, 32 * ne), A("pin", 0, 32 * ne))
-        cp(vs, A("pe", 0, 32), A("pt", 0, 32 * ne, ind=A("lp")))
-        aff(vs, A("pe", 32, 48), A("pe", 0, 16), kc("ev"), 0.0)
-        aff(vs, A("pe", 48, 64), A("pe", 16, 32), QH, 0.0)
-        tt(A("pe", 32, 48), A("pe", 32, 48), A("pe", 48, 64), ALU.add)
-        slots("ox", A("pe", 32, 48), 16, A("bext"), 1.0, (kc("w2x"), kc("mw2x")))
-        choose("ox", 16, A("lfx"))
+        o_ = [A("ox", 16 * i, 16 * i + 16) for i in range(13)]
+        cp(vs, A("ox", 0, 32), A("frow", ind=A("lfx")))
+        aff(vs, o_[2], o_[0], kc("ev8"), kc("ev"))
+        aff(vs, o_[3], o_[1], kc("od8"), QH)
+        aff(vs, o_[4], o_[0], kc("wev4"), kc("wev"))
+        aff(vs, o_[5], o_[1], kc("wod4"), kc("wod"))
+        aff(vs, o_[7], o_[0], kc("ev4"), 0.0)
+        aff(vs, o_[8], o_[1], kc("od4"), 0.0)
+        tt(o_[7], o_[7], A("bext"), ALU.add)
+        tt(A("ox", 212, 288, 5), o_[7], o_[8], ALU.add)
+        ts(A("ox", 144, 176), A("pt", 0, 32 * ne, ind=A("lp")), Q7, ALU.is_gt)
+        ts(A("ox", 176, 208), A("pt", 0, 32 * ne, ind=A("lp")), Q7, ALU.is_equal)
+        for i in range(4):
+            tt(A("ox", 208 + i, 288, 5), o_[9 + i], o_[2 + i], ALU.mult)
+        scan(A("ox", 288, 368), A("c5"), A("ox", 208, 288), 0.0, ALU.mult, ALU.add)
         if uL:
-            cp("v", A("lzx", 0, uL // 2), A("ox", 96 + (nL - uL) // 2, 96 + nL // 2))
+            cp("v", A("lzx", 0, uL // 2), A("ox", 292 + 5 * ((nL - uL) // 2), 288 + 5 * (nL // 2), 5))
         if uR:
-            cp("v", A("lzx", 8, 8 + uR // 2), A("ox", 96 + nL // 2, 96 + (nL + uR) // 2))
+            cp("v", A("lzx", 8, 8 + uR // 2), A("ox", 292 + 5 * (nL // 2), 288 + 5 * ((nL + uR) // 2), 5))
         for b in range(4):
             if uL:
                 zgather(b, 0, uL, "fe", XW, A("lzx", 0, uL // 2))

@@ -1,3 +1,4 @@
+import numpy as np
 from concourse.bass import DstId, RemoteDMATransfer
 from concourse.mybir import dt, AluOpType, AxisListType, ActivationFunctionType
 
@@ -8,10 +9,10 @@ BIG = 1.0e29
 FLOOR = 2.0 ** -100
 MAGIC = 12582912.0
 PW = 432
-XW = 320
-HX = 160
-B0 = 528
-ZC = B0 + 128
+T0 = 16
+Z0 = 96
+B0 = 576
+ZC = B0 + 3 * S
 F32, BF, I32, U16, CODE, PLANE = "float32", "bfloat16", "int32", "uint16", "float8_e4m3fn_x4", "uint8"
 WIDTH = {F32: 4, BF: 2, I32: 4, U16: 2, CODE: 4, PLANE: 1}
 
@@ -23,30 +24,28 @@ def _buf(dtype, **kw):
         SCRATCH[k] = ("sbuf", [128, n], dtype)
 
 
-_buf(BF, xin=1536, uin=512, vin=512, xt=1536, fb=4 * PW, fe=4 * XW, zt=4 * ZC, vt=512, ve=512, st=512, eb=2048,
-     mv=512, zer=512, fl32=32, frow=128, fone=128)
-_buf(CODE, tn=384, tq=512, tf=384, uq=128, vq=128, wq=512, eq=512, mq=128, sq=128, vcq=128, veq=128, zq=ZC, gq=384,
-     bq=192, lq0=224, lq1=224, lq2=224)
-_buf(PLANE, tns=384, tqs=512, tfs=384, uqs=128, vqs=128, wqs=512, eqs=512, mqs=128, sqs=128, vcqs=128, veqs=128,
-     zqs=ZC, gqs=384, bqs=192, lq0s=224, lq1s=224, lq2s=224)
-_buf(F32, kc=56, te=160, mo=160, mz=160, tc=16, ca=72, cb=72, cn=216, cq=144, tau=360, ctau=72, mc=24, acc=8, dump=64,
-     msg=4, sp=64, prow=76, oa=192, ox=416, bown=24, bext=16, pin=64, pt=64, kt=256, ki=128, inr=256, row=256, cg=32,
-     ct=32, cmp=256, cnt=4, c96=32, c5=80, z32=32, c98=128, pos=132, t7=68, th=68, cl=204, sums=8, lo=8, dk=96, xr=96,
-     rr=96, mm5=120, tmp=1536, ysb=384, olb=48, o8=48, io1=128, w0=24, w3=8, w4=8, w5=8, w6=8, w7=8,
-     thp=4, cl0=16, cl1=16, cl2=16, pl0=8, pl1=8, pl2=8)
-_buf(I32, pi=8)
-_buf(U16, l0=24, lf=24, lb=12, lv=4, lve=2, lz=24, lzx=16, lp=2, lc=2, ls=6, lm=24, lfo=4, lfx=2)
+_buf(BF, xin=1536, uin=512, vin=512, xt=1536, fb=4 * PW, zt=1536, ft=512, vt=512, st=512, eb=2048, mv=512, zer=512,
+     cmp=288, cnt=288, fone=128, fd=128)
+_buf(CODE, tn=384, tq=528, tf=384, uq=128, vq=128, wq=512, eq=512, mq=128, sq=128, vcq=128, fq=128, gq=384,
+     zq0=ZC, zq1=ZC, zq2=ZC)
+_buf(PLANE, tns=384, tqs=528, tfs=384, uqs=128, vqs=128, wqs=512, eqs=512, mqs=128, sqs=128, vcqs=128, fqs=128,
+     gqs=384, zq0s=ZC, zq1s=ZC, zq2s=ZC)
+_buf(F32, kc=64, te=120, mo=1048, mz=160, tc=24, ee=96, we=128, ww=128, wm=128, nb=120, t3=360, u3=360, tau=360,
+     tau2=360, dd=120, c3=144, c8=64, flo=24, wb=24, mc=8, acc=8, dump=64,
+     sp=64, prow=52, oa=144, la=96, lb=96, lo_=96, basec=48, bown=24, kt=256, kw=128, km=4, key=8, inr=256, row=256,
+     c78=128, pos=132, t7=68, th=68, cl=408, rs=6, sums=8, lo=6, lu=6, dk=144, mm5=144, tmp=1536, ysb=384,
+     olb=48, o8=48, io1=128, w0=24, w3=8, w4=8, w5=8, thp=4, cl0=128, cl1=128, cl2=128)
+_buf(I32, pi=8, xr=96)
+_buf(U16, l0=24, lf=24, lv=4, lz=48, ls=6, lm=24, l48=4, lw=44)
 
 SEMAPHORES = ["cv", "cs", "cp", "cg", "dx", "dx2", "du", "dv", "dw", "dws", "dol", "dy", "doc", "dos"] + [
-    "%s%d" % (k, t) for t in range(R) for k in ("ac", "as", "ak", "ap", "sc", "ss", "sk", "sp")]
+    "%s%d" % (k, t) for t in range(R) for k in ("ac", "as", "ak", "af", "ag", "sc", "ss", "sk", "sf", "sg")]
 COUNTER = {"v": "cv", "s": "cs", "p": "cp", "g": "cg"}
-CY, GAT, WAKE, PE, HOP, DMA = 0.95, 1.3, 200.0, 0.6, 2500.0, 2000.0
-FINE = ("oa", "ox", "tq", "mo", "mz", "te", "cn", "cq", "tc", "cmp", "cnt", "gq", "gqs", "xt", "tmp", "ca", "cb", "tau",
-        "th", "rr", "mm5", "cl", "pe", "fb", "fe")
-AHEAD = {'zt<fbi': 800, 'lz<oa': 800, 'vcq': 500, 'vt<fbi': 500, 'tau93': 300, 'tn': 800, 'ox112': -2000, 'cl2': -2000,
-         'cl0': -2000, 'cl136': -2000, 'kt': -300, 'cn1': -300, 'xr': -2000, 'cq59': 800, 'w5': 300, 'mm548': -800,
-         'eqgq': -800}
-SPARE = {'zt<fe': 0, 've<fei': -100}
+CY, GAT, WAKE, PE, HOP, DMA = 0.95, 1.4, 200.0, 0.6, 1900.0, 2000.0
+FINE = ("oa", "tq", "mo", "mz", "te", "cn", "cq", "tc", "gq", "gqs", "xt", "tmp", "ca", "cb", "tau",
+        "th", "rr", "mm5", "cl", "fb", "zt")
+SPARE, TRIES, SHAKE, SPAN = 60.0, 400, 300.0, 3000.0
+VARIANTS = ((200.0, 1.0, 1.0, 1.0), (150.0, 0.9, 0.8, 0.7), (260.0, 1.15, 1.2, 1.25))
 
 
 def A(name, c0=0, c1=None, step=1, p0=0, p1=128, ind=None, cast=None):
@@ -111,6 +110,87 @@ def schedule(ops):
     return order, done
 
 
+def plan(ops):
+    n = len(ops)
+    pre = []
+    for o in ops:
+        far = set()
+        for j in o["deps"]:
+            far |= ops[j]["hard"] if j in o["hard"] else set()
+        pre.append([(j, j in o["order"]) for j in o["deps"] if j not in far])
+    after = [[] for o in ops]
+    for i in range(n):
+        for j, soft in pre[i]:
+            after[j].append((i, soft))
+    way = [0.0] * n
+    for i in range(n - 1, -1, -1):
+        way[i] = min(ops[i]["cost"].values()) + max(
+            [way[j] + (0.0 if soft else ops[i]["lat"] + WAKE) for j, soft in after[i]] + [ops[i]["lat"]])
+
+    def place(prio):
+        left = [len(p) for p in pre]
+        ready = [i for i in range(n) if not left[i]]
+        busy, start, end, where = {}, [0.0] * n, [0.0] * n, [None] * n
+        while ready:
+            i = max(ready, key=lambda k: prio[k])
+            ready.remove(i)
+            at = max([end[j] + (0.0 if soft else ops[j]["lat"] + WAKE) for j, soft in pre[i]] + [0.0])
+            best = None
+            for q, c_ in ops[i]["cost"].items():
+                b, t, k = busy.setdefault(q, []), at, 0
+                lo_, hi_ = 0, len(b)
+                while lo_ < hi_:
+                    mid = (lo_ + hi_) // 2
+                    if b[mid][1] <= at:
+                        lo_ = mid + 1
+                    else:
+                        hi_ = mid
+                k = lo_
+                while k < len(b) and b[k][0] < t + c_:
+                    t = max(t, b[k][1])
+                    k += 1
+                x = (t + c_ + (SPARE if q == "v" else 0.0), t, q, k, c_)
+                if best is None or x < best:
+                    best = x
+            x, t, q, k, c_ = best
+            busy[q].insert(k, (t, t + c_))
+            start[i], end[i], where[i] = t, t + c_, q
+            for j, soft in after[i]:
+                left[j] -= 1
+                if not left[j]:
+                    ready.append(j)
+        return sorted(range(n), key=lambda k: (start[k], k)), where, start
+
+    def length(order, where):
+        tot = 0.0
+        for wake, fc, fp, fl in VARIANTS:
+            free, end, done = {}, [0.0] * n, [0.0] * n
+            for i in order:
+                q, t = where[i], free.get(where[i], 0.0)
+                for j, soft in pre[i]:
+                    x = end[j] if soft else done[j] + wake
+                    if x > t:
+                        t = x
+                end[i] = free[q] = t + ops[i]["cost"][q] * (fp if q == "p" else fc)
+                done[i] = end[i] + ops[i]["lat"] * fl
+            tot += max(done)
+        return tot
+
+    rng = np.random.default_rng(0)
+    prio = list(way)
+    order, where, start = place(prio)
+    best = length(order, where)
+    for it in range(TRIES):
+        at = rng.random() * max(start)
+        z = rng.normal(0.0, SHAKE, n)
+        trial = [prio[i] + (float(z[i]) if abs(start[i] - at) < SPAN else 0.0) for i in range(n)]
+        o2, w2, s2 = place(trial)
+        x = length(o2, w2)
+        if x <= best:
+            best, prio, order, where, start = x, trial, o2, w2, s2
+    return [(i, where[i]) for i in order]
+
+
 def rank_program(g, core, T, topo):
     r = T.rank_of(core)
     if r is None:
@@ -152,7 +232,7 @@ def rank_program(g, core, T, topo):
     def price(out, in_, k=1.0):
         if in_[6] is not None:
             return 55.0 + GAT * size(out)
-        if WIDTH[SCRATCH[out[0]][2]] == 2 and WIDTH[SCRATCH[in_[0]][2]] == 2:
+        if k == 1.0 and WIDTH[SCRATCH[out[0]][2]] == 2 and WIDTH[SCRATCH[in_[0]][2]] == 2:
             k = 0.5
         return CY * max(64.0, k * size(in_))
 
@@ -215,7 +295,7 @@ def rank_program(g, core, T, topo):
 
     def quant(name_, c0, c1, src, e0):
         o, s_, i_ = A(name_, c0, c1), A(name_ + "s", c0, c1), A(src, e0, e0 + 4 * (c1 - c0))
-        emit({"v": lambda e: e.quantize_mx(X(o), X(s_), X(i_))}, {"v": 12.0 + 0.27 * size(i_)}, [o, s_], [i_])
+        emit({"v": lambda e: e.quantize_mx(X(o), X(s_), X(i_))}, {"v": 14.0 + 0.25 * size(i_)}, [o, s_], [i_])
 
     def mm(bank, w, w0, x, x0, n, soft=()):
         o = A("ps", 512 * bank, 512 * bank + n)
@@ -244,7 +324,7 @@ def rank_program(g, core, T, topo):
             tot += len(es)
         i = emit({"g": lambda e: e.remote_dma_fused(trs, local_sem=T.sem[lsem])}, {"g": 300.0}, [],
                  [m_[0] for m_ in moves], lsem, tot, False, hop)
-        emit({"x": None}, {"x": 0.0}, [lands], [], rsem, inc, False, 0.0, [i])
+        emit({"x": None}, {"x": 0.0}, lands, [], rsem, inc, False, 0.0, [i])
 
     def share(k):
         return len(topo.engines(T.cores[k], core)) // (2 if 0 < k < N - 1 else 1)
@@ -252,19 +332,17 @@ def rank_program(g, core, T, topo):
     def ps(bank, c0, c1, step=1):
         return A("ps", 512 * bank + c0, 512 * bank + c1, step)
 
-    left, right = (r - 1 if r > 0 else None), (r + 1 if r < N - 1 else None)
-    sent = [8, 12, 12, 8]
-    nL = sent[left] if left is not None else 0
-    nR = sent[right] if right is not None else 0
-    uL, uR = [0, 6, 12, 8][r], [8, 12, 6, 0][r]
-    nx, n = nL + nR, uL + S + uR
-    mir = r >= N // 2
-    sg = -1 if mir else 1
-    n0 = S * (N - 1 - r) - uR if mir else S * r - uL
-    init = -float(S * (N - 1 - r) if mir else S * r)
-    nbs = [k for k in (left, right) if k is not None]
+    sent = [6, 12, 12, 6]
+    uL, uR = [0, 6, 11, 6][r + 0], [7, 11, 6, 0][r]
+    uL = [0, 6, 11, 7][r]
+    n, w0 = uL + S + uR, S * r - uL
+    upper = r >= N // 2
+    kb = 64 if upper else 0
+    blk = [2, 3, 5, 4] if upper else [0, 1, 3, 2]
+    i0 = w0 - kb
+    sh = 16 * (r % 2)
+    nbs = [k for k in (r - 1, r + 1) if 0 <= k < N]
     others = [k for k in range(N) if k != r]
-    ne = len(nbs)
     u8 = dt.uint8
     vs = "vs"
     K = {}
@@ -283,392 +361,318 @@ def rank_program(g, core, T, topo):
     iota(col("pi", 0), [[0, 1]], 0, 1)
     iota(A("w0"), [[1, 8], [128, 3]])
     iota(A("io1"), [[1, 128]])
-    iota(A("ctau", 0, 70), [[0, 7], [1, 10]], -5)
-    off = [0, 0, 32, 96]
-    iota(A("ki"), [[48, 4], [-sg, 32]])
+    iota(A("wb", 0, 8), [[16, 2], [2, 4]])
+    iota(A("t3"), [[0, 12], [1, 10], [0, 3]], -6)
     for a in range(4):
-        c_ = [(191 - 32 * d + off[a] if mir else 32 * d + off[a]) for d in (a, (a + 2) % 4)]
-        iota(A("thp", 0, 2, 1, 32 * a, 32 * a + 32), [[c_[1] - c_[0], 2]], c_[0] - 32 * a, -1)
-
-    def iotas_late():
-        for a in range(4):
-            c_ = []
-            for kk in range(2):
-                i = 191 - 32 * a - 16 * kk if mir else 32 * a + 16 * kk
-                s_ = i % S
-                c_.append(128 * int((s_ >= 32) != (a in (1, 2))) + 32 * (i // S) + s_ % 32)
-            iota(A("thp", 2, 4, 1, 32 * a, 32 * a + 32), [[c_[1] - c_[0], 2]], c_[0], 0)
-        iota(A("dk", 0, 24), [[sg * 9, 8], [sg * 128 * (n + 8), 3]])
-        iota(A("dk", 24, 96), [[0, 3], [sg, 8], [sg * 128 * n, 3]])
+        c_ = [-32 * blk[d] for d in (a, (a + 2) % 4)]
+        iota(A("thp", 0, 2, 1, 32 * a, 32 * a + 32), [[c_[1] - c_[0], 2]], c_[0], 0)
+    iota(A("dk", 24, 48), [[1, 8], [0, 3]])
 
     fill(A("zer"), 0.0)
     ts(col("pi", 1), col("pi", 0), 15, ALU.bitwise_and)
     ts(col("pi", 2), col("pi", 0), 4, ALU.arith_shift_right)
     ts(col("pi", 3), col("pi", 0), 7, ALU.bitwise_and)
-    ts(col("pi", 4), col("pi", 0), 16, ALU.bitwise_and)
+    ts(col("pi", 4), col("pi", 0), 31, ALU.bitwise_and)
     ts(col("pi", 5), col("pi", 0), 3, ALU.arith_shift_right, 1, ALU.bitwise_and)
     ts(col("pi", 6), col("pi", 0), 1, ALU.bitwise_and)
-    ts(col("pi", 7), col("pi", 0), 1, ALU.arith_shift_right)
-    P, Q, G, Q7, H16, QH, ODD, HALF = [kc(k) for k in ("p", "q", "g", "q7", "h16", "qh", "odd", "half")]
+    ts(col("pi", 7), col("pi", 0), 1, ALU.arith_shift_right, 7, ALU.bitwise_and)
+    P, Q, G, Q7, LANE, QH, ODD, SLOT = [kc(k) for k in ("p", "q", "g", "q7", "lane", "qh", "odd", "slot")]
     cp("v", A("kc", 0, 8), A("pi", 0, 8))
     aff(vs, kc("q8"), Q, 8.0, 0.0)
-    aff(vs, kc("fin"), Q7, 48.0, QH)
     ts(A("l0"), A("w0"), kc("q8"), ALU.add)
-    quant("tq", 384, 512, "zer", 0)
-    aff(vs, A("bown"), A("io1", 0, 48, 2), 1.0, kc("fin"))
-    cp("v", A("lf"), A("bown"))
-    if ne == 2:
-        cp("v", A("lb", 0, 6), A("bown", 0, 6))
-        cp("v", A("lb", 6, 12), A("bown", 18, 24))
-    ts(kc("eb"), P, 48.0, ALU.is_ge, BIG, ALU.mult)
-    fill(A("mo"), BIG)
+    quant("tq", 0, 128, "zer", 0)
+    quant("tq", 400, 528, "zer", 0)
+    ts(kc("eb"), P, float(sh + 23.5), ALU.subtract)
+    act(kc("eb"), kc("eb"), ACT.Abs)
+    ts(kc("eb"), kc("eb"), 24.0, ALU.is_ge, BIG, ALU.mult)
+    fill(A("mo", 7, 1048, 8), BIG)
     fill(A("te"), BIG)
     fill(A("mz"), 0.0)
     quant("uq", 0, 128, "uin", 0)
     quant("tn", 0, 192, "xin", 0)
     quant("tn", 192, 384, "xin", 768)
-    pick("tq", 0, 384, "tn", 384, A("l0"))
+    pick("tq", T0, 384, "tn", 384, A("l0"))
     quant("vq", 0, 128, "vin", 0)
     for b in range(4):
         cp(vs, A("eb", 512 * b, 512 * b + 512), A("zer"))
         ts(A("eb", 512 * b + b, 512 * b + 512, 4), A("io1"), P, ALU.is_equal)
         quant("eq", 128 * b, 128 * b + 128, "eb", 512 * b)
-    if ne == 1:
-        for t in range(R):
-            quant("lq%d" % t, 96, 224, "zer", 0)
-    aff(vs, A("ctau", 50, 60), A("ctau", 50, 60), 1.0, 3.5)
+    aff(vs, kc("fin"), Q7, 48.0, QH)
+    aff(vs, A("bown"), A("io1", 0, 48, 2), 1.0, kc("fin"))
+    ts(A("lf"), A("bown"), float(T0), ALU.add)
+    aff(vs, A("t3", 330, 360, 3), A("t3", 330, 360, 3), 1.0, 3.5)
     fill(A("sp"), 0.0)
     cp(vs, A("mv"), A("zer"))
     fill(A("sp", 0, 64, 4), 1.0)
     ts(A("sp", 1, 64, 4), A("io1", 0, 16), Q, ALU.is_equal)
-    aff(vs, A("sp", 2, 32, 4), A("sp", 0, 32, 4), ODD, -1.0)
-    aff(vs, A("sp", 2, 32, 4), A("sp", 2, 32, 4), -1.0, 0.0)
-    aff(vs, A("sp", 34, 64, 4), A("sp", 0, 32, 4), ODD, 0.0)
-    ts(A("mv", 0, 192, 4), A("io1", 0, 48), P, ALU.is_equal)
-    ts(A("mv", 193, 204, 4), A("io1", 0, 3), G, ALU.is_equal)
-    ts(A("mv", 4 * 52 + 2, 4 * 76, 4), A("io1", 0, 24), HALF, ALU.is_equal)
+    ts(A("mv", 0, 192, 4), A("io1", sh, sh + 48), P, ALU.is_equal)
+    ts(A("mv", 193, 204, 4), A("io1", sh // 16, sh // 16 + 3), G, ALU.is_equal)
     quant("mq", 0, 128, "mv", 0)
     ts(kc("g7"), G, 7.0, ALU.is_equal)
     cp(vs, A("vt"), A("zer"))
-    cp(vs, A("ve"), A("zer"))
-    cp(vs, A("zt", 4 * B0, 4 * ZC), A("zer"))
-    if 8 * n < B0:
-        fill(A("zt", 32 * n, 4 * B0), 0.0)
-        quant("zq", B0 - 128, B0, "zer", 0)
-    fill(A("z32"), 0.0)
+    cp(vs, A("ft"), A("zer"))
     aff(vs, kc("al"), kc("g7"), -0.5, -0.5)
     aff(vs, kc("be"), kc("g7"), -3.5, 3.5)
-    aff(vs, kc("q16"), Q, 1.0, 16.0)
-    aff(vs, kc("q32"), Q, 1.0, 32.0)
-    aff(vs, kc("w2"), Q7, -48.0, 384.0)
-    aff(vs, kc("w2x"), Q7, -1.0, float(HX))
-    aff(vs, kc("ev4"), QH, -4.0, 4.0)
-    aff(vs, kc("od4"), QH, 4.0, 0.0)
-    aff(vs, kc("ev"), QH, -1.0, 1.0)
-    aff(vs, kc("ev8"), QH, 8.0, -8.0)
-    aff(vs, kc("od8"), QH, -8.0, 0.0)
-    aff(vs, kc("wev"), kc("w2x"), kc("ev"), 0.0)
-    aff(vs, kc("wod"), kc("w2x"), QH, 0.0)
-    aff(vs, kc("wev4"), kc("wev"), -4.0, 0.0)
-    aff(vs, kc("wod4"), kc("wod"), -4.0, 0.0)
-    aff(vs, A("bext", 0, 16), A("io1", 0, 16), 16.0, Q)
-
-    def consts_c():
-        for d in range(2):
-            ts(A("kt", d, 256, 2), A("ki"), col("thp", d), ALU.is_lt, -2.0 ** -24, ALU.mult)
-        aff(vs, A("kt"), A("kt"), 1.0, 1.0)
-        aff(vs, kc("sq"), Q, float(sg), 0.0)
-        aff(vs, A("w3", 0, 6), A("io1", 0, 96, 16), 1.0, Q)
-        z8 = 47.0 if mir else 0.0
-        ts(kc("up"), P, 64.0, ALU.is_ge)
-        ca_, cb_, da_, db_ = (-4096.0, 1024.0, 4095.0, 1.125) if mir else (-4097.0, 1025.125, 4096.0, 0.0)
-        aff(vs, kc("ta"), kc("up"), da_ - ca_, ca_)
-        aff(vs, kc("tb"), kc("up"), db_ - cb_, cb_)
-        aff(vs, kc("lo"), kc("up"), 0.0 if mir else -0.125, z8)
-        aff(vs, kc("hi"), kc("up"), 0.125 if mir else 0.0, z8 + 1)
-        aff(vs, A("lo", 0, 3), A("w3", 0, 3), float(sg), kc("lo"))
-        aff(vs, A("lo", 4, 7), A("w3", 0, 3), float(sg), kc("hi"))
-        tab = [(n + 8, 1.125, n - 3.5 / 8 - (8 * n - 1 if mir else 0)),
-               (n, 0.125, n - 3.5 / 8 + (-(B0 + n - 1) if mir else B0 - 1)),
-               (n, 0.125, 1.125 * n - 0.5 if mir else n - 0.375), (n, 0.125, 1.125 * n - 0.375 if mir else n - 0.5)]
-        for i, (a_, b_, c_) in enumerate(tab):
-            aff(vs, kc("d%d" % i), Q, float(sg * a_), c_ + (47 * a_ + 7 * b_ if mir else 0.0))
-            aff(vs, A("dk", 24 * i, 24 * i + 24), A("dk", 24 * i, 24 * i + 24), 0.125, kc("d%d" % i))
-        ts(A("lc"), A("thp", 2, 4), kc("sq"), ALU.add)
-        aff(vs, A("w4", 0, 6), A("w3", 0, 6), 1.0 / 3, -1.0 / 3)
-        ts(A("w4", 0, 6), A("w4", 0, 6), MAGIC, ALU.add, MAGIC, ALU.subtract)
-        ts(A("w5", 0, 6), A("w3", 0, 6), 48.0, ALU.is_ge, kc("up"), ALU.not_equal)
-        tt(A("w4", 0, 6), A("w5", 0, 6), A("w4", 0, 6), ALU.subtract)
-        aff(vs, A("w4", 0, 6), A("w4", 0, 6), 3.0, 0.0)
-        tt(A("w4", 0, 6), A("w4", 0, 6), A("w3", 0, 6), ALU.add)
-        cp("v", A("ls"), A("w4", 0, 6))
-        fill(A("c96"), 96.0)
-        fill(A("c5"), 1.0)
-        fill(A("c5", 0, 80, 5), 0.0)
-        fill(A("c98"), 1.125)
-        fill(col("pos", 0), init)
-        fill(A("sums"), 0.0)
-        for b in range(4):
-            cp(vs, A("fe", XW * b + 8 * nx, XW * b + XW), A("zer", 0, XW - 8 * nx))
-        f0 = float(n0 + n - 1 if mir else n0)
-        ts(A("w6", 0, 3), A("w3", 0, 3), 24.0, ALU.is_ge, -23.5, ALU.mult)
-        tt(A("w6", 0, 3), A("w6", 0, 3), A("w3", 0, 3), ALU.add)
-        aff("v", A("lfo", 0, 3), A("w6", 0, 3), 2.0 * sg, f0 + sg * uL)
-        aff(vs, A("w7", 0, 2), A("io1", 0, 2), 0.5, Q)
-        ts(A("w7", 2, 4), A("w7", 0, 2), nL / 2.0, ALU.is_ge)
-        aff(vs, A("w6", 4, 6), A("w7", 2, 4), 24.0, 0.0)
-        tt(A("w6", 4, 6), A("w6", 4, 6), A("w7", 0, 2), ALU.add)
-        aff(vs, A("w6", 4, 6), A("w6", 4, 6), 2.0 * sg, f0 - sg * (nL - uL))
-        ts(A("lfx"), A("w6", 4, 6), 0.0, ALU.max, 127.0, ALU.min)
-        if ne == 2:
-            aff(vs, A("w7", 4, 6), A("w7", 2, 4), 8.0, (16 - nL) / 2.0)
-            tt(A("w7", 4, 6), A("w7", 4, 6), A("w7", 0, 2), ALU.add)
-            ts(A("w7", 4, 6), A("w7", 4, 6), 2.0, ALU.mult, 47.0, ALU.min)
-        else:
-            aff(vs, A("w7", 4, 6), A("w7", 0, 2), 2.0, float(16 - nL if nL else 0))
-            ts(A("w7", 4, 6), A("w7", 4, 6), 15.0, ALU.min)
-        ts(A("lp"), A("w7", 4, 6), H16, ALU.add)
-        if nL:
-            ts(kc("xl"), Q, float(nL - 16), ALU.add, 0.0, ALU.max)
-            aff(vs, kc("xl"), kc("xl"), 8.0, 0.0)
-        if nR:
-            ts(kc("xr"), Q, float(nR - 1), ALU.min, float(nL), ALU.add)
-            aff(vs, kc("xr"), kc("xr"), 8.0, 0.0)
-
-    def slots(buf, p, w, base, stride, w2):
-        a_, b_, c_ = [A(buf, k * w, k * w + w) for k in (3, 4, 5)]
-        ts(a_, p, Q7, ALU.is_gt, stride, ALU.mult)
-        ts(b_, p, Q7, ALU.is_equal, w2, ALU.mult)
-        ts(c_, p, Q7, ALU.is_le, stride, ALU.mult)
-        tt(a_, a_, b_, ALU.add)
-        tt(A(buf, 0, w), a_, base, ALU.add)
-        tt(c_, c_, a_, ALU.subtract)
-        aff(vs, A(buf, w, 2 * w), c_, kc("ev4"), 0.0)
-        aff(vs, A(buf, 2 * w, 3 * w), c_, kc("od4"), 0.0)
-
-    def choose(buf, w, lst):
-        tt(A(buf, 6 * w, 8 * w), A("frow", ind=lst), A(buf, w, 3 * w), ALU.mult)
-        tt(A(buf, 6 * w, 7 * w), A(buf, 6 * w, 7 * w), A(buf, 7 * w, 8 * w), ALU.add)
-        tt(A(buf, 6 * w, 7 * w), A(buf, 6 * w, 7 * w), A(buf, 0, w), ALU.add)
-
-    def zgather(b, z0, k, src, w, lst):
-        cp(vs, A("zt", 32 * z0 + b, 32 * (z0 + k), 4), A(src, w * b, w * b + w, ind=lst))
+    aff(vs, kc("al48"), kc("al"), 48.0, 0.0)
+    aff(vs, kc("be48"), kc("be"), 48.0, Q)
+    aff(vs, A("w3", 0, 6), A("io1", 0, 96, 16), 1.0, Q)
+    aff(vs, A("w5", 0, 3), A("io1", 0, 48, 16), 1.0, kc("be48"))
+    cp("v", A("l48", 0, 3), A("w3", 0, 3))
+    aff(vs, kc("ns"), SLOT, -1.0, -0.5)
+    aff(vs, kc("w2"), SLOT, -1.0, 8.0)
+    aff(vs, kc("sb"), SLOT, 48.0, 0.0)
+    aff(vs, kc("sb"), ODD, 2.0 * PW, kc("sb"))
+    aff(vs, A("basec"), A("io1", 0, 48), 1.0, kc("sb"))
+    fill(A("la"), 0.0)
+    ts(kc("mid"), P, 63.5, ALU.subtract)
+    act(kc("mid"), kc("mid"), ACT.Abs)
+    ts(kc("mid"), kc("mid"), 32.0, ALU.is_lt)
+    aff(vs, kc("h+"), kc("mid"), 32.0, LANE)
+    aff(vs, kc("h-"), kc("mid"), -32.0, LANE)
+    for i, k in enumerate(others + [r]):
+        h, a_ = (("h+", 0), ("h-", 16), ("h-", 32), ("h+", -16))[k]
+        ts(A("kw", 32 * i, 32 * i + 32), A("io1", 0, 32), kc(h), ALU.subtract, float(S * k + a_), ALU.subtract)
+        ts(col("km", k), col("kw", 32 * i), LANE, ALU.add, col("thp", 0), ALU.not_equal)
+    for d in range(2):
+        ts(A("kt", d, 256, 2), A("kw"), col("thp", d), ALU.is_gt, -2.0 ** -24, ALU.mult)
+    aff(vs, A("kt"), A("kt"), 1.0, 1.0)
+    aff(vs, A("km"), A("km"), BIG, 0.0)
+    for i in (2, 4, 6):
+        ts(kc("g%d" % i), Q7, float(i), ALU.is_ge)
+    ts(kc("c0"), kc("g4"), kc("g6"), ALU.add, QH, ALU.add)
+    ts(kc("isn"), kc("g2"), kc("g6"), ALU.subtract)
+    ts(kc("x"), Q7, kc("g4"), ALU.subtract, 1.0, ALU.max)
+    ts(kc("x"), kc("x"), 5.0, ALU.min, QH, ALU.add)
+    aff(vs, kc("x"), kc("x"), 8.0, -9.0)
+    aff(vs, kc("c1"), kc("isn"), 32.0, kc("c0"))
+    ts(A("lw", 0, 8), A("wb", 0, 8), kc("c1"), ALU.add)
+    ts(A("lw", 8, 16), A("wb", 0, 8), QH, ALU.add, 1.0, ALU.add)
+    ts(A("wb", 8, 12), A("io1", 0, 64, 16), kc("x"), ALU.add, 7.0, ALU.max)
+    ts(A("lw", 16, 20), A("wb", 8, 12), 79.0, ALU.min)
+    fill(A("ee"), BIG)
+    fill(A("c8"), 0.0)
+    fill(A("c8", 0, 64, 8), BIG)
+    fill(A("c3"), 1.0)
+    fill(A("c3", 0, 144, 3), 0.0)
+    fill(A("tau", 90, 126), 0.0)
+    fill(A("flo"), FLOOR)
+    cp(vs, A("cmp", 256, 288), A("zer", 0, 32))
+    ts(kc("up"), P, 64.0, ALU.is_ge)
+    far = N * C if upper else 0
+    aff(vs, kc("ta"), kc("up"), -1024.0, 512.0)
+    aff(vs, kc("tb"), kc("up"), 128.0 - 0.875, 0.875)
+    aff(vs, kc("sc"), kc("up"), -1.0 / 9, 1.0)
+    aff(vs, kc("-sc"), kc("sc"), -1.0, 0.0)
+    aff(vs, kc("lo"), kc("up"), -0.125, float(S * r - far // 8))
+    ts(A("lo", 0, 3), A("w3", 0, 3), kc("lo"), ALU.add, kc("-sc"), ALU.mult)
+    ts(A("lo", 3, 6), A("w3", 0, 3), float(S * r - far // 8 + 1), ALU.add, kc("-sc"), ALU.mult)
+    kj, kf = C * r - 8 * (S * r - Z0 // 8) + 8 * w0 - far, B0 + S - S * r + w0 + 2 * n - 1
+    aff(vs, A("dk", 0, 24), A("w0"), 1.0, kc("q8"))
+    aff(vs, A("dk", 48, 72), A("dk", 24, 48), 1.0 / 9, -3.0 / 9)
+    aff(vs, A("dk", 72, 96), A("dk", 24, 48), 1.0 / 9, -4.0 / 9)
+    aff(vs, A("dk", 96, 120), A("dk", 24, 48), 0.125, kj - 3.5 / 8)
+    aff(vs, A("dk", 120, 144), A("dk", 24, 48), 1.0 / 9, kf - kj - 3.0 / 9)
+    tt(A("dk", 96, 120), A("dk", 96, 120), A("dk", 0, 24), ALU.add)
+    tt(A("dk", 120, 144), A("dk", 120, 144), A("dk", 0, 24), ALU.subtract)
+    fill(A("mm5", 48, 96, 2), 0.0)
+    aff(vs, A("w4", 0, 6), A("w3", 0, 6), 1.0 / 3, -1.0 / 3)
+    ts(A("w4", 0, 6), A("w4", 0, 6), MAGIC, ALU.add, MAGIC, ALU.subtract)
+    ts(A("dump", 0, 6), A("w3", 0, 6), 24.0, ALU.is_ge, kc("up"), ALU.not_equal)
+    tt(A("w4", 0, 6), A("dump", 0, 6), A("w4", 0, 6), ALU.subtract)
+    aff(vs, A("w4", 0, 6), A("w4", 0, 6), 3.0, 0.0)
+    tt(A("w4", 0, 6), A("w4", 0, 6), A("w3", 0, 6), ALU.add)
+    cp("v", A("ls"), A("w4", 0, 6))
+    fill(A("c78"), 0.875)
+    fill(col("pos", 0), 0.0)
+    fill(A("sums"), 0.0)
 
     def score(out, gr, bias=0.0):
         act(out, A("ps", 16 * gr, 3585 + 16 * gr, 512), ACT.Abs, bias=bias)
 
-    def level(o, eo, do, w, held=True):
-        tt(A("te", 2 * eo + 2, 2 * (eo + w) + 2, 2), odd("mo", o, w), odd("mo", o + 2, w), ALU.min)
-        if held:
-            cp(vs, odd("mz", o + 1, w), odd("mo", o + 1, w))
-        scan(A("mo", 2 * do + 2, 2 * (do + w) + 2), A("mz", 2 * o + 2, 2 * (o + w) + 2),
+    def mo(o, w):
+        return A("mo", 8 * o + 7, 8 * (o + w), 8)
+
+    def third(buf, k, o, w):
+        return A(buf, 3 * o + k, 3 * (o + w), 3)
+
+    def level(o, zo, eo, do, w):
+        tt(A("te", 2 * eo + 2, 2 * (eo + w) + 2, 2), mo(o, w), mo(o + 2, w), ALU.min)
+        cp(vs, odd("mz", zo + 1, w), mo(o + 1, w))
+        scan(A("mo", 8 * do + 11, 8 * (do + w) + 8, 4), A("mz", 2 * zo + 2, 2 * (zo + w) + 2),
              A("te", 2 * eo + 2, 2 * (eo + w) + 2), 0.0, ALU.min, ALU.max)
 
+    def weights(o, c_, e_):
+        cp("s", A("we", o, o + 128), e_)
+        tt(A("ww", o, o + 128), c_, A("we", o, o + 128), ALU.max)
+
+    def twice(o, do, wo, k, lst):
+        tt(A("wm", wo, wo + 64 * k), A("mo", 8 * o, 8 * o + 80 * k, ind=lst), A("ww", wo, wo + 64 * k), ALU.max)
+        for i in range(k):
+            scan(A("mo", 8 * (do + 10 * i) + 8, 8 * (do + 10 * i) + 72), A("c8"),
+                 A("wm", wo + 64 * i, wo + 64 * i + 64), 0.0, ALU.max, ALU.min)
+
+    def back(o, w):
+        tt(A("nb", o - 2, o + w), mo(o - 2, w + 2), mo(o - 1, w + 2), ALU.min)
+        tt(third("t3", 1, o, w), A("nb", o - 2, o + w - 2), mo(o, w), ALU.is_le)
+        tt(third("t3", 2, o, w), mo(o - 1, w), A("nb", o, o + w), ALU.is_le)
+        scan(A("tau", 3 * o, 3 * (o + w)), A("c3", 0, 3 * w), A("t3", 3 * o, 3 * (o + w)), 0.0, ALU.mult, ALU.add)
+
+    def back2(o, w):
+        tt(A("dd", o, o + w + 1), third("tau", 2, o, w + 1), third("tau", 2, o - 1, w + 1), ALU.subtract)
+        cp(vs, third("u3", 0, o, w), third("tau", 2, o - 1, w))
+        tt(third("u3", 1, o, w), A("dd", o, o + w), third("t3", 1, o - 20, w), ALU.mult)
+        tt(third("u3", 2, o, w), A("dd", o + 1, o + w + 1), third("t3", 2, o - 20, w), ALU.mult)
+        scan(A("tau2", 3 * o, 3 * (o + w)), A("c3", 0, 3 * w), A("u3", 3 * o, 3 * (o + w)), 0.0, ALU.mult, ALU.add)
+
+    def borders(buf, w, lo_, hi_, to_left, to_right, cast):
+        mv_, lands = [], []
+        for k in nbs:
+            if k < r:
+                mv_.append((A(buf[0], lo_, lo_ + w[r], cast=cast), A(buf[1], to_left, to_left + w[r], cast=cast), [k]))
+                lands.append(A(buf[1], to_right - w[k], to_right))
+            else:
+                mv_.append((A(buf[0], hi_ - w[r], hi_, cast=cast), A(buf[1], to_right - w[r], to_right, cast=cast), [k]))
+                lands.append(A(buf[1], to_left, to_left + w[k]))
+        return mv_, lands
+
     for t in range(R):
-        lq, cl, pl = "lq%d" % t, "cl%d" % t, "pl%d" % t
+        zq, cl = "zq%d" % t, "cl%d" % t
         for l in range(L - 1, -1, -1):
-            mm(l, "tq", 48 * l, "uq", 0, 128)
-        ns = 8 * sent[r]
-        lst = A("lb") if ne == 2 else (A("lf", 20, 24) if r == 0 else A("lf", 0, 4))
-        pick("bq", 0, ns * ne, "tq", 384, lst)
-        for nm, cast, rs, ls_ in (("", u8, "ac", "sc"), ("s", None, "as", "ss")):
-            mv_ = []
-            for i, k in enumerate(nbs):
-                d0 = 0 if k > r or k == 0 else 8 * sent[k - 1]
-                mv_.append((A("bq" + nm, ns * i, ns * i + ns, cast=cast), A(lq + nm, d0, d0 + ns, cast=cast), [k]))
-            remote(mv_, "%s%d" % (rs, t), "%s%d" % (ls_, t), A(lq + nm, 0, 8 * nx), sum(share(k) for k in nbs),
-                   HOP + 600)
-        if t == 0:
-            iotas_late()
-            consts_c()
-        score(odd("mo", 1, 8), 0, kc("eb"))
-        score(odd("mo", 11, 8), 7)
-        for k in range(1, 4):
-            score(odd("te", 20 * k + 1, 8), k)
-            score(odd("te", 20 * k + 11, 8), 7 - k)
-        score(odd("te", 11, 8), 7)
-        ts(odd("te", 71, 8), odd("te", 71, 8), FLOOR, ALU.max)
+            mm(l, "tq", T0 + 48 * l - sh, "uq", 0, 128)
+        score(mo(1, 8), 0, kc("eb"))
+        score(mo(11, 8), 7)
+        for o, gr in enumerate((1, 6, 2, 5, 3, 4)):
+            score(odd("te", 10 * o + 1, 8), gr)
+        for o, gr in enumerate((5, 7, 4, 6)):
+            score(A("ee", 16 * o + 1, 16 * o + 9), gr)
         for b in range(4):
-            mm(b, "eq", 128 * b, "tq", 0, 384)
-        for b in range(4):
-            mm(4 + b, "eq", 128 * b, lq, 0, max(128, 8 * nx))
+            mm(b, "eq", 128 * b, "tq", T0, 384)
         for b in range(4):
             cp("s", A("fb", PW * b, PW * b + 384), ps(b, 0, 384))
         for o in (0, 20, 40):
-            level(o, o + 20, o + 20, 18)
-        tt(A("tc", 0, 16, 2), odd("mo", 60, 8), odd("mo", 62, 8), ALU.min)
-        cp(vs, odd("tc", 0, 8), odd("mo", 71, 8))
-        cp(vs, odd("mz", 61, 8), odd("mo", 61, 8))
-        scan(A("mc", 0, 16), A("mz", 122, 138), A("tc"), 0.0, ALU.min, ALU.max)
-        red(col("msg", 0, 0, 64), A("mc", 1, 16, 2, 0, 64), ALU.min)
-        red(col("msg", 0, 64, 96), A("mc", 1, 16, 2, 32, 64), ALU.min)
-        red(col("msg", 0, 96, 128), A("mc", 1, 16, 2, 0, 32), ALU.min)
-        remote([(col("msg", 0), col(cl, 4 * r), others)], "ak%d" % t, "sk%d" % t, A(cl),
+            level(o, o, o, o + 20, 18)
+        for x in range(3):
+            tt(A("tc", 8 * x, 8 * x + 8), mo(60 + x, 8), mo(71, 8), ALU.max)
+        for a, b, w in ((0, 0, 64), (64, 32, 32), (96, 0, 32)) if r in (0, 3) else ((0, 32, 32), (32, 0, 32), (64, 0, 64)):
+            scan(A(cl, 32 * r + 8, 32 * r + 32, 1, a, a + w), A("tc", 0, 24, 1, b, b + w), A("flo", 0, 24, 1, b, b + w),
+                 BIG, ALU.min, ALU.max)
+        cost = [col(cl, 32 * k + 31) for k in range(N)]
+        remote([(cost[r], cost[r], others)], "ak%d" % t, "sk%d" % t, [cost[k] for k in others],
                sum(len(topo.engines(T.cores[k], core)) for k in others), HOP + 300)
-        level(60, 70, 10, 8, False)
-        for o in (10, 30, 50):
-            level(o, 60 - o, o + 20, 8)
-        scan(A("mc", 16, 24), odd("mo", 71, 8), odd("mo", 71, 8), BIG, ALU.min, ALU.min)
-        for o, w in ((0, 49), (59, 10), (50, 9)):
-            tt(A("ca", o, o + w), odd("mo", o, w), odd("mo", o + 1, w), ALU.is_le)
-            tt(A("cb", o, o + w), odd("mo", o, w), odd("mo", o + 2, w), ALU.is_le)
-            tt(A("cn", o + 1, o + w), A("cb", o, o + w - 1), A("ca", o + 1, o + w), ALU.max)
-            tt(A("cq", o, o + w), A("ca", o, o + w), A("cb", o, o + w), ALU.mult)
-            tt(A("cq", 72 + o, 72 + o + w), A("cq", o, o + w), A("ctau", o, o + w), ALU.add)
-            tt(A("tau", o + 1, o + w), A("cn", o + 1, o + w), A("cq", 73 + o, 72 + o + w), ALU.add)
-        tt(A("cn", 73, 120), A("cn", 1, 48), A("cq", 1, 48), ALU.max)
-        tt(A("cn", 145, 192), A("cn", 1, 48), A("cq", 1, 48), ALU.mult)
-        for o, w in ((21, 17), (61, 7)):
-            tt(A("tau", 72 + o, 73 + o + w), A("tau", o, o + w + 1), A("tau", o - 1, o + w), ALU.subtract)
-            tt(A("tau", 144 + o, 144 + o + w), A("tau", 72 + o, 72 + o + w), A("cn", 52 + o, 52 + o + w), ALU.mult)
-            tt(A("tau", 216 + o, 216 + o + w), A("tau", 73 + o, 73 + o + w), A("cn", 124 + o, 124 + o + w), ALU.mult)
-            tt(A("tau", 144 + o, 144 + o + w), A("tau", 144 + o, 144 + o + w), A("tau", o - 1, o + w - 1), ALU.add)
-            tt(A("tau", 288 + o, 288 + o + w), A("tau", 144 + o, 144 + o + w), A("tau", 216 + o, 216 + o + w), ALU.add)
-        act(A("dump", 56, 64), A("mc", 16, 24), ACT.Sign, bias=col("mc", 23), scale=-1.0, accum=col("acc", 7))
+        for b in range(4):
+            cp(vs, A("ft", b, 4 * S, 4), A("fb", PW * b, PW * b + S))
+        quant("fq", 0, 128, "ft", 0)
+        pick(zq, B0 + S, S, "fq", 128, A("l48", 0, 3))
+        for nm, cast, rs, ls_ in (("", u8, "af", "sf"), ("s", None, "ag", "sg")):
+            m1, l1 = borders(("fq" + nm, zq + nm), [8, 12, 12, 8], 0, S, B0 + 2 * S, B0 + S, cast)
+            remote(m1, "%s%d" % (rs, t), "%s%d" % (ls_, t), l1, sum(share(k) for k in nbs))
+        tt(A("ee", 64, 89), A("ee", 32, 57), A("ee", 33, 58), ALU.min)
+        weights(0, A("ee", 32, 96, ind=A("lw", 0, 8)), A("ee", 0, 32, ind=A("lw", 8, 16)))
+        twice(60, 100, 0, 1, A("lw", 16, 20))
+        twice(100, 120, 64, 1, A("lw", 16, 20))
+        level(60, 60, 50, 80, 8)
+        level(100, 70, 10, 110, 8)
+        scan(A("mc", 0, 8), mo(121, 8), mo(121, 8), BIG, ALU.min, ALU.min)
+        for o, w in ((2, 28), (42, 28), (82, 28), (112, 7)):
+            back(o, w)
+        for o, w in ((22, 47), (102, 7)):
+            back2(o, w)
+        act(A("dump", 56, 64), A("mc", 0, 8), ACT.Sign, bias=col("mc", 7), scale=-1.0, accum=col("acc", 7))
         for gr, to in ((7, 6), (6, 4), (6, 5), (4, 2), (4, 3), (2, 0), (2, 1)):
-            o = [0, 20, 40, 60, 10, 30, 50][gr - 1] + (288 if gr - to == 2 else 0)
-            act(A("dump", 8 * to, 8 * to + 7), A("tau", o + 1, o + 8), ACT.Sign, bias=col("acc", gr),
-                scale=1.0 if gr == 7 else 2.0, accum=col("acc", to))
+            o = [2, 22, 42, 62, 82, 102, 112][gr - 1]
+            act(A("dump", 8 * to, 8 * to + 7), third("tau2" if gr - to == 2 else "tau", 2, o, 7), ACT.Sign,
+                bias=col("acc", gr), scale=1.0 if gr == 7 else 2.0, accum=col("acc", to))
         for gr in range(7, -1, -1):
             aff(vs, A("st", 64 * gr, 64 * gr + 64), A("sp"), col("acc", gr), 0.0)
         quant("sq", 0, 128, "st", 0)
-        mm(0, "sq", 0, "mq", 0, 128)
-        for b in range(4):
-            cp("s", A("fe", XW * b, XW * b + 8 * nx), ps(4 + b, 0, 8 * nx))
-        aff("v", A("prow", 0, 76), ps(0, 0, 76), kc("al"), kc("be"))
-        mv_ = []
-        if left is not None:
-            mv_.append((col("prow", 48), col(pl, 4), [left]))
-        if right is not None:
-            mv_.append((col("prow", 50), col(pl, 0), [right]))
-        remote(mv_, "ap%d" % t, "sp%d" % t, A(pl), sum(share(k) for k in nbs))
-        for m_, qq in enumerate((Q, kc("q16"), kc("q32"))):
-            aff("v", col("lv", m_), col("prow", 48 + m_), 48.0, qq)
+        mm(4, "sq", 0, "mq", 0, 128)
+        for m_ in range(3):
+            aff("v", col("lv", m_), ps(4, 48 + m_, 49 + m_), kc("al48"), col("w5", m_))
+        aff("v", A("prow", 0, S), ps(4, 0, S), kc("al"), kc("be"))
         for b in range(4):
             cp(vs, A("vt", b, 192, 4), A("fb", PW * b, PW * b + 384, ind=A("lv", 0, 3)))
         quant("vcq", 0, 128, "vt", 0)
         for b in range(4):
-            mm(4 + b, "wq", 128 * b, "vcq", 0, 128)
-        slots("oa", A("prow", 52, 76), 24, A("bown"), 48.0, kc("w2"))
+            mm(4 + (b + 1) % 4, "wq", 128 * b, "vcq", 0, 128)
         for b in range(4):
-            relu("s", A("fb", PW * b + 384, PW * b + 432), ps(4 + b, 0, 48), 0.03125)
-        for b in range(4):
-            cp(vs, A("zt", 4 * (B0 + uL) + b, 4 * (B0 + uL + S), 4), A("fb", PW * b, PW * b + S))
-            if uL:
-                cp(vs, A("zt", 4 * B0 + b, 4 * (B0 + uL), 4), A("fe", XW * b + 8 * (nL - uL), XW * b + 8 * nL, 8))
-            if uR:
-                cp(vs, A("zt", 4 * (B0 + uL + S) + b, 4 * (B0 + n), 4),
-                   A("fe", XW * b + 8 * nL, XW * b + 8 * (nL + uR), 8))
-        quant("zq", B0, ZC, "zt", 4 * B0)
+            relu(vs, A("fb", PW * b + 384, PW * b + 432), ps(4 + (b + 1) % 4, 0, 48), 0.03125)
+        act(A("oa", 0, 48), A("prow", 0, S), ACT.Sign, bias=kc("ns"))
+        ts(A("oa", 48, 96), A("prow", 0, S), SLOT, ALU.is_equal, kc("w2"), ALU.mult)
+        ts(A("oa", 96, 144), A("prow", 0, S), SLOT, ALU.is_le, 48.0, ALU.mult)
+        tt(odd("la", 0, S), A("oa", 0, 48), A("oa", 48, 96), ALU.add)
+        tt(odd("lb", 0, S), A("oa", 96, 144), A("basec"), ALU.add)
         if t == R - 1:
             aff(vs, A("o8"), A("io1", 0, 48), 8.0, 0.0)
             tt(A("olb"), A("prow", 0, 48), A("o8"), ALU.add)
             for gr in range(8):
                 dma("y", T.ol[gr:gr + 1, :], A("olb", 0, 48, 1, 16 * gr, 16 * gr + 1), "dol")
-        for k in [r] + others:
-            aff(vs, A("inr", 64 * k, 64 * k + 64), A("kt", 64 * k, 64 * k + 64),
-                col("msg", 0) if k == r else col(cl, 4 * k), 0.0)
-        tr(A("row", 0, 128), A("inr", 0, 256, 2))
-        tr(A("row", 128, 256, 1, 64, 128), A("inr", 1, 256, 2, 0, 64))
-        tr(A("row", 128, 256, 1, 0, 64), A("inr", 1, 256, 2, 64, 128))
-        cp(vs, A("cg"), A("row", ind=A("lc")))
-        tr(A("ct"), A("cg"))
-        key = col("ct", 31 if mir else 0)
-        ts(A("cmp", 0, 128), A("row", 0, 128), key, ALU.is_lt)
-        red(col("cnt", 0), A("cmp", 0, 128), ALU.add)
-        act(A("cmp", 128, 256), A("row", 128, 256), ACT.Sign, bias=key, scale=-1.0)
-        act(A("cmp", 128, 256), A("cmp", 128, 256), ACT.Relu, accum=col("cnt", 2))
-        ts(A("fl32"), A("c96"), col("cnt", 0), ALU.subtract, col("cnt", 2), ALU.is_gt)
+        for i, k in enumerate(others + [r]):
+            aff(vs, A("inr", 64 * i, 64 * i + 64), A("kt", 64 * i, 64 * i + 64), cost[k], 0.0)
+        tt(A("key", 0, 4), A(cl, 31, 128, 32), A("km"), ALU.add)
+        red(col("key", 4), A("key", 0, 4), ALU.min)
+        for o, w in ((96, 32), (0, 96)):
+            tr(A("row", o, o + w), A("inr", 2 * o, 2 * (o + w), 2))
+            tr(A("row", 128 + o, 128 + o + w, 1, 64, 128), A("inr", 2 * o + 1, 2 * (o + w), 2, 0, 64))
+            tr(A("row", 128 + o, 128 + o + w, 1, 0, 64), A("inr", 2 * o + 1, 2 * (o + w), 2, 64, 128))
+        ts(A("cmp", 0, 256), A("row"), col("key", 4), ALU.is_lt)
+        scan(A("cnt"), A("cmp"), A("zer", 0, 288), 0.0, ALU.add, ALU.add)
         for a in range(4):
-            tr(A("fone", 32 * a, 32 * a + 32, 1, 0, 32), A("fl32", 0, 32, 1, 32 * a, 32 * a + 32))
+            o = 32 * blk[a] - kb
+            tr(A("fone", o, o + 32, 1, 0, 32), A("cnt", 256, 288, 1, 32 * a, 32 * a + 32))
+        o = S * r - kb
         for a in range(4):
-            aff("v", A("frow", 0, 128, 1, 32 * a, 32 * a + 32), A("fone", 0, 128, 1, 0, 32), 0.25, 0.0)
-        choose("oa", 24, A("lfo", 0, 3))
-        cp("v", A("lz"), A("oa", 144, 168))
-        for b in range(4):
-            if b < 2:
-                zgather(b, uL, S, "fb", PW, A("lz"))
-            else:
-                for h in range(2):
-                    zgather(b, uL + 24 * h, 24, "fb", PW, A("lz", 12 * h, 12 * h + 12))
-        sides = ([(0, kc("xl"))] if nL else []) + ([(4, kc("xr"))] if nR else [])
-        for i, (c_, xb) in enumerate(sides):
-            ts(col("lve", i), col(pl, c_), xb, ALU.add)
-        for b in range(4):
-            cp(vs, A("ve", b, 64 * ne, 4), A("fe", XW * b, XW * b + 8 * nx, ind=A("lve", 0, ne)))
-        quant("veq", 0, 128, "ve", 0)
-        for b in range(4):
-            mm(b, "wq", 128 * b, "veq", 0, 128)
-        v0 = 16 - nL if nL else 0
-        for b in range(4):
-            relu("s", A("fe", XW * b + HX, XW * b + HX + 8 * nx, 8), ps(b, v0, v0 + nx), 0.03125)
-        for i, (c_, xb) in enumerate(sides):
-            aff(vs, A("pin", 32 * i, 32 * i + 32), A("z32"), 1.0, col(pl, c_))
-        tr(A("pt", 0, 32 * ne), A("pin", 0, 32 * ne))
-        o_ = [A("ox", 16 * i, 16 * i + 16) for i in range(13)]
-        cp(vs, A("ox", 0, 32), A("frow", ind=A("lfx")))
-        aff(vs, o_[2], o_[0], kc("ev8"), kc("ev"))
-        aff(vs, o_[3], o_[1], kc("od8"), QH)
-        aff(vs, o_[4], o_[0], kc("wev4"), kc("wev"))
-        aff(vs, o_[5], o_[1], kc("wod4"), kc("wod"))
-        aff(vs, o_[7], o_[0], kc("ev4"), 0.0)
-        aff(vs, o_[8], o_[1], kc("od4"), 0.0)
-        tt(o_[7], o_[7], A("bext"), ALU.add)
-        tt(A("ox", 212, 288, 5), o_[7], o_[8], ALU.add)
-        ts(A("ox", 144, 176), A("pt", 0, 32 * ne, ind=A("lp")), Q7, ALU.is_gt)
-        ts(A("ox", 176, 208), A("pt", 0, 32 * ne, ind=A("lp")), Q7, ALU.is_equal)
-        for i in range(4):
-            tt(A("ox", 208 + i, 288, 5), o_[9 + i], o_[2 + i], ALU.mult)
-        scan(A("ox", 288, 368), A("c5"), A("ox", 208, 288), 0.0, ALU.mult, ALU.add)
-        if uL:
-            cp("v", A("lzx", 0, uL // 2), A("ox", 292 + 5 * ((nL - uL) // 2), 288 + 5 * (nL // 2), 5))
-        if uR:
-            cp("v", A("lzx", 8, 8 + uR // 2), A("ox", 292 + 5 * (nL // 2), 288 + 5 * ((nL + uR) // 2), 5))
-        for b in range(4):
-            if uL:
-                zgather(b, 0, uL, "fe", XW, A("lzx", 0, uL // 2))
-            if uR:
-                zgather(b, uL + S, uR, "fe", XW, A("lzx", 8, 8 + uR // 2))
-        scan(A("pos", 1, 1 + n0 + n), A("c98", 0, n0 + n), A("frow", 0, n0 + n), init, ALU.add, ALU.subtract)
-        aff(vs, A("t7", 0, n), A("frow", n0, n0 + n), kc("ta"), kc("tb"))
-        tt(A("th", 0, n), A("pos", n0, n0 + n), A("t7", 0, n), ALU.add)
-        aff(vs, col("cnt", 1), col("pos", n0), 8.0, 0.0)
-        for m_ in range(3):
-            ts(A("cl", 68 * m_, 68 * m_ + n), A("th", 0, n), col("lo", m_), ALU.max, col("lo", 4 + m_), ALU.min)
-            red(col("sums", m_), A("cl", 68 * m_, 68 * m_ + n), ALU.add)
-        cp(vs, A("sums", 3, 6, 1, 0, 64), A("sums", 0, 3, 1, 64, 128))
-        cp(vs, A("sums", 3, 6, 1, 64, 128), A("sums", 0, 3, 1, 0, 64))
-        tt(A("xr"), A("sums", ind=A("ls")), A("dk"), ALU.subtract)
-        c1, c4, da, db = [A("rr", 24 * i, 24 * i + 24) for i in range(4)]
-        ts(A("rr", 48, 96), A("xr", 48, 96), 8.0 / 9, ALU.mult, MAGIC, ALU.add)
-        ts(c4, A("xr", 24, 48), MAGIC, ALU.add, -2 * MAGIC, ALU.add)
-        ts(c1, A("xr", 0, 24), MAGIC, ALU.add, col("cnt", 1), ALU.add)
-        x0, x1, x2, x3, x4 = [A("mm5", 24 * i, 24 * i + 24) for i in range(5)]
-        tt(x0, da, db, ALU.subtract)
-        tt(x1, c4, da, ALU.add)
-        if mir:
-            tt(x2, c1, da, ALU.subtract)
+            ts(A("lb", 0, 96, 2, 32 * a, 32 * a + 32), A("fone", o, o + S, 1, 0, 32), 96.0, ALU.is_ge, 48.0, ALU.mult)
+        for a in range(4):
+            ts(A("fd", 0, 128, 1, 32 * a, 32 * a + 32), A("fone", 0, 128, 1, 0, 32), 96.0, ALU.is_ge, 0.25, ALU.mult)
+        scan(A("lo_"), A("la"), A("lb"), 0.0, ALU.mult, ALU.add)
+        cp("v", A("lz"), odd("lo_", 0, S))
+        for c_ in ((2, 1, 0) if r == 0 else (0, 2, 1) if r < N - 1 else (0, 1, 2)):
+            for b in range(2):
+                cp(vs, A("zt", 512 * c_ + b, 512 * c_ + 512, 2),
+                   A("fb", PW * b, PW * (b + 3), ind=A("lz", 16 * c_, 16 * c_ + 16)))
+            quant(zq, Z0 + 128 * c_, Z0 + 128 * c_ + 128, "zt", 512 * c_)
+        for nm, cast, rs, ls_ in (("", u8, "ac", "sc"), ("s", None, "as", "ss")):
+            m1, l1 = borders((zq + nm, zq + nm), [64, 96, 96, 64], Z0, Z0 + C, Z0 + C, Z0, cast)
+            remote(m1, "%s%d" % (rs, t), "%s%d" % (ls_, t), l1, sum(share(k) for k in nbs), HOP + 400)
+        e_ = 128 if upper else i0 + n
+        scan(A("pos", 1, 1 + e_), A("c78", 0, e_), A("fd", 0, e_), 0.0, ALU.add, ALU.add)
+        aff(vs, A("t7", 0, n), A("fd", i0, i0 + n), kc("ta"), kc("tb"))
+        tt(A("th", 0, n), A("pos", i0, i0 + n), A("t7", 0, n), ALU.add)
+        lo_ = "lo"
+        if upper:
+            lo_ = "lu"
+            aff(vs, kc("pe"), col("pos", 128), kc("-sc"), 0.0)
+            aff(vs, A("lu"), A("lo"), 1.0, kc("pe"))
+            ts(kc("p8"), col("pos", i0), col("pos", 128), ALU.subtract, -8.0, ALU.mult)
         else:
-            tt(x2, da, c1, ALU.subtract)
-        tt(x3, x0, x1, ALU.mult)
-        tt(x4, x3, x2, ALU.max)
-        cp("v", A("lm"), x4)
-        quant("zq", 128, 8 * n - 128, "zt", 512)
-        quant("zq", 0, 128, "zt", 0)
-        quant("zq", 8 * n - 128, 8 * n, "zt", 32 * n - 512)
+            aff(vs, kc("p8"), col("pos", i0), -8.0, 0.0)
+        aff(vs, A("dk", 0, 24), A("dk", 96, 120), 1.0, kc("p8"))
+        ts(A("dk", 24, 48), A("dk", 120, 144), kc("p8"), ALU.subtract)
+        for m_ in range(6):
+            act(A("cl", 68 * m_, 68 * m_ + n), A("th", 0, n), ACT.Relu, col(lo_, m_), kc("sc"), col("rs", m_))
+        tt(A("sums", 0, 3), A("rs", 0, 3), A("rs", 3, 6), ALU.subtract)
+        for a, b in ((0, 64), (64, 0)):
+            tt(A("sums", 3, 6, 1, a, a + 64), A("rs", 0, 3, 1, b, b + 64), A("rs", 3, 6, 1, b, b + 64), ALU.subtract)
+        tt(A("xr"), A("sums", ind=A("ls")), A("dk", 0, 96), ALU.subtract)
+        c1, c4, da, db = [A("xr", 24 * i, 24 * i + 24) for i in range(4)]
+        tt(A("mm5", 0, 48, 2), da, db, ALU.subtract)
+        tt(A("mm5", 49, 96, 2), c4, da, ALU.add)
+        tt(A("mm5", 1, 48, 2), da, c1, ALU.subtract)
+        scan(A("mm5", 96, 144), A("mm5", 48, 96), A("mm5", 0, 48), 0.0, ALU.mult, ALU.add)
+        cp("v", A("lm"), A("mm5", 97, 144, 2))
         for h in (1, 0):
-            pick("gq", 192 * h, 192, "zq", ZC, A("lm", 12 * h, 12 * h + 12))
+            pick("gq", 192 * h, 192, zq, ZC, A("lm", 12 * h, 12 * h + 12))
         for h in (1, 0):
             for b in range(4):
-                i = mm(b, "wq", 128 * b, "gq", 192 * h, 192, [i] if 1 - h + b else [])
-                i = mm(4 + b, "eq", 128 * b, "gq", 192 * h, 192, [i])
+                i = mm(7 - 2 * b, "wq", 128 * b, "gq", 192 * h, 192, [i] if 1 - h + b else [])
+                i = mm(6 - 2 * b, "eq", 128 * b, "gq", 192 * h, 192, [i])
             for b in range(4):
                 o = 384 * b + 192 * h
-                relu("s", A("tmp", o, o + 192), ps(b, 0, 192), 0.015625)
-                tt(A("xt", 768 * h + b, 768 * h + 768, 4), ps(4 + b, 0, 192), A("tmp", o, o + 192), ALU.add)
-            quant("tq", 192 * h, 192 * h + 192, "xt", 768 * h)
+                relu("s", A("tmp", o, o + 192), ps(7 - 2 * b, 0, 192), 0.015625)
+                tt(A("xt", 768 * h + b, 768 * h + 768, 4), ps(6 - 2 * b, 0, 192), A("tmp", o, o + 192), ALU.add)
+            quant("tq", T0 + 192 * h, T0 + 192 * h + 192, "xt", 768 * h)
 
-    pick("tf", 0, 384, "tq", 384, A("lf"))
+    pick("tf", 0, 384, "tq", 400, A("lf"))
     for h in range(2):
         mm(h, "vq", 0, "tf", 192 * h, 192)
         cp("vs"[h], A("ysb", 192 * h, 192 * h + 192), ps(h, 0, 192))
@@ -678,7 +682,7 @@ def rank_program(g, core, T, topo):
     dma("y", T.y[:, :], A("ysb"), "dy")
 
     count, known, mark = {}, {q: {} for q in eng}, {}
-    for i, q in schedule(ops)[0]:
+    for i, q in plan(ops):
         o = ops[i]
         sem = o["sem"] or COUNTER[q]
         count[sem] = count.get(sem, 0) + o["inc"]

@@ -13,6 +13,7 @@ T0 = 16
 Z0 = 96
 B0 = 576
 ZC = B0 + 3 * S
+PARTS = ((128, 256), (0, 128))
 F32, BF, I32, U16, CODE, PLANE = "float32", "bfloat16", "int32", "uint16", "float8_e4m3fn_x4", "uint8"
 WIDTH = {F32: 4, BF: 2, I32: 4, U16: 2, CODE: 4, PLANE: 1}
 
@@ -24,7 +25,7 @@ def _buf(dtype, **kw):
         SCRATCH[k] = ("sbuf", [128, n], dtype)
 
 
-_buf(BF, xin=1536, uin=512, vin=512, xt=1536, fb=4 * PW, zt=1536, ft=512, vt=512, st=512, eb=2048, mv=512, zer=512,
+_buf(BF, xin=1536, uin=512, vin=512, xt=1536, fb=4 * PW, zt=1536, ft=512, vt=512, st=512, eb=516, mv=512, zer=512,
      cmp=288, cnt=288, fone=128, fd=128)
 _buf(CODE, tn=384, tq=528, tf=384, uq=128, vq=128, wq=512, eq=512, mq=128, sq=128, vcq=128, fq=128, gq=384,
      zq0=ZC, zq1=ZC, zq2=ZC)
@@ -32,20 +33,23 @@ _buf(PLANE, tns=384, tqs=528, tfs=384, uqs=128, vqs=128, wqs=512, eqs=512, mqs=1
      gqs=384, zq0s=ZC, zq1s=ZC, zq2s=ZC)
 _buf(F32, kc=64, te=120, mo=1048, mz=160, tc=24, ee=96, we=128, ww=128, wm=128, nb=120, t3=360, u3=360, tau=360,
      tau2=360, dd=120, c3=144, c8=64, flo=24, wb=24, mc=8, acc=8, dump=64,
-     sp=64, prow=52, oa=144, la=96, lb=96, lo_=96, basec=48, bown=24, kt=256, kw=128, km=4, key=8, inr=256, row=256,
+     sp=64, prow=52, oa=96, la=144, lb=144, lo_=144, kt=256, kw=128, km=4, key=8, inr=256, row=256,
      c78=128, pos=132, t7=68, th=68, cl=408, rs=6, sums=8, lo=6, lu=6, dk=144, mm5=144, tmp=1536, ysb=384,
      olb=48, o8=48, io1=128, w0=24, w3=8, w4=8, w5=8, thp=4, cl0=128, cl1=128, cl2=128)
 _buf(I32, pi=8, xr=96)
-_buf(U16, l0=24, lf=24, lv=4, lz=48, ls=6, lm=24, l48=4, lw=44)
+_buf(U16, l0=24, lf=8, lv=4, lz=48, ls=6, lm=24, l48=10, lw=20)
+_buf(CODE, tl=384, bq=192)
+_buf(PLANE, tls=384, bqs=192)
 
 SEMAPHORES = ["cv", "cs", "cp", "cg", "dx", "dx2", "du", "dv", "dw", "dws", "dol", "dy", "doc", "dos"] + [
     "%s%d" % (k, t) for t in range(R) for k in ("ac", "as", "ak", "af", "ag", "sc", "ss", "sk", "sf", "sg")]
 COUNTER = {"v": "cv", "s": "cs", "p": "cp", "g": "cg"}
-CY, GAT, WAKE, PE, HOP, DMA = 0.95, 1.4, 200.0, 0.6, 1900.0, 2000.0
+CY, GAT, WAKE, PE, HOP, DMA = 0.95, 1.4, 195.0, 0.6, 1200.0, 1200.0
 FINE = ("oa", "tq", "mo", "mz", "te", "cn", "cq", "tc", "gq", "gqs", "xt", "tmp", "ca", "cb", "tau",
         "th", "rr", "mm5", "cl", "fb", "zt")
-SPARE, TRIES, SHAKE, SPAN = 60.0, 400, 300.0, 3000.0
-VARIANTS = ((200.0, 1.0, 1.0, 1.0), (150.0, 0.9, 0.8, 0.7), (260.0, 1.15, 1.2, 1.25))
+FIRST = 800.0
+SPARE, TRIES, SHAKE, SPAN = 150.0, 1200, 300.0, 3000.0
+VARIANTS = ((195.0, 1.0, 1.0, 1.0), (130.0, 1.15, 0.8, 0.9), (230.0, 1.2, 1.2, 1.5))
 
 
 def A(name, c0=0, c1=None, step=1, p0=0, p1=128, ind=None, cast=None):
@@ -127,14 +131,20 @@ def plan(ops):
         way[i] = min(ops[i]["cost"].values()) + max(
             [way[j] + (0.0 if soft else ops[i]["lat"] + WAKE) for j, soft in after[i]] + [ops[i]["lat"]])
 
-    def place(prio):
-        left = [len(p) for p in pre]
+    gap = [[(j, 0.0 if soft else ops[j]["lat"] + WAKE) for j, soft in pre[i]] for i in range(n)]
+    pag = [[(j, 0.0 if soft else ops[i]["lat"] + WAKE) for j, soft in after[i]] + [(n, ops[i]["lat"])] for i in range(n)]
+
+    def place(prio, back=False):
+        left = [len(p) for p in (after if back else pre)]
         ready = [i for i in range(n) if not left[i]]
-        busy, start, end, where = {}, [0.0] * n, [0.0] * n, [None] * n
+        busy, start, end, where = {}, [0.0] * n, [0.0] * (n + 1), [None] * n
         while ready:
             i = max(ready, key=lambda k: prio[k])
             ready.remove(i)
-            at = max([end[j] + (0.0 if soft else ops[j]["lat"] + WAKE) for j, soft in pre[i]] + [0.0])
+            at = 0.0
+            for j, d in (pag if back else gap)[i]:
+                if end[j] + d > at:
+                    at = end[j] + d
             best = None
             for q, c_ in ops[i]["cost"].items():
                 b, t, k = busy.setdefault(q, []), at, 0
@@ -155,39 +165,58 @@ def plan(ops):
             x, t, q, k, c_ = best
             busy[q].insert(k, (t, t + c_))
             start[i], end[i], where[i] = t, t + c_, q
-            for j, soft in after[i]:
+            for j, soft in (pre if back else after)[i]:
                 left[j] -= 1
                 if not left[j]:
                     ready.append(j)
-        return sorted(range(n), key=lambda k: (start[k], k)), where, start
+        return end[:n] if back else (sorted(range(n), key=lambda k: (start[k], k)), where, start)
 
     def length(order, where):
-        tot = 0.0
+        tot, held = 0.0, []
         for wake, fc, fp, fl in VARIANTS:
-            free, end, done = {}, [0.0] * n, [0.0] * n
+            free, last, end, done, by = {}, {}, [0.0] * n, [0.0] * n, [None] * n
             for i in order:
-                q, t = where[i], free.get(where[i], 0.0)
+                q = where[i]
+                t, k = free.get(q, 0.0), (last.get(q), True)
                 for j, soft in pre[i]:
                     x = end[j] if soft else done[j] + wake
-                    if x > t:
-                        t = x
+                    if x >= t:
+                        t, k = x, (j, False)
                 end[i] = free[q] = t + ops[i]["cost"][q] * (fp if q == "p" else fc)
-                done[i] = end[i] + ops[i]["lat"] * fl
-            tot += max(done)
-        return tot
+                done[i], last[q], by[i] = end[i] + ops[i]["lat"] * fl, i, k
+            i = max(range(n), key=lambda k: done[k])
+            tot += done[i]
+            while i is not None:
+                if by[i][1] and by[i][0] is not None:
+                    held.append((i, by[i][0]))
+                i = by[i][0]
+        return tot, held
 
     rng = np.random.default_rng(0)
     prio = list(way)
     order, where, start = place(prio)
-    best = length(order, where)
+    best, held = length(order, where)
     for it in range(TRIES):
-        at = rng.random() * max(start)
-        z = rng.normal(0.0, SHAKE, n)
-        trial = [prio[i] + (float(z[i]) if abs(start[i] - at) < SPAN else 0.0) for i in range(n)]
+        trial = list(prio)
+        if it % 50 < 2:
+            trial = place(start, True)
+        elif it % 4 == 0 or not held:
+            at, z = rng.random() * max(start), rng.normal(0.0, SHAKE, n)
+            for i in range(n):
+                if abs(start[i] - at) < SPAN:
+                    trial[i] += float(z[i])
+        else:
+            i, j = held[int(rng.integers(len(held)))]
+            d = max(prio[j] - prio[i], 0.0) + rng.random() * 2 * SHAKE
+            if it % 2:
+                trial[j] -= d
+            else:
+                for k in [i] + [k for k, soft in pre[i]]:
+                    trial[k] += d
         o2, w2, s2 = place(trial)
-        x = length(o2, w2)
+        x, h2 = length(o2, w2)
         if x <= best:
-            best, prio, order, where, start = x, trial, o2, w2, s2
+            best, held, prio, order, where, start = x, h2, trial, o2, w2, s2
     return [(i, where[i]) for i in order]
 
 
@@ -352,10 +381,10 @@ def rank_program(g, core, T, topo):
             K[name_] = len(K)
         return col("kc", K[name_])
 
-    dma("y", A("xin", 0, 768), T.x[:, 0:768], "dx", 2600.0)
-    dma("s", A("xin", 768, 1536), T.x[:, 768:1536], "dx2", 2800.0)
-    dma("s", A("uin"), T.u[:, :], "du")
-    dma("y", A("wq", cast=u8), T.wc[:, :], "dw", 3000.0, [A("xin")])
+    dma("y", A("xin", 0, 768), T.x[:, 0:768], "dx", DMA + 800.0)
+    dma("s", A("xin", 768, 1536), T.x[:, 768:1536], "dx2", DMA + 1000.0)
+    dma("s", A("uin"), T.u[:, :], "du", DMA + 1000.0)
+    dma("y", A("wq", cast=u8), T.wc[:, :], "dw", DMA + 1200.0, [A("xin")])
     dma("y", A("wqs"), T.ws[:, :], "dws", DMA, [A("xin")])
     dma("y", A("vin"), T.v[:, :], "dv", DMA, [A("wq")])
     iota(col("pi", 0), [[0, 1]], 0, 1)
@@ -393,24 +422,23 @@ def rank_program(g, core, T, topo):
     quant("tn", 192, 384, "xin", 768)
     pick("tq", T0, 384, "tn", 384, A("l0"))
     quant("vq", 0, 128, "vin", 0)
+    fill(A("eb"), 0.0)
+    ts(A("eb", 3, 512, 4), A("io1"), P, ALU.is_equal)
     for b in range(4):
-        cp(vs, A("eb", 512 * b, 512 * b + 512), A("zer"))
-        ts(A("eb", 512 * b + b, 512 * b + 512, 4), A("io1"), P, ALU.is_equal)
-        quant("eq", 128 * b, 128 * b + 128, "eb", 512 * b)
-    aff(vs, kc("fin"), Q7, 48.0, QH)
-    aff(vs, A("bown"), A("io1", 0, 48, 2), 1.0, kc("fin"))
-    ts(A("lf"), A("bown"), float(T0), ALU.add)
+        quant("eq", 128 * b, 128 * b + 128, "eb", 3 - b)
+    aff(vs, kc("fin"), Q7, 16.0, QH)
+    ts(A("lf"), A("io1", 0, 16, 2), kc("fin"), ALU.add)
     aff(vs, A("t3", 330, 360, 3), A("t3", 330, 360, 3), 1.0, 3.5)
     fill(A("sp"), 0.0)
-    cp(vs, A("mv"), A("zer"))
+    fill(A("mv"), 0.0)
     fill(A("sp", 0, 64, 4), 1.0)
     ts(A("sp", 1, 64, 4), A("io1", 0, 16), Q, ALU.is_equal)
     ts(A("mv", 0, 192, 4), A("io1", sh, sh + 48), P, ALU.is_equal)
     ts(A("mv", 193, 204, 4), A("io1", sh // 16, sh // 16 + 3), G, ALU.is_equal)
     quant("mq", 0, 128, "mv", 0)
     ts(kc("g7"), G, 7.0, ALU.is_equal)
-    cp(vs, A("vt"), A("zer"))
-    cp(vs, A("ft"), A("zer"))
+    fill(A("vt", 4 * S, 512), 0.0)
+    fill(A("ft", 4 * S, 512), 0.0)
     aff(vs, kc("al"), kc("g7"), -0.5, -0.5)
     aff(vs, kc("be"), kc("g7"), -3.5, 3.5)
     aff(vs, kc("al48"), kc("al"), 48.0, 0.0)
@@ -418,12 +446,14 @@ def rank_program(g, core, T, topo):
     aff(vs, A("w3", 0, 6), A("io1", 0, 96, 16), 1.0, Q)
     aff(vs, A("w5", 0, 3), A("io1", 0, 48, 16), 1.0, kc("be48"))
     cp("v", A("l48", 0, 3), A("w3", 0, 3))
+    ts(A("l48", 6, 9), A("w3", 0, 3), float(S), ALU.add)
     aff(vs, kc("ns"), SLOT, -1.0, -0.5)
     aff(vs, kc("w2"), SLOT, -1.0, 8.0)
-    aff(vs, kc("sb"), SLOT, 48.0, 0.0)
+    aff(vs, kc("sb"), SLOT, 48.0, 24.0)
     aff(vs, kc("sb"), ODD, 2.0 * PW, kc("sb"))
-    aff(vs, A("basec"), A("io1", 0, 48), 1.0, kc("sb"))
-    fill(A("la"), 0.0)
+    cp(vs, A("lb", 2, 144, 3), A("io1", 0, 48))
+    fill(A("la", 0, 144, 3), 0.0)
+    fill(A("la", 2, 144, 3), 1.0)
     ts(kc("mid"), P, 63.5, ALU.subtract)
     act(kc("mid"), kc("mid"), ACT.Abs)
     ts(kc("mid"), kc("mid"), 32.0, ALU.is_lt)
@@ -432,11 +462,12 @@ def rank_program(g, core, T, topo):
     for i, k in enumerate(others + [r]):
         h, a_ = (("h+", 0), ("h-", 16), ("h-", 32), ("h+", -16))[k]
         ts(A("kw", 32 * i, 32 * i + 32), A("io1", 0, 32), kc(h), ALU.subtract, float(S * k + a_), ALU.subtract)
-        ts(col("km", k), col("kw", 32 * i), LANE, ALU.add, col("thp", 0), ALU.not_equal)
+        ts(col("km", k), col("kw", 32 * i), LANE, ALU.add, col("thp", 0), ALU.is_equal)
+        ts(col("km", k), col("kw", 32 * i), -S * (k + 1.0 - k % 2), ALU.is_le if k % 2 else ALU.is_gt, col("km", k),
+           ALU.mult)
     for d in range(2):
         ts(A("kt", d, 256, 2), A("kw"), col("thp", d), ALU.is_gt, -2.0 ** -24, ALU.mult)
     aff(vs, A("kt"), A("kt"), 1.0, 1.0)
-    aff(vs, A("km"), A("km"), BIG, 0.0)
     for i in (2, 4, 6):
         ts(kc("g%d" % i), Q7, float(i), ALU.is_ge)
     ts(kc("c0"), kc("g4"), kc("g6"), ALU.add, QH, ALU.add)
@@ -464,8 +495,8 @@ def rank_program(g, core, T, topo):
     aff(vs, kc("sc"), kc("up"), -1.0 / 9, 1.0)
     aff(vs, kc("-sc"), kc("sc"), -1.0, 0.0)
     aff(vs, kc("lo"), kc("up"), -0.125, float(S * r - far // 8))
-    ts(A("lo", 0, 3), A("w3", 0, 3), kc("lo"), ALU.add, kc("-sc"), ALU.mult)
-    ts(A("lo", 3, 6), A("w3", 0, 3), float(S * r - far // 8 + 1), ALU.add, kc("-sc"), ALU.mult)
+    ts(A("lo", 0, 3), A("w3", 0, 3), kc("lo"), ALU.add, 1.0 if upper else kc("-sc"), ALU.mult)
+    ts(A("lo", 3, 6), A("w3", 0, 3), float(S * r - far // 8 + 1), ALU.add, 1.0 if upper else kc("-sc"), ALU.mult)
     kj, kf = C * r - 8 * (S * r - Z0 // 8) + 8 * w0 - far, B0 + S - S * r + w0 + 2 * n - 1
     aff(vs, A("dk", 0, 24), A("w0"), 1.0, kc("q8"))
     aff(vs, A("dk", 48, 72), A("dk", 24, 48), 1.0 / 9, -3.0 / 9)
@@ -505,11 +536,10 @@ def rank_program(g, core, T, topo):
         cp("s", A("we", o, o + 128), e_)
         tt(A("ww", o, o + 128), c_, A("we", o, o + 128), ALU.max)
 
-    def twice(o, do, wo, k, lst):
-        tt(A("wm", wo, wo + 64 * k), A("mo", 8 * o, 8 * o + 80 * k, ind=lst), A("ww", wo, wo + 64 * k), ALU.max)
-        for i in range(k):
-            scan(A("mo", 8 * (do + 10 * i) + 8, 8 * (do + 10 * i) + 72), A("c8"),
-                 A("wm", wo + 64 * i, wo + 64 * i + 64), 0.0, ALU.max, ALU.min)
+    def twice(o, do, wo, running=False):
+        tt(A("wm", wo, wo + 64), A("mo", 8 * o, 8 * o + 80, ind=A("lw", 16, 20)), A("ww", wo, wo + 64), ALU.max)
+        scan(A("mo", 8 * do + 8, 8 * do + 72), A("zer", 0, 64) if running else A("c8"), A("wm", wo, wo + 64), BIG,
+             ALU.max, ALU.min)
 
     def back(o, w):
         tt(A("nb", o - 2, o + w), mo(o - 2, w + 2), mo(o - 1, w + 2), ALU.min)
@@ -535,6 +565,19 @@ def rank_program(g, core, T, topo):
                 lands.append(A(buf[1], to_left, to_left + w[k]))
         return mv_, lands
 
+    def firsts(t, src, o):
+        zq = "zq%d" % t
+        pick(zq, B0 + S, S, src, 128, A("l48", 6, 9) if o else A("l48", 0, 3))
+        for nm, cast, rs, ls_ in (("", u8, "af", "sf"), ("s", None, "ag", "sg")):
+            m1, l1 = borders((src + nm, zq + nm), [8, 12, 12, 8], o, o + S, B0 + 2 * S, B0 + S, cast)
+            remote(m1, "%s%d" % (rs, t), "%s%d" % (ls_, t), l1, sum(share(k) for k in nbs), HOP + (0 if t else FIRST))
+
+    for b in range(4):
+        mm(b, "eq", 128 * b, "tn", 0, 384)
+        cp(vs, A("ft", b, 4 * S, 4), ps(b, 0, 384, 8))
+    quant("fq", 0, 128, "ft", 0)
+    firsts(0, "fq", 0)
+
     for t in range(R):
         zq, cl = "zq%d" % t, "cl%d" % t
         for l in range(L - 1, -1, -1):
@@ -559,25 +602,17 @@ def rank_program(g, core, T, topo):
         cost = [col(cl, 32 * k + 31) for k in range(N)]
         remote([(cost[r], cost[r], others)], "ak%d" % t, "sk%d" % t, [cost[k] for k in others],
                sum(len(topo.engines(T.cores[k], core)) for k in others), HOP + 300)
-        for b in range(4):
-            cp(vs, A("ft", b, 4 * S, 4), A("fb", PW * b, PW * b + S))
-        quant("fq", 0, 128, "ft", 0)
-        pick(zq, B0 + S, S, "fq", 128, A("l48", 0, 3))
-        for nm, cast, rs, ls_ in (("", u8, "af", "sf"), ("s", None, "ag", "sg")):
-            m1, l1 = borders(("fq" + nm, zq + nm), [8, 12, 12, 8], 0, S, B0 + 2 * S, B0 + S, cast)
-            remote(m1, "%s%d" % (rs, t), "%s%d" % (ls_, t), l1, sum(share(k) for k in nbs))
         tt(A("ee", 64, 89), A("ee", 32, 57), A("ee", 33, 58), ALU.min)
         weights(0, A("ee", 32, 96, ind=A("lw", 0, 8)), A("ee", 0, 32, ind=A("lw", 8, 16)))
-        twice(60, 100, 0, 1, A("lw", 16, 20))
-        twice(100, 120, 64, 1, A("lw", 16, 20))
+        twice(60, 100, 0)
+        twice(100, 120, 64, True)
         level(60, 60, 50, 80, 8)
         level(100, 70, 10, 110, 8)
-        scan(A("mc", 0, 8), mo(121, 8), mo(121, 8), BIG, ALU.min, ALU.min)
         for o, w in ((2, 28), (42, 28), (82, 28), (112, 7)):
             back(o, w)
         for o, w in ((22, 47), (102, 7)):
             back2(o, w)
-        act(A("dump", 56, 64), A("mc", 0, 8), ACT.Sign, bias=col("mc", 7), scale=-1.0, accum=col("acc", 7))
+        act(A("dump", 56, 64), mo(121, 8), ACT.Sign, bias=mo(128, 1), scale=-1.0, accum=col("acc", 7))
         for gr, to in ((7, 6), (6, 4), (6, 5), (4, 2), (4, 3), (2, 0), (2, 1)):
             o = [2, 22, 42, 62, 82, 102, 112][gr - 1]
             act(A("dump", 8 * to, 8 * to + 7), third("tau2" if gr - to == 2 else "tau", 2, o, 7), ACT.Sign,
@@ -588,19 +623,22 @@ def rank_program(g, core, T, topo):
         mm(4, "sq", 0, "mq", 0, 128)
         for m_ in range(3):
             aff("v", col("lv", m_), ps(4, 48 + m_, 49 + m_), kc("al48"), col("w5", m_))
-        aff("v", A("prow", 0, S), ps(4, 0, S), kc("al"), kc("be"))
+        aff(vs, A("prow", 0, S), ps(4, 0, S), kc("al"), kc("be"))
         for b in range(4):
             cp(vs, A("vt", b, 192, 4), A("fb", PW * b, PW * b + 384, ind=A("lv", 0, 3)))
+            if t:
+                cp(vs, A("vt", 4 * S + b, 8 * S, 4), A("fb", PW * b, PW * b + S))
         quant("vcq", 0, 128, "vt", 0)
+        if t:
+            firsts(t, "vcq", S)
         for b in range(4):
             mm(4 + (b + 1) % 4, "wq", 128 * b, "vcq", 0, 128)
         for b in range(4):
             relu(vs, A("fb", PW * b + 384, PW * b + 432), ps(4 + (b + 1) % 4, 0, 48), 0.03125)
         act(A("oa", 0, 48), A("prow", 0, S), ACT.Sign, bias=kc("ns"))
         ts(A("oa", 48, 96), A("prow", 0, S), SLOT, ALU.is_equal, kc("w2"), ALU.mult)
-        ts(A("oa", 96, 144), A("prow", 0, S), SLOT, ALU.is_le, 48.0, ALU.mult)
-        tt(odd("la", 0, S), A("oa", 0, 48), A("oa", 48, 96), ALU.add)
-        tt(odd("lb", 0, S), A("oa", 96, 144), A("basec"), ALU.add)
+        tt(third("la", 1, 0, S), A("oa", 0, 48), A("oa", 48, 96), ALU.add)
+        aff(vs, third("lb", 1, 0, S), A("oa", 0, 48), -24.0, kc("sb"))
         if t == R - 1:
             aff(vs, A("o8"), A("io1", 0, 48), 8.0, 0.0)
             tt(A("olb"), A("prow", 0, 48), A("o8"), ALU.add)
@@ -608,8 +646,9 @@ def rank_program(g, core, T, topo):
                 dma("y", T.ol[gr:gr + 1, :], A("olb", 0, 48, 1, 16 * gr, 16 * gr + 1), "dol")
         for i, k in enumerate(others + [r]):
             aff(vs, A("inr", 64 * i, 64 * i + 64), A("kt", 64 * i, 64 * i + 64), cost[k], 0.0)
-        tt(A("key", 0, 4), A(cl, 31, 128, 32), A("km"), ALU.add)
-        red(col("key", 4), A("key", 0, 4), ALU.min)
+        keys = [r] + [k for k in others if (k > 0 if upper else k < N - 1)]
+        for i, k in enumerate(keys):
+            aff(vs, col("key", i + 2), cost[k], col("km", k), col("key", i + 1) if i else 0.0)
         for o, w in ((96, 32), (0, 96)):
             tr(A("row", o, o + w), A("inr", 2 * o, 2 * (o + w), 2))
             tr(A("row", 128 + o, 128 + o + w, 1, 64, 128), A("inr", 2 * o + 1, 2 * (o + w), 2, 0, 64))
@@ -621,18 +660,26 @@ def rank_program(g, core, T, topo):
             tr(A("fone", o, o + 32, 1, 0, 32), A("cnt", 256, 288, 1, 32 * a, 32 * a + 32))
         o = S * r - kb
         for a in range(4):
-            ts(A("lb", 0, 96, 2, 32 * a, 32 * a + 32), A("fone", o, o + S, 1, 0, 32), 96.0, ALU.is_ge, 48.0, ALU.mult)
+            ts(A("lb", 0, 144, 3, 32 * a, 32 * a + 32), A("fone", o, o + S, 1, 0, 32), 96.0, ALU.is_ge, 48.0, ALU.mult)
         for a in range(4):
             ts(A("fd", 0, 128, 1, 32 * a, 32 * a + 32), A("fone", 0, 128, 1, 0, 32), 96.0, ALU.is_ge, 0.25, ALU.mult)
         scan(A("lo_"), A("la"), A("lb"), 0.0, ALU.mult, ALU.add)
-        cp("v", A("lz"), odd("lo_", 0, S))
-        for c_ in ((2, 1, 0) if r == 0 else (0, 2, 1) if r < N - 1 else (0, 1, 2)):
+        cp("v", A("lz", 0, 16), third("lo_", 2, 32, 16))
+        cp("v", A("lz", 16, S), third("lo_", 2, 0, 32))
+        both = len(nbs) == 2
+        for a, b_ in ((4, 28), (28, 48), (0, 4)) if both else ((0, 16), (16, 48)) if r == 0 else ((16, 32), (32, 48), (0, 16)):
             for b in range(2):
-                cp(vs, A("zt", 512 * c_ + b, 512 * c_ + 512, 2),
-                   A("fb", PW * b, PW * (b + 3), ind=A("lz", 16 * c_, 16 * c_ + 16)))
-            quant(zq, Z0 + 128 * c_, Z0 + 128 * c_ + 128, "zt", 512 * c_)
+                cp(vs, A("zt", 32 * a + b, 32 * b_, 2), A("fb", PW * b, PW * (b + 3), ind=A("lz", a, b_)))
+        if both:
+            quant("bq", 0, 192, "zt", 128)
+        quant(zq, Z0 + 256, Z0 + 384, "zt", 0)
+        for a, b_ in ((0, 128), (128, 256)) if r == N - 1 else ((0, 256),):
+            quant(zq, Z0 + a, Z0 + b_, "zt", 512 + 4 * a)
         for nm, cast, rs, ls_ in (("", u8, "ac", "sc"), ("s", None, "as", "ss")):
-            m1, l1 = borders((zq + nm, zq + nm), [64, 96, 96, 64], Z0, Z0 + C, Z0 + C, Z0, cast)
+            if both:
+                m1, l1 = borders(("bq" + nm, zq + nm), [56, 88, 88, 56], 96, 96, Z0 + C, Z0, cast)
+            else:
+                m1, l1 = borders((zq + nm, zq + nm), [56, 88, 88, 56], Z0, Z0 + C, Z0 + C, Z0, cast)
             remote(m1, "%s%d" % (rs, t), "%s%d" % (ls_, t), l1, sum(share(k) for k in nbs), HOP + 400)
         e_ = 128 if upper else i0 + n
         scan(A("pos", 1, 1 + e_), A("c78", 0, e_), A("fd", 0, e_), 0.0, ALU.add, ALU.add)
@@ -641,8 +688,7 @@ def rank_program(g, core, T, topo):
         lo_ = "lo"
         if upper:
             lo_ = "lu"
-            aff(vs, kc("pe"), col("pos", 128), kc("-sc"), 0.0)
-            aff(vs, A("lu"), A("lo"), 1.0, kc("pe"))
+            ts(A("lu"), A("lo"), col("pos", 128), ALU.add, kc("-sc"), ALU.mult)
             ts(kc("p8"), col("pos", i0), col("pos", 128), ALU.subtract, -8.0, ALU.mult)
         else:
             aff(vs, kc("p8"), col("pos", i0), -8.0, 0.0)
@@ -659,27 +705,43 @@ def rank_program(g, core, T, topo):
         tt(A("mm5", 49, 96, 2), c4, da, ALU.add)
         tt(A("mm5", 1, 48, 2), da, c1, ALU.subtract)
         scan(A("mm5", 96, 144), A("mm5", 48, 96), A("mm5", 0, 48), 0.0, ALU.mult, ALU.add)
+        if t == R - 1:
+            break
         cp("v", A("lm"), A("mm5", 97, 144, 2))
-        for h in (1, 0):
-            pick("gq", 192 * h, 192, zq, ZC, A("lm", 12 * h, 12 * h + 12))
-        for h in (1, 0):
+        for c0, w in PARTS:
+            pick("gq", c0, w, zq, ZC, A("lm", c0 // 16, (c0 + w) // 16))
+        for c0, w in PARTS:
             for b in range(4):
-                i = mm(7 - 2 * b, "wq", 128 * b, "gq", 192 * h, 192, [i] if 1 - h + b else [])
-                i = mm(6 - 2 * b, "eq", 128 * b, "gq", 192 * h, 192, [i])
+                i = mm(7 - 2 * b, "wq", 128 * b, "gq", c0, w, [i] if C - c0 - w + b else [])
+                i = mm(6 - 2 * b, "eq", 128 * b, "gq", c0, w, [i])
             for b in range(4):
-                o = 384 * b + 192 * h
-                relu("s", A("tmp", o, o + 192), ps(7 - 2 * b, 0, 192), 0.015625)
-                tt(A("xt", 768 * h + b, 768 * h + 768, 4), ps(6 - 2 * b, 0, 192), A("tmp", o, o + 192), ALU.add)
-            quant("tq", T0 + 192 * h, T0 + 192 * h + 192, "xt", 768 * h)
+                o = 384 * b + c0
+                relu("s", A("tmp", o, o + w), ps(7 - 2 * b, 0, w), 0.015625)
+                tt(A("xt", 4 * c0 + b, 4 * (c0 + w), 4), ps(6 - 2 * b, 0, w), A("tmp", o, o + w), ALU.add)
+            quant("tq", T0 + c0, T0 + c0 + w, "xt", 4 * c0)
 
-    pick("tf", 0, 384, "tq", 400, A("lf"))
-    for h in range(2):
-        mm(h, "vq", 0, "tf", 192 * h, 192)
-        cp("vs"[h], A("ysb", 192 * h, 192 * h + 192), ps(h, 0, 192))
-    dma("y", T.oc[:, :], A("tf", cast=u8), "doc")
+    for m_ in range(3):
+        c0, c1 = 128 * m_, 128 * m_ + 128
+        cp("v", A("lm", 8 * m_, 8 * m_ + 8), A("mm5", 97 + 2 * m_, 144, 6))
+        pick("gq", c0, 128, zq, ZC, A("lm", 8 * m_, 8 * m_ + 8))
+        for b in range(4):
+            i = mm(7 - 2 * b, "wq", 128 * b, "gq", c0, 128, [i] if m_ + b else [])
+            i = mm(6 - 2 * b, "eq", 128 * b, "gq", c0, 128, [i])
+        for b in range(4):
+            o = 384 * b + c0
+            relu("s", A("tmp", o, o + 128), ps(7 - 2 * b, 0, 128), 0.015625)
+            tt(A("xt", 4 * c0 + b, 4 * c1, 4), ps(6 - 2 * b, 0, 128), A("tmp", o, o + 128), ALU.add)
+        quant("tl", c0, c1, "xt", 4 * c0)
+        cp("v", A("tf", c0, c1, cast=dt.uint32), A("tl", c0, c1, ind=A("lf"), cast=dt.uint32))
+        cp("s", A("tfs", c0, c1), A("tls", c0, c1, ind=A("lf")))
+        dma("y", T.oc[:, 4 * c0:4 * c1], A("tf", c0, c1, cast=u8), "doc")
+    for m_ in range(3):
+        c0, c1 = 128 * m_, 128 * m_ + 128
+        mm(7 - 2 * m_, "vq", 0, "tf", c0, 128)
+        cp(vs, A("ysb", c0, c1), ps(7 - 2 * m_, 0, 128))
+        dma("y", T.y[:, c0:c1], A("ysb", c0, c1), "dy")
     for k in range(4):
         dma("sy"[k % 2], T.osc[4 * k:4 * k + 4, :], A("tfs", 0, 384, 1, 32 * k, 32 * k + 4), "dos")
-    dma("y", T.y[:, :], A("ysb"), "dy")
 
     count, known, mark = {}, {q: {} for q in eng}, {}
     for i, q in plan(ops):

@@ -13,7 +13,7 @@ T0 = 16
 Z0 = 96
 B0 = 576
 ZC = B0 + 3 * S
-PARTS = ((128, 256), (0, 128))
+PARTS = ((256, 128), (128, 128), (0, 128))
 F32, BF, I32, U16, CODE, PLANE = "float32", "bfloat16", "int32", "uint16", "float8_e4m3fn_x4", "uint8"
 WIDTH = {F32: 4, BF: 2, I32: 4, U16: 2, CODE: 4, PLANE: 1}
 
@@ -31,7 +31,7 @@ _buf(CODE, tn=384, tq=528, tf=384, uq=128, vq=128, wq=512, eq=512, mq=128, sq=12
      zq0=ZC, zq1=ZC, zq2=ZC)
 _buf(PLANE, tns=384, tqs=528, tfs=384, uqs=128, vqs=128, wqs=512, eqs=512, mqs=128, sqs=128, vcqs=128, fqs=128,
      gqs=384, zq0s=ZC, zq1s=ZC, zq2s=ZC)
-_buf(F32, kc=64, te=120, mo=1048, mz=160, tc=24, ee=96, we=128, ww=128, wm=128, nb=120, t3=360, u3=360, tau=360,
+_buf(F32, kc=64, te=244, mo=1048, mz=220, tc=24, ee=96, we=128, ww=128, wm=128, t3=360, u3=360, tau=360,
      tau2=360, dd=120, c3=144, c8=64, flo=24, wb=24, mc=8, acc=8, dump=64,
      sp=64, prow=52, oa=96, la=144, lb=144, lo_=144, kt=256, kw=128, km=4, key=8, inr=256, row=256,
      c78=128, pos=132, t7=68, th=68, cl=408, rs=6, sums=8, lo=6, lu=6, dk=144, mm5=144, tmp=1536, ysb=384,
@@ -47,8 +47,9 @@ COUNTER = {"v": "cv", "s": "cs", "p": "cp", "g": "cg"}
 CY, GAT, WAKE, PE, HOP, DMA = 0.95, 1.4, 195.0, 0.6, 1200.0, 1200.0
 FINE = ("oa", "tq", "mo", "mz", "te", "cn", "cq", "tc", "gq", "gqs", "xt", "tmp", "ca", "cb", "tau",
         "th", "rr", "mm5", "cl", "fb", "zt")
-FIRST = 800.0
-SPARE, TRIES, SHAKE, SPAN = 150.0, 1200, 300.0, 3000.0
+FIRST, EARLY, ALIKE, SHIFT, MOVES, SLACK = 800.0, 0.25, 0.7, {}, 0, 60.0
+SPARE, TRIES, SHAKE, SPAN = 150.0, 2400, 200.0, 1500.0
+AHEAD = {"tc": 1000.0, "cl0": 1000.0, "cl1": 1000.0, "cl2": 1000.0}
 VARIANTS = ((195.0, 1.0, 1.0, 1.0), (130.0, 1.15, 0.8, 0.9), (230.0, 1.2, 1.2, 1.5))
 
 
@@ -82,38 +83,6 @@ def clash(a, b):
     return not (a[3] == b[3] and a[3] > 1 and (a[1] - b[1]) % a[3] != 0)
 
 
-def schedule(ops):
-    n = len(ops)
-    after, prio = [[] for o in ops], [0.0] * n
-    for i in range(n - 1, -1, -1):
-        prio[i] = min(ops[i]["cost"].values()) + max(
-            [prio[j] + (0.0 if i in ops[j]["order"] else ops[i]["lat"] + WAKE) for j in after[i]] + [ops[i]["lat"]])
-        for j in ops[i]["deps"]:
-            after[j].append(i)
-    prio = [prio[i] + AHEAD.get(ops[i]["tag"], 0.0) for i in range(n)]
-    left, at = [len(o["deps"]) for o in ops], [0.0] * n
-    ready = [i for i in range(n) if not left[i]]
-    free, done, order = {}, [0.0] * n, []
-    while ready:
-        cand = []
-        for i in ready:
-            pen = SPARE.get(ops[i]["tag"], 100)
-            q = min((max(at[i], free.get(q, 0.0)) + c_ + (pen if q == "v" else 0.0), q) for q, c_ in ops[i]["cost"].items())[1]
-            end = max(at[i], free.get(q, 0.0)) + ops[i]["cost"][q]
-            cand.append((end, q, i, end - ops[i]["cost"][q]))
-        end, q, i, t = min(cand)
-        end, q, i, t = max([x for x in cand if x[1] == q and x[3] < end] + [(end, q, i, t)], key=lambda x: prio[x[2]])
-        free[q], done[i] = end, end + ops[i]["lat"]
-        order.append((i, q))
-        ready.remove(i)
-        for j in after[i]:
-            at[j] = max(at[j], end if i in ops[j]["order"] else done[i] + WAKE)
-            left[j] -= 1
-            if not left[j]:
-                ready.append(j)
-    return order, done
-
-
 def plan(ops):
     n = len(ops)
     pre = []
@@ -131,35 +100,31 @@ def plan(ops):
         way[i] = min(ops[i]["cost"].values()) + max(
             [way[j] + (0.0 if soft else ops[i]["lat"] + WAKE) for j, soft in after[i]] + [ops[i]["lat"]])
 
+    way = [way[i] + AHEAD.get(ops[i]["out"], 0.0) for i in range(n)]
     gap = [[(j, 0.0 if soft else ops[j]["lat"] + WAKE) for j, soft in pre[i]] for i in range(n)]
     pag = [[(j, 0.0 if soft else ops[i]["lat"] + WAKE) for j, soft in after[i]] + [(n, ops[i]["lat"])] for i in range(n)]
 
-    def place(prio, back=False):
+    def place(prio, spare, back=False):
         left = [len(p) for p in (after if back else pre)]
-        ready = [i for i in range(n) if not left[i]]
+        ready = sorted((prio[i], i) for i in range(n) if not left[i])
         busy, start, end, where = {}, [0.0] * n, [0.0] * (n + 1), [None] * n
         while ready:
-            i = max(ready, key=lambda k: prio[k])
-            ready.remove(i)
+            i = ready.pop()[1]
             at = 0.0
             for j, d in (pag if back else gap)[i]:
                 if end[j] + d > at:
                     at = end[j] + d
             best = None
             for q, c_ in ops[i]["cost"].items():
-                b, t, k = busy.setdefault(q, []), at, 0
-                lo_, hi_ = 0, len(b)
-                while lo_ < hi_:
-                    mid = (lo_ + hi_) // 2
-                    if b[mid][1] <= at:
-                        lo_ = mid + 1
-                    else:
-                        hi_ = mid
-                k = lo_
-                while k < len(b) and b[k][0] < t + c_:
-                    t = max(t, b[k][1])
+                b, t = busy.setdefault(q, []), at
+                k = m_ = len(b)
+                while k and b[k - 1][1] > at:
+                    k -= 1
+                while k < m_ and b[k][0] < t + c_:
+                    if b[k][1] > t:
+                        t = b[k][1]
                     k += 1
-                x = (t + c_ + (SPARE if q == "v" else 0.0), t, q, k, c_)
+                x = (t + c_ + (spare[i] if q == "v" else 0.0), t, q, k, c_)
                 if best is None or x < best:
                     best = x
             x, t, q, k, c_ = best
@@ -168,7 +133,10 @@ def plan(ops):
             for j, soft in (pre if back else after)[i]:
                 left[j] -= 1
                 if not left[j]:
-                    ready.append(j)
+                    k = len(ready)
+                    while k and ready[k - 1][0] > prio[j]:
+                        k -= 1
+                    ready.insert(k, (prio[j], j))
         return end[:n] if back else (sorted(range(n), key=lambda k: (start[k], k)), where, start)
 
     def length(order, where):
@@ -185,21 +153,54 @@ def plan(ops):
                 end[i] = free[q] = t + ops[i]["cost"][q] * (fp if q == "p" else fc)
                 done[i], last[q], by[i] = end[i] + ops[i]["lat"] * fl, i, k
             i = max(range(n), key=lambda k: done[k])
-            tot += done[i]
-            while i is not None:
-                if by[i][1] and by[i][0] is not None:
-                    held.append((i, by[i][0]))
-                i = by[i][0]
+            tot += done[i] + EARLY * sum(end[k] for k in sends)
+            seen = set()
+            for i in [i] + sends:
+                while i is not None and i not in seen:
+                    seen.add(i)
+                    if by[i][1] and by[i][0] is not None:
+                        held.append((i, by[i][0]))
+                    i = by[i][0]
         return tot, held
 
+    sends = [i for i in range(n) if ops[i]["tag"] in ("sk", "sc")]
+    last = [i for i in range(n) if not after[i]]
+
+    def rough(start):
+        return max(start[i] + ops[i]["lat"] for i in last) + EARLY * sum(start[k] for k in sends)
+
+    same = {}
+    for i in range(n):
+        same.setdefault(ops[i]["kind"], []).append(i)
     rng = np.random.default_rng(0)
-    prio = list(way)
-    order, where, start = place(prio)
-    best, held = length(order, where)
+    label = {j: (k, x) for k in same for x, j in enumerate(same[k])}
+    best = None
+    for found in ({}, SHIFT):
+        trial = [way[i] + found.get(label[i], (0.0, SPARE))[0] for i in range(n)]
+        lean = [found.get(label[i], (0.0, SPARE))[1] for i in range(n)]
+        o2, w2, s2 = place(trial, lean)
+        x, h2 = length(o2, w2)
+        if best is None or x < best:
+            best, held, prio, spare, order, where, start = x, h2, trial, lean, o2, w2, s2
     for it in range(TRIES):
-        trial = list(prio)
+        trial, lean = list(prio), spare
         if it % 50 < 2:
-            trial = place(start, True)
+            trial = place(start, spare, True)
+        elif it % 8 == 4:
+            free = [k for pair in held for k in pair if len(ops[k]["cost"]) > 1] or [0]
+            i, lean = free[int(rng.integers(len(free)))], list(spare)
+            for j in same[ops[i]["kind"]] if it < TRIES * ALIKE else [i]:
+                lean[j] = 1000.0 if where[i] == "v" else -1000.0
+        elif it % 4 == 2:
+            i, d = int(rng.integers(n)), float(rng.normal(0.0, 2 * SHAKE))
+            cone, todo = {i}, [i]
+            while todo:
+                for j, soft in (pre if d > 0 else after)[todo.pop()]:
+                    if j not in cone and abs(start[j] - start[i]) < SPAN / 2:
+                        cone.add(j)
+                        todo.append(j)
+            for j in cone:
+                trial[j] += d
         elif it % 4 == 0 or not held:
             at, z = rng.random() * max(start), rng.normal(0.0, SHAKE, n)
             for i in range(n):
@@ -208,15 +209,22 @@ def plan(ops):
         else:
             i, j = held[int(rng.integers(len(held)))]
             d = max(prio[j] - prio[i], 0.0) + rng.random() * 2 * SHAKE
-            if it % 2:
+            if it % 4 == 1:
                 trial[j] -= d
             else:
                 for k in [i] + [k for k, soft in pre[i]]:
                     trial[k] += d
-        o2, w2, s2 = place(trial)
+        if it % 50 >= 2 and it < TRIES * ALIKE:
+            for i in [i for i in range(n) if trial[i] != prio[i]]:
+                for j in same[ops[i]["kind"]]:
+                    trial[j] = prio[j] + trial[i] - prio[i]
+        o2, w2, s2 = place(trial, lean)
+        if rough(s2) > rough(start) + SLACK:
+            continue
         x, h2 = length(o2, w2)
         if x <= best:
-            best, held, prio, order, where, start = x, h2, trial, o2, w2, s2
+            best, held, prio, spare, order, where, start = x, h2, trial, lean, o2, w2, s2
+    SHIFT.update({label[i]: (prio[i] - way[i], spare[i]) for i in range(n)})
     return [(i, where[i]) for i in order]
 
 
@@ -255,7 +263,8 @@ def rank_program(g, core, T, topo):
             last_g.append(i)
         ops.append({"fns": fns, "cost": cost, "hard": hard, "deps": hard | soft,
                     "order": set() if "x" in fns else soft - hard, "sem": sem, "inc": inc, "chain": chain,
-                    "lat": lat, "tag": tag or (name(outs[0]) if outs else sem[:2])})
+                    "lat": lat, "tag": tag or (name(outs[0]) if outs else sem[:2]),
+                    "out": outs[0][0] if outs else None, "kind": tuple((a[0][:2],) + a[1:6] for a in list(outs[:1]) + rd[:1])})
         return i
 
     def price(out, in_, k=1.0):
@@ -304,7 +313,12 @@ def rank_program(g, core, T, topo):
                lambda e: e.activation(X(out), X(in_), ACT.Relu, scale=k), out, [in_])
 
     def fill(out, v):
-        emit({"v": lambda e: e.memset(X(out), v)}, {"v": price(out, out)}, [out], [])
+        if out[0] == "zer" or size(out) > 256:
+            emit({"v": lambda e: e.memset(X(out), v)}, {"v": price(out, out)}, [out], [])
+            return
+        z = A("zer", 0, size(out), 1, out[4], out[5])
+        emit({"v": lambda e: e.memset(X(out), v), "s": lambda e: e.activation(X(out), X(z), ACT.Copy, bias=v)},
+             {"v": price(out, out), "s": CY * max(64.0, size(out))}, [out], [z])
 
     def tr(out, in_):
         vec(lambda e: e.transpose(X(out), X(in_)), [out], [in_])
@@ -346,7 +360,7 @@ def rank_program(g, core, T, topo):
         for i, (src, dst, ranks) in enumerate(moves):
             es = [x for x in topo.engines(core, T.cores[ranks[0]])
                   if all(x in topo.engines(core, T.cores[k]) for k in ranks)]
-            es = es[i * len(es) // n_:(i + 1) * len(es) // n_]
+            es = es[i::n_]
             ids = [DstId(rid=topo.addr(T.cores[k])[0], pnc=topo.addr(T.cores[k])[1]) for k in ranks]
             trs.append(RemoteDMATransfer(dst_ids=ids, dma_engine_mask=sum(1 << x for x in es), remote_sem=T.sem[rsem],
                                          srcs=[X(src)], dsts=[X(dst) for k in ranks]))
@@ -420,7 +434,8 @@ def rank_program(g, core, T, topo):
     quant("uq", 0, 128, "uin", 0)
     quant("tn", 0, 192, "xin", 0)
     quant("tn", 192, 384, "xin", 768)
-    pick("tq", T0, 384, "tn", 384, A("l0"))
+    for c0, w in PARTS:
+        pick("tq", T0 + c0, w, "tn", 384, A("l0", c0 // 16, (c0 + w) // 16))
     quant("vq", 0, 128, "vin", 0)
     fill(A("eb"), 0.0)
     ts(A("eb", 3, 512, 4), A("io1"), P, ALU.is_equal)
@@ -447,7 +462,9 @@ def rank_program(g, core, T, topo):
     aff(vs, A("w5", 0, 3), A("io1", 0, 48, 16), 1.0, kc("be48"))
     cp("v", A("l48", 0, 3), A("w3", 0, 3))
     ts(A("l48", 6, 9), A("w3", 0, 3), float(S), ALU.add)
-    aff(vs, kc("ns"), SLOT, -1.0, -0.5)
+    ts(kc("ns"), kc("be"), SLOT, ALU.subtract, -0.5, ALU.add)
+    aff(vs, kc("at"), kc("g7"), -1.0, 2.0)
+    ts(kc("at"), kc("ns"), 0.5, ALU.add, kc("at"), ALU.mult)
     aff(vs, kc("w2"), SLOT, -1.0, 8.0)
     aff(vs, kc("sb"), SLOT, 48.0, 24.0)
     aff(vs, kc("sb"), ODD, 2.0 * PW, kc("sb"))
@@ -526,15 +543,18 @@ def rank_program(g, core, T, topo):
     def third(buf, k, o, w):
         return A(buf, 3 * o + k, 3 * (o + w), 3)
 
-    def level(o, zo, eo, do, w):
-        tt(A("te", 2 * eo + 2, 2 * (eo + w) + 2, 2), mo(o, w), mo(o + 2, w), ALU.min)
-        cp(vs, odd("mz", zo + 1, w), mo(o + 1, w))
-        scan(A("mo", 8 * do + 11, 8 * (do + w) + 8, 4), A("mz", 2 * zo + 2, 2 * (zo + w) + 2),
-             A("te", 2 * eo + 2, 2 * (eo + w) + 2), 0.0, ALU.min, ALU.max)
+    def nb(o, w):
+        return A("te", 2 * o + 2, 2 * (o + w) + 2, 2)
 
-    def weights(o, c_, e_):
-        cp("s", A("we", o, o + 128), e_)
-        tt(A("ww", o, o + 128), c_, A("we", o, o + 128), ALU.max)
+    def level(o, do, w):
+        tt(nb(o, w + 1), mo(o, w + 1), mo(o + 1, w + 1), ALU.min)
+        cp(vs, odd("mz", o + 1, w), mo(o + 2, w))
+        scan(A("mo", 8 * do + 11, 8 * (do + w) + 8, 4), A("mz", 2 * o + 2, 2 * (o + w) + 2),
+             A("te", 2 * o + 2, 2 * (o + w) + 2), 0.0, ALU.min, ALU.max)
+
+    def weights(o, w, c_, e_):
+        cp(vs, A("we", o, o + w), e_)
+        tt(A("ww", o, o + w), c_, A("we", o, o + w), ALU.max)
 
     def twice(o, do, wo, running=False):
         tt(A("wm", wo, wo + 64), A("mo", 8 * o, 8 * o + 80, ind=A("lw", 16, 20)), A("ww", wo, wo + 64), ALU.max)
@@ -542,9 +562,8 @@ def rank_program(g, core, T, topo):
              ALU.max, ALU.min)
 
     def back(o, w):
-        tt(A("nb", o - 2, o + w), mo(o - 2, w + 2), mo(o - 1, w + 2), ALU.min)
-        tt(third("t3", 1, o, w), A("nb", o - 2, o + w - 2), mo(o, w), ALU.is_le)
-        tt(third("t3", 2, o, w), mo(o - 1, w), A("nb", o, o + w), ALU.is_le)
+        tt(third("t3", 1, o, w), nb(o - 2, w), mo(o, w), ALU.is_le)
+        tt(third("t3", 2, o, w), mo(o - 1, w), nb(o, w), ALU.is_le)
         scan(A("tau", 3 * o, 3 * (o + w)), A("c3", 0, 3 * w), A("t3", 3 * o, 3 * (o + w)), 0.0, ALU.mult, ALU.add)
 
     def back2(o, w):
@@ -572,6 +591,13 @@ def rank_program(g, core, T, topo):
             m1, l1 = borders((src + nm, zq + nm), [8, 12, 12, 8], o, o + S, B0 + 2 * S, B0 + S, cast)
             remote(m1, "%s%d" % (rs, t), "%s%d" % (ls_, t), l1, sum(share(k) for k in nbs), HOP + (0 if t else FIRST))
 
+    both = len(nbs) == 2
+    rot = 17 if both else 16
+    pieces = (((0, 16), (16, 48)), ((6, 24), (24, 48), (0, 6)), ((10, 28), (28, 48), (0, 10)),
+              ((16, 32), (32, 48), (0, 16)))[r]
+    if both:
+        quant("bq", 48 * (2 - r), 48 * (2 - r) + 128, "zer", 0)
+
     for b in range(4):
         mm(b, "eq", 128 * b, "tn", 0, 384)
         cp(vs, A("ft", b, 4 * S, 4), ps(b, 0, 384, 8))
@@ -584,16 +610,17 @@ def rank_program(g, core, T, topo):
             mm(l, "tq", T0 + 48 * l - sh, "uq", 0, 128)
         score(mo(1, 8), 0, kc("eb"))
         score(mo(11, 8), 7)
-        for o, gr in enumerate((1, 6, 2, 5, 3, 4)):
+        for o, gr in ((0, 1), (1, 6), (2, 2), (3, 5), (4, 3), (5, 4), (6, 4), (10, 6)):
             score(odd("te", 10 * o + 1, 8), gr)
         for o, gr in enumerate((5, 7, 4, 6)):
             score(A("ee", 16 * o + 1, 16 * o + 9), gr)
         for b in range(4):
             mm(b, "eq", 128 * b, "tq", T0, 384)
         for b in range(4):
-            cp("s", A("fb", PW * b, PW * b + 384), ps(b, 0, 384))
+            for c0 in (0, 192):
+                cp("s", A("fb", PW * b + c0, PW * b + c0 + 192), ps(b, c0, c0 + 192))
         for o in (0, 20, 40):
-            level(o, o, o, o + 20, 18)
+            level(o, o + 20, 18)
         for x in range(3):
             tt(A("tc", 8 * x, 8 * x + 8), mo(60 + x, 8), mo(71, 8), ALU.max)
         for a, b, w in ((0, 0, 64), (64, 32, 32), (96, 0, 32)) if r in (0, 3) else ((0, 32, 32), (32, 0, 32), (64, 0, 64)):
@@ -603,11 +630,13 @@ def rank_program(g, core, T, topo):
         remote([(cost[r], cost[r], others)], "ak%d" % t, "sk%d" % t, [cost[k] for k in others],
                sum(len(topo.engines(T.cores[k], core)) for k in others), HOP + 300)
         tt(A("ee", 64, 89), A("ee", 32, 57), A("ee", 33, 58), ALU.min)
-        weights(0, A("ee", 32, 96, ind=A("lw", 0, 8)), A("ee", 0, 32, ind=A("lw", 8, 16)))
+        weights(0, 128, A("ee", 32, 96, ind=A("lw", 0, 8)), A("ee", 0, 32, ind=A("lw", 8, 16)))
         twice(60, 100, 0)
         twice(100, 120, 64, True)
-        level(60, 60, 50, 80, 8)
-        level(100, 70, 10, 110, 8)
+        level(60, 80, 8)
+        level(100, 110, 8)
+        for o in (80, 110):
+            tt(nb(o, 9), mo(o, 9), mo(o + 1, 9), ALU.min)
         for o, w in ((2, 28), (42, 28), (82, 28), (112, 7)):
             back(o, w)
         for o, w in ((22, 47), (102, 7)):
@@ -623,7 +652,11 @@ def rank_program(g, core, T, topo):
         mm(4, "sq", 0, "mq", 0, 128)
         for m_ in range(3):
             aff("v", col("lv", m_), ps(4, 48 + m_, 49 + m_), kc("al48"), col("w5", m_))
-        aff(vs, A("prow", 0, S), ps(4, 0, S), kc("al"), kc("be"))
+        mm(5, "sq", 0, "mq", 0, 128)
+        act(A("oa", 0, 48), ps(5, 0, S), ACT.Sign, kc("ns"), kc("al"))
+        ts(A("oa", 48, 96), ps(4, 0, S), kc("at"), ALU.is_equal, kc("w2"), ALU.mult)
+        if t == R - 1:
+            aff("v", A("prow", 0, S), ps(4, 0, S), kc("al"), kc("be"))
         for b in range(4):
             cp(vs, A("vt", b, 192, 4), A("fb", PW * b, PW * b + 384, ind=A("lv", 0, 3)))
             if t:
@@ -632,11 +665,9 @@ def rank_program(g, core, T, topo):
         if t:
             firsts(t, "vcq", S)
         for b in range(4):
-            mm(4 + (b + 1) % 4, "wq", 128 * b, "vcq", 0, 128)
+            mm(4 + (b + 2) % 4, "wq", 128 * b, "vcq", 0, 128)
         for b in range(4):
-            relu(vs, A("fb", PW * b + 384, PW * b + 432), ps(4 + (b + 1) % 4, 0, 48), 0.03125)
-        act(A("oa", 0, 48), A("prow", 0, S), ACT.Sign, bias=kc("ns"))
-        ts(A("oa", 48, 96), A("prow", 0, S), SLOT, ALU.is_equal, kc("w2"), ALU.mult)
+            relu(vs, A("fb", PW * b + 384, PW * b + 432), ps(4 + (b + 2) % 4, 0, 48), 0.03125)
         tt(third("la", 1, 0, S), A("oa", 0, 48), A("oa", 48, 96), ALU.add)
         aff(vs, third("lb", 1, 0, S), A("oa", 0, 48), -24.0, kc("sb"))
         if t == R - 1:
@@ -664,20 +695,19 @@ def rank_program(g, core, T, topo):
         for a in range(4):
             ts(A("fd", 0, 128, 1, 32 * a, 32 * a + 32), A("fone", 0, 128, 1, 0, 32), 96.0, ALU.is_ge, 0.25, ALU.mult)
         scan(A("lo_"), A("la"), A("lb"), 0.0, ALU.mult, ALU.add)
-        cp("v", A("lz", 0, 16), third("lo_", 2, 32, 16))
-        cp("v", A("lz", 16, S), third("lo_", 2, 0, 32))
-        both = len(nbs) == 2
-        for a, b_ in ((4, 28), (28, 48), (0, 4)) if both else ((0, 16), (16, 48)) if r == 0 else ((16, 32), (32, 48), (0, 16)):
+        cp("v", A("lz", 0, rot), third("lo_", 2, S - rot, rot))
+        cp("v", A("lz", rot, S), third("lo_", 2, 0, S - rot))
+        for a, b_ in pieces:
             for b in range(2):
                 cp(vs, A("zt", 32 * a + b, 32 * b_, 2), A("fb", PW * b, PW * (b + 3), ind=A("lz", a, b_)))
         if both:
-            quant("bq", 0, 192, "zt", 128)
-        quant(zq, Z0 + 256, Z0 + 384, "zt", 0)
-        for a, b_ in ((0, 128), (128, 256)) if r == N - 1 else ((0, 256),):
-            quant(zq, Z0 + a, Z0 + b_, "zt", 512 + 4 * a)
+            quant("bq", 88 - 8 * (rot - pieces[0][0]), 88 + 8 * (pieces[0][1] - rot), "zt", 32 * pieces[0][0])
+        quant(zq, Z0 + C - 8 * rot, Z0 + C, "zt", 0)
+        for a, b_ in ((0, 128), (128, 256)) if r == N - 1 else ((0, C - 8 * rot),):
+            quant(zq, Z0 + a, Z0 + b_, "zt", 32 * rot + 4 * a)
         for nm, cast, rs, ls_ in (("", u8, "ac", "sc"), ("s", None, "as", "ss")):
             if both:
-                m1, l1 = borders(("bq" + nm, zq + nm), [56, 88, 88, 56], 96, 96, Z0 + C, Z0, cast)
+                m1, l1 = borders(("bq" + nm, zq + nm), [56, 88, 88, 56], 88, 88, Z0 + C, Z0, cast)
             else:
                 m1, l1 = borders((zq + nm, zq + nm), [56, 88, 88, 56], Z0, Z0 + C, Z0 + C, Z0, cast)
             remote(m1, "%s%d" % (rs, t), "%s%d" % (ls_, t), l1, sum(share(k) for k in nbs), HOP + 400)
@@ -712,12 +742,12 @@ def rank_program(g, core, T, topo):
             pick("gq", c0, w, zq, ZC, A("lm", c0 // 16, (c0 + w) // 16))
         for c0, w in PARTS:
             for b in range(4):
-                i = mm(7 - 2 * b, "wq", 128 * b, "gq", c0, w, [i] if C - c0 - w + b else [])
-                i = mm(6 - 2 * b, "eq", 128 * b, "gq", c0, w, [i])
+                mm(7 - b, "wq", 128 * b, "gq", c0, w)
+                mm(3 - b, "eq", 128 * b, "gq", c0, w)
             for b in range(4):
                 o = 384 * b + c0
-                relu("s", A("tmp", o, o + w), ps(7 - 2 * b, 0, w), 0.015625)
-                tt(A("xt", 4 * c0 + b, 4 * (c0 + w), 4), ps(6 - 2 * b, 0, w), A("tmp", o, o + w), ALU.add)
+                relu("s", A("tmp", o, o + w), ps(7 - b, 0, w), 0.015625)
+                tt(A("xt", 4 * c0 + b, 4 * (c0 + w), 4), ps(3 - b, 0, w), A("tmp", o, o + w), ALU.add)
             quant("tq", T0 + c0, T0 + c0 + w, "xt", 4 * c0)
 
     for m_ in range(3):
@@ -725,8 +755,8 @@ def rank_program(g, core, T, topo):
         cp("v", A("lm", 8 * m_, 8 * m_ + 8), A("mm5", 97 + 2 * m_, 144, 6))
         pick("gq", c0, 128, zq, ZC, A("lm", 8 * m_, 8 * m_ + 8))
         for b in range(4):
-            i = mm(7 - 2 * b, "wq", 128 * b, "gq", c0, 128, [i] if m_ + b else [])
-            i = mm(6 - 2 * b, "eq", 128 * b, "gq", c0, 128, [i])
+            mm(7 - 2 * b, "wq", 128 * b, "gq", c0, 128)
+            mm(6 - 2 * b, "eq", 128 * b, "gq", c0, 128)
         for b in range(4):
             o = 384 * b + c0
             relu("s", A("tmp", o, o + 128), ps(7 - 2 * b, 0, 128), 0.015625)

@@ -31,9 +31,9 @@ _buf(CODE, tn=384, tq=528, tf=384, uq=128, vq=128, wq=512, eq=512, mq=128, sq=12
      zq0=ZC, zq1=ZC, zq2=ZC)
 _buf(PLANE, tns=384, tqs=528, tfs=384, uqs=128, vqs=128, wqs=512, eqs=512, mqs=128, sqs=128, vcqs=128, fqs=128,
      gqs=384, zq0s=ZC, zq1s=ZC, zq2s=ZC)
-_buf(F32, kc=64, te=244, mo=1048, mz=220, tc=24, ee=96, we=128, ww=128, wm=128, t3=360, u3=360, tau=360,
-     tau2=360, dd=120, c3=144, c8=64, flo=24, wb=24, mc=8, acc=8, dump=64,
-     sp=64, prow=52, oa=96, la=144, lb=144, lo_=144, kt=256, kw=128, km=4, key=8, inr=256, row=256,
+_buf(F32, kc=64, te=244, mo=1048, mz=220, tc=24, ee=64, ww=128, wm=128, t3=330, u3=330, v3=330, tau=330,
+     tau2=330, q0=28, q1=28, q2=28, c3=84, c8=128, flo=24, wb=24, mc=8, acc=8, dump=64,
+     sp=64, prow=52, oa=144, la=144, lb=144, lo_=144, kt=256, kw=128, km=4, key=8, inr=256, row=256,
      c78=128, pos=132, t7=68, th=68, cl=408, rs=6, sums=8, lo=6, lu=6, dk=144, mm5=144, tmp=1536, ysb=384,
      olb=48, o8=48, io1=128, w0=24, w3=8, w4=8, w5=8, thp=4, cl0=128, cl1=128, cl2=128)
 _buf(I32, pi=8, xr=96)
@@ -42,15 +42,19 @@ _buf(CODE, tl=384, bq=192)
 _buf(PLANE, tls=384, bqs=192)
 
 SEMAPHORES = ["cv", "cs", "cp", "cg", "dx", "dx2", "du", "dv", "dw", "dws", "dol", "dy", "doc", "dos"] + [
-    "%s%d" % (k, t) for t in range(R) for k in ("ac", "as", "ak", "af", "ag", "sc", "ss", "sk", "sf", "sg")]
+    "%s%d" % (k, t) for t in range(R) for k in ("ac", "as", "ak", "af", "ag", "sc", "ss", "sk", "sf", "sg", "dh", "dhs",
+                                                "dl", "dls")]
 COUNTER = {"v": "cv", "s": "cs", "p": "cp", "g": "cg"}
-CY, GAT, WAKE, PE, HOP, DMA = 0.95, 1.4, 195.0, 0.6, 1200.0, 1200.0
+CY, GAT, WAKE, PE, HOP, DMA = 0.95, 1.4, 200.0, 0.6, 800.0, 1200.0
 FINE = ("oa", "tq", "mo", "mz", "te", "cn", "cq", "tc", "gq", "gqs", "xt", "tmp", "ca", "cb", "tau",
         "th", "rr", "mm5", "cl", "fb", "zt")
-FIRST, EARLY, ALIKE, SHIFT, MOVES, SLACK = 800.0, 0.25, 0.7, {}, 0, 60.0
-SPARE, TRIES, SHAKE, SPAN = 150.0, 2400, 200.0, 1500.0
-AHEAD = {"tc": 1000.0, "cl0": 1000.0, "cl1": 1000.0, "cl2": 1000.0}
-VARIANTS = ((195.0, 1.0, 1.0, 1.0), (130.0, 1.15, 0.8, 0.9), (230.0, 1.2, 1.2, 1.5))
+FIRST, EARLY, ALIKE, SLACK, PLAN = 800.0, 0.03, 0.75, 60.0, []
+DM, STARTS, MARKS, SEED = 1, 4, ("lm", "vcq", "tq"), 0
+SPARE, ALONE, TRIES, SHAKE, SPAN = 150.0, 450, 1800, 200.0, 1500.0
+AHEAD = dict([(k, 1000.0) for k in ("tc", "cl0", "cl1", "cl2")]
+             + [(k, 600.0) for k in ("inr", "key", "row", "cmp", "cnt", "fone", "fd")]
+             + [(k, 400.0) for k in ("pos", "t7", "th")])
+VARIANTS = ((200.0, 1.0, 1.0, 1.0), (150.0, 1.15, 0.8, 0.7), (230.0, 1.2, 1.2, 1.6))
 
 
 def A(name, c0=0, c1=None, step=1, p0=0, p1=128, ind=None, cast=None):
@@ -83,31 +87,50 @@ def clash(a, b):
     return not (a[3] == b[3] and a[3] > 1 and (a[1] - b[1]) % a[3] != 0)
 
 
-def plan(ops):
+def plan(ranks, TRIES, EARLY, found, SEED):
+    ops, pre, base, sent = [], [], [], {}
+    for r, own in enumerate(ranks):
+        base.append(len(ops))
+        behind = []
+        for i, o in enumerate(own):
+            far = near = 0
+            for j in o["hard"]:
+                far |= behind[j]
+                near |= 1 << j
+            behind.append(far | near)
+            pre.append([(base[r] + j, j in o["order"]) for j in sorted(o["deps"]) if not far >> j & 1])
+            ops.append(dict(o, cost={q + str(r): c_ for q, c_ in o["cost"].items()}))
+            sent[r, o["sem"]] = base[r] + i
     n = len(ops)
-    pre = []
-    for o in ops:
-        far = set()
-        for j in o["deps"]:
-            far |= ops[j]["hard"] if j in o["hard"] else set()
-        pre.append([(j, j in o["order"]) for j in o["deps"] if j not in far])
+    for i in range(n):
+        pre[i] += [(j, False) for j in sorted({sent[k % len(ranks), s_] for k, s_ in ops[i]["from"]})]
     after = [[] for o in ops]
     for i in range(n):
         for j, soft in pre[i]:
             after[j].append((i, soft))
-    way = [0.0] * n
-    for i in range(n - 1, -1, -1):
+    left, todo, way = [len(a) for a in after], [i for i in range(n) if not after[i]], [0.0] * n
+    while todo:
+        i = todo.pop()
         way[i] = min(ops[i]["cost"].values()) + max(
             [way[j] + (0.0 if soft else ops[i]["lat"] + WAKE) for j, soft in after[i]] + [ops[i]["lat"]])
+        for j, soft in pre[i]:
+            left[j] -= 1
+            if not left[j]:
+                todo.append(j)
 
     way = [way[i] + AHEAD.get(ops[i]["out"], 0.0) for i in range(n)]
     gap = [[(j, 0.0 if soft else ops[j]["lat"] + WAKE) for j, soft in pre[i]] for i in range(n)]
     pag = [[(j, 0.0 if soft else ops[i]["lat"] + WAKE) for j, soft in after[i]] + [(n, ops[i]["lat"])] for i in range(n)]
 
+    cost = [list(o["cost"].items()) for o in ops]
+    queues = {q for c_ in cost for q, x in c_}
+    edges = [[[(j, 0.0 if soft else ops[j]["lat"] * fl + wake) for j, soft in pre[i]] for i in range(n)]
+             for wake, fc, fp, fl in VARIANTS]
+
     def place(prio, spare, back=False):
         left = [len(p) for p in (after if back else pre)]
         ready = sorted((prio[i], i) for i in range(n) if not left[i])
-        busy, start, end, where = {}, [0.0] * n, [0.0] * (n + 1), [None] * n
+        busy, start, end, where = {q: [] for q in queues}, [0.0] * n, [0.0] * (n + 1), [None] * n
         while ready:
             i = ready.pop()[1]
             at = 0.0
@@ -115,16 +138,18 @@ def plan(ops):
                 if end[j] + d > at:
                     at = end[j] + d
             best = None
-            for q, c_ in ops[i]["cost"].items():
-                b, t = busy.setdefault(q, []), at
+            for q, c_ in cost[i]:
+                b, t = busy[q], at
                 k = m_ = len(b)
+                while k > 7 and b[k - 8][1] > at:
+                    k -= 8
                 while k and b[k - 1][1] > at:
                     k -= 1
                 while k < m_ and b[k][0] < t + c_:
                     if b[k][1] > t:
                         t = b[k][1]
                     k += 1
-                x = (t + c_ + (spare[i] if q == "v" else 0.0), t, q, k, c_)
+                x = (t + c_ + (spare[i] if q[0] == "v" else 0.0), t, q, k, c_)
                 if best is None or x < best:
                     best = x
             x, t, q, k, c_ = best
@@ -133,37 +158,41 @@ def plan(ops):
             for j, soft in (pre if back else after)[i]:
                 left[j] -= 1
                 if not left[j]:
-                    k = len(ready)
-                    while k and ready[k - 1][0] > prio[j]:
-                        k -= 1
-                    ready.insert(k, (prio[j], j))
+                    k, m_, x = 0, len(ready), prio[j]
+                    while k < m_:
+                        if ready[(k + m_) >> 1][0] > x:
+                            m_ = (k + m_) >> 1
+                        else:
+                            k = ((k + m_) >> 1) + 1
+                    ready.insert(k, (x, j))
         return end[:n] if back else (sorted(range(n), key=lambda k: (start[k], k)), where, start)
 
     def length(order, where):
         tot, held = 0.0, []
-        for wake, fc, fp, fl in VARIANTS:
-            free, last, end, done, by = {}, {}, [0.0] * n, [0.0] * n, [None] * n
+        before, at = [n] * n, {q: n for q in queues}
+        for i in order:
+            before[i], at[where[i]] = at[where[i]], i
+        own = [ops[i]["cost"][where[i]] for i in range(n)]
+        for (wake, fc, fp, fl), edge in zip(VARIANTS, edges):
+            end = [0.0] * (n + 1)
             for i in order:
-                q = where[i]
-                t, k = free.get(q, 0.0), (last.get(q), True)
-                for j, soft in pre[i]:
-                    x = end[j] if soft else done[j] + wake
-                    if x >= t:
-                        t, k = x, (j, False)
-                end[i] = free[q] = t + ops[i]["cost"][q] * (fp if q == "p" else fc)
-                done[i], last[q], by[i] = end[i] + ops[i]["lat"] * fl, i, k
-            i = max(range(n), key=lambda k: done[k])
-            tot += done[i] + EARLY * sum(end[k] for k in sends)
-            seen = set()
-            for i in [i] + sends:
-                while i is not None and i not in seen:
-                    seen.add(i)
-                    if by[i][1] and by[i][0] is not None:
-                        held.append((i, by[i][0]))
-                    i = by[i][0]
+                t = end[before[i]]
+                for j, d in edge[i]:
+                    if end[j] + d > t:
+                        t = end[j] + d
+                end[i] = t + own[i] * (fp if where[i][0] == "p" else fc)
+            i = max(last, key=lambda k: end[k] + ops[k]["lat"] * fl)
+            tot += end[i] + ops[i]["lat"] * fl + EARLY * sum(end[k] for k in sends)
+            while i < n:
+                x, j = max([(end[j] + d, j) for j, d in edge[i]] + [(-1.0, n)])
+                if end[before[i]] > x:
+                    j = before[i]
+                    if j < n:
+                        held.append((i, j))
+                i = j
         return tot, held
 
-    sends = [i for i in range(n) if ops[i]["tag"] in ("sk", "sc")]
+    sends = [i for i in range(n) if ops[i]["tag"] in ("sk", "sc", "dy") or ops[i]["out"] in MARKS]
     last = [i for i in range(n) if not after[i]]
 
     def rough(start):
@@ -172,25 +201,25 @@ def plan(ops):
     same = {}
     for i in range(n):
         same.setdefault(ops[i]["kind"], []).append(i)
-    rng = np.random.default_rng(0)
-    label = {j: (k, x) for k in same for x, j in enumerate(same[k])}
-    best = None
-    for found in ({}, SHIFT):
-        trial = [way[i] + found.get(label[i], (0.0, SPARE))[0] for i in range(n)]
-        lean = [found.get(label[i], (0.0, SPARE))[1] for i in range(n)]
-        o2, w2, s2 = place(trial, lean)
-        x, h2 = length(o2, w2)
-        if best is None or x < best:
-            best, held, prio, spare, order, where, start = x, h2, trial, lean, o2, w2, s2
+    rng = np.random.default_rng(SEED)
+    label, seen = [], {}
+    for i in range(n):
+        k = (ops[i]["kind"], int(list(ops[i]["cost"])[0][1:]))
+        seen[k] = seen.get(k, 0) + 1
+        label.append((found[k[1]], (k[0], seen[k])))
+    prio = [way[i] + f.get(k, (0.0, SPARE))[0] for i, (f, k) in enumerate(label)]
+    spare = [f.get(k, (0.0, SPARE))[1] for f, k in label]
+    order, where, start = place(prio, spare)
+    best, held = length(order, where)
     for it in range(TRIES):
         trial, lean = list(prio), spare
         if it % 50 < 2:
-            trial = place(start, spare, True)
+            trial = [x + AHEAD.get(o["out"], 0.0) * (it % 100 < 2) for x, o in zip(place(start, spare, True), ops)]
         elif it % 8 == 4:
             free = [k for pair in held for k in pair if len(ops[k]["cost"]) > 1] or [0]
             i, lean = free[int(rng.integers(len(free)))], list(spare)
             for j in same[ops[i]["kind"]] if it < TRIES * ALIKE else [i]:
-                lean[j] = 1000.0 if where[i] == "v" else -1000.0
+                lean[j] = 1000.0 if where[i][0] == "v" else -1000.0
         elif it % 4 == 2:
             i, d = int(rng.integers(n)), float(rng.normal(0.0, 2 * SHAKE))
             cone, todo = {i}, [i]
@@ -224,16 +253,15 @@ def plan(ops):
         x, h2 = length(o2, w2)
         if x <= best:
             best, held, prio, spare, order, where, start = x, h2, trial, lean, o2, w2, s2
-    SHIFT.update({label[i]: (prio[i] - way[i], spare[i]) for i in range(n)})
-    return [(i, where[i]) for i in order]
+    found[0]["best"] = (best, rough(start), max(start))
+    for i, (f, k) in enumerate(label):
+        f[k] = (prio[i] - way[i], spare[i])
+    return [[(i - base[r], where[i][0]) for i in order if where[i][1:] == str(r)] for r in range(len(ranks))]
 
 
-def rank_program(g, core, T, topo):
-    r = T.rank_of(core)
-    if r is None:
-        return
-    eng = {"v": g.vector, "s": g.scalar, "p": g.tensor, "g": g, "y": g.sync}
-    ops, touched, last_g = [], {}, []
+def calls(r, T, topo):
+    core = T.cores[r]
+    ops, touched, last_g, stage, seen = [], {}, [], ["set-up"], {}
 
     def X(a):
         if not isinstance(a, tuple):
@@ -245,7 +273,7 @@ def rank_program(g, core, T, topo):
             t = t.indirect(X(a[6]))
         return t
 
-    def emit(fns, cost, outs, ins, sem=None, inc=1, chain=True, lat=0.0, soft=(), tag=None):
+    def emit(fns, cost, outs, ins, sem=None, inc=1, chain=True, lat=0.0, soft=(), tag=None, senders=()):
         rd = [a for a in ins if isinstance(a, tuple)]
         rd += [a[6] for a in rd if a[6] is not None]
         i, hard = len(ops), set()
@@ -261,10 +289,12 @@ def rank_program(g, core, T, topo):
                 hard.add(last_g[-1])
             soft |= set(last_g[-1:])
             last_g.append(i)
-        ops.append({"fns": fns, "cost": cost, "hard": hard, "deps": hard | soft,
+        kind = (stage[0],) + tuple(a[0].rstrip("012s") for a in list(outs[:1]) + rd[:1])
+        seen[kind] = seen.get(kind, 0) + 1
+        ops.append({"from": senders, "kind": kind + (seen[kind],), "fns": fns, "cost": cost, "hard": hard, "deps": hard | soft,
                     "order": set() if "x" in fns else soft - hard, "sem": sem, "inc": inc, "chain": chain,
                     "lat": lat, "tag": tag or (name(outs[0]) if outs else sem[:2]),
-                    "out": outs[0][0] if outs else None, "kind": tuple((a[0][:2],) + a[1:6] for a in list(outs[:1]) + rd[:1])})
+                    "out": outs[0][0] if outs else None})
         return i
 
     def price(out, in_, k=1.0):
@@ -348,7 +378,7 @@ def rank_program(g, core, T, topo):
 
     def pick(dst, d0, n, src, w, lst):
         cp("v", A(dst, d0, d0 + n, cast=dt.uint32), A(src, 0, w, ind=lst, cast=dt.uint32))
-        cp("s", A(dst + "s", d0, d0 + n), A(src + "s", 0, w, ind=lst))
+        cp("vs" if dst == "gq" else "s", A(dst + "s", d0, d0 + n), A(src + "s", 0, w, ind=lst))
 
     def dma(q, out, in_, sem, lat=DMA, more=()):
         emit({q: lambda e: e.dma_start(X(out), X(in_))}, {q: 60.0}, [a for a in [out] if isinstance(a, tuple)],
@@ -365,9 +395,10 @@ def rank_program(g, core, T, topo):
             trs.append(RemoteDMATransfer(dst_ids=ids, dma_engine_mask=sum(1 << x for x in es), remote_sem=T.sem[rsem],
                                          srcs=[X(src)], dsts=[X(dst) for k in ranks]))
             tot += len(es)
-        i = emit({"g": lambda e: e.remote_dma_fused(trs, local_sem=T.sem[lsem])}, {"g": 300.0}, [],
-                 [m_[0] for m_ in moves], lsem, tot, False, hop)
-        emit({"x": None}, {"x": 0.0}, lands, [], rsem, inc, False, 0.0, [i])
+        emit({"g": lambda e: e.remote_dma_fused(trs, local_sem=T.sem[lsem])}, {"g": 300.0}, [],
+             [m_[0] for m_ in moves], lsem, tot, False, hop)
+        emit({"x": None}, {"x": 0.0}, lands, [], rsem, inc, False,
+             senders=[(k, lsem) for m_ in moves for k in m_[2]])
 
     def share(k):
         return len(topo.engines(T.cores[k], core)) // (2 if 0 < k < N - 1 else 1)
@@ -405,7 +436,7 @@ def rank_program(g, core, T, topo):
     iota(A("w0"), [[1, 8], [128, 3]])
     iota(A("io1"), [[1, 128]])
     iota(A("wb", 0, 8), [[16, 2], [2, 4]])
-    iota(A("t3"), [[0, 12], [1, 10], [0, 3]], -6)
+    iota(A("t3"), [[0, 11], [1, 10], [0, 3]], -6)
     for a in range(4):
         c_ = [-32 * blk[d] for d in (a, (a + 2) % 4)]
         iota(A("thp", 0, 2, 1, 32 * a, 32 * a + 32), [[c_[1] - c_[0], 2]], c_[0], 0)
@@ -443,7 +474,10 @@ def rank_program(g, core, T, topo):
         quant("eq", 128 * b, 128 * b + 128, "eb", 3 - b)
     aff(vs, kc("fin"), Q7, 16.0, QH)
     ts(A("lf"), A("io1", 0, 16, 2), kc("fin"), ALU.add)
-    aff(vs, A("t3", 330, 360, 3), A("t3", 330, 360, 3), 1.0, 3.5)
+    aff(vs, A("q1", 3, 28, 4), A("io1", 0, 7), 1.0, -0.5)
+    fill(A("q0"), 1.0)
+    fill(A("q0", 0, 28, 4), 0.0)
+    fill(A("v3", 0, 330, 3), 0.0)
     fill(A("sp"), 0.0)
     fill(A("mv"), 0.0)
     fill(A("sp", 0, 64, 4), 1.0)
@@ -463,9 +497,9 @@ def rank_program(g, core, T, topo):
     cp("v", A("l48", 0, 3), A("w3", 0, 3))
     ts(A("l48", 6, 9), A("w3", 0, 3), float(S), ALU.add)
     ts(kc("ns"), kc("be"), SLOT, ALU.subtract, -0.5, ALU.add)
-    aff(vs, kc("at"), kc("g7"), -1.0, 2.0)
-    ts(kc("at"), kc("ns"), 0.5, ALU.add, kc("at"), ALU.mult)
+    aff(vs, kc("at"), kc("ns"), 1.0, 0.5)
     aff(vs, kc("w2"), SLOT, -1.0, 8.0)
+    aff(vs, kc("-w2"), SLOT, 1.0, -8.0)
     aff(vs, kc("sb"), SLOT, 48.0, 24.0)
     aff(vs, kc("sb"), ODD, 2.0 * PW, kc("sb"))
     cp(vs, A("lb", 2, 144, 3), A("io1", 0, 48))
@@ -485,27 +519,27 @@ def rank_program(g, core, T, topo):
     for d in range(2):
         ts(A("kt", d, 256, 2), A("kw"), col("thp", d), ALU.is_gt, -2.0 ** -24, ALU.mult)
     aff(vs, A("kt"), A("kt"), 1.0, 1.0)
-    for i in (2, 4, 6):
+    for i in (1, 3, 5):
         ts(kc("g%d" % i), Q7, float(i), ALU.is_ge)
-    ts(kc("c0"), kc("g4"), kc("g6"), ALU.add, QH, ALU.add)
-    ts(kc("isn"), kc("g2"), kc("g6"), ALU.subtract)
-    ts(kc("x"), Q7, kc("g4"), ALU.subtract, 1.0, ALU.max)
-    ts(kc("x"), kc("x"), 5.0, ALU.min, QH, ALU.add)
-    aff(vs, kc("x"), kc("x"), 8.0, -9.0)
-    aff(vs, kc("c1"), kc("isn"), 32.0, kc("c0"))
-    ts(A("lw", 0, 8), A("wb", 0, 8), kc("c1"), ALU.add)
-    ts(A("lw", 8, 16), A("wb", 0, 8), QH, ALU.add, 1.0, ALU.add)
-    ts(A("wb", 8, 12), A("io1", 0, 64, 16), kc("x"), ALU.add, 7.0, ALU.max)
-    ts(A("lw", 16, 20), A("wb", 8, 12), 79.0, ALU.min)
+    ts(kc("l7"), Q7, 7.0, ALU.is_lt)
+    ts(kc("c0"), kc("g3"), kc("g5"), ALU.add, QH, ALU.add)
+    ts(kc("isn"), kc("g1"), kc("g5"), ALU.subtract, 32.0, ALU.mult)
+    ts(kc("x"), Q7, kc("g3"), ALU.subtract, 4.0, ALU.min)
+    ts(kc("x"), kc("x"), QH, ALU.add, 8.0, ALU.mult)
+    aff(vs, kc("c0"), kc("c0"), 1.0, kc("isn"))
+    ts(A("lw", 0, 8), A("wb", 0, 8), kc("c0"), ALU.add, kc("l7"), ALU.mult)
+    ts(A("wb", 8, 12), A("io1", 0, 64, 16), kc("x"), ALU.add, 8.0, ALU.max)
+    ts(A("lw", 16, 20), A("wb", 8, 12), 80.0, ALU.min, -1.0, ALU.add)
     fill(A("ee"), BIG)
     fill(A("c8"), 0.0)
-    fill(A("c8", 0, 64, 8), BIG)
+    fill(A("c8", 0, 128, 8), BIG)
     fill(A("c3"), 1.0)
-    fill(A("c3", 0, 144, 3), 0.0)
+    fill(A("c3", 0, 84, 3), 0.0)
     fill(A("tau", 90, 126), 0.0)
     fill(A("flo"), FLOOR)
     cp(vs, A("cmp", 256, 288), A("zer", 0, 32))
-    ts(kc("up"), P, 64.0, ALU.is_ge)
+    ts(kc("up"), P, 32.0, ALU.is_ge)
+    fill(A("fd", 0, 128, 1, 64, 128), 0.0)
     far = N * C if upper else 0
     aff(vs, kc("ta"), kc("up"), -1024.0, 512.0)
     aff(vs, kc("tb"), kc("up"), 128.0 - 0.875, 0.875)
@@ -552,14 +586,9 @@ def rank_program(g, core, T, topo):
         scan(A("mo", 8 * do + 11, 8 * (do + w) + 8, 4), A("mz", 2 * o + 2, 2 * (o + w) + 2),
              A("te", 2 * o + 2, 2 * (o + w) + 2), 0.0, ALU.min, ALU.max)
 
-    def weights(o, w, c_, e_):
-        cp(vs, A("we", o, o + w), e_)
-        tt(A("ww", o, o + w), c_, A("we", o, o + w), ALU.max)
-
-    def twice(o, do, wo, running=False):
+    def twice(o, do, wo):
         tt(A("wm", wo, wo + 64), A("mo", 8 * o, 8 * o + 80, ind=A("lw", 16, 20)), A("ww", wo, wo + 64), ALU.max)
-        scan(A("mo", 8 * do + 8, 8 * do + 72), A("zer", 0, 64) if running else A("c8"), A("wm", wo, wo + 64), BIG,
-             ALU.max, ALU.min)
+        scan(A("mo", 8 * do + 8, 8 * do + 72), A("c8", wo, wo + 64), A("wm", wo, wo + 64), 0.0, ALU.max, ALU.min)
 
     def back(o, w):
         tt(third("t3", 1, o, w), nb(o - 2, w), mo(o, w), ALU.is_le)
@@ -567,11 +596,19 @@ def rank_program(g, core, T, topo):
         scan(A("tau", 3 * o, 3 * (o + w)), A("c3", 0, 3 * w), A("t3", 3 * o, 3 * (o + w)), 0.0, ALU.mult, ALU.add)
 
     def back2(o, w):
-        tt(A("dd", o, o + w + 1), third("tau", 2, o, w + 1), third("tau", 2, o - 1, w + 1), ALU.subtract)
-        cp(vs, third("u3", 0, o, w), third("tau", 2, o - 1, w))
-        tt(third("u3", 1, o, w), A("dd", o, o + w), third("t3", 1, o - 20, w), ALU.mult)
-        tt(third("u3", 2, o, w), A("dd", o + 1, o + w + 1), third("t3", 2, o - 20, w), ALU.mult)
-        scan(A("tau2", 3 * o, 3 * (o + w)), A("c3", 0, 3 * w), A("u3", 3 * o, 3 * (o + w)), 0.0, ALU.mult, ALU.add)
+        for k in range(2):
+            cp(vs, third("v3", 2 - k, o, w), third("t3", 1 + k, o - 20, w))
+            tt(third("u3", 1 - k, o, w), third("tau", 2, o + k, w), third("tau", 2, o + k - 1, w), ALU.subtract)
+        cp(vs, third("u3", 2, o, w), third("tau", 2, o - 1, w))
+        scan(A("tau2", 3 * o, 3 * (o + w)), A("v3", 3 * o, 3 * (o + w)), A("u3", 3 * o, 3 * (o + w)), 0.0, ALU.mult,
+             ALU.add)
+
+    def back_last(o):
+        tt(A("q1", 0, 28, 4), mo(o - 1, 7), mo(o + 1, 7), ALU.is_le)
+        tt(A("q1", 1, 28, 4), mo(o - 2, 7), mo(o, 7), ALU.is_gt)
+        tt(A("q1", 2, 28, 4), mo(o - 2, 7), mo(o, 7), ALU.is_le)
+        tt(A("q0", 2, 28, 4), mo(o - 1, 7), mo(o, 7), ALU.is_le)
+        scan(A("q2"), A("q0"), A("q1"), 0.0, ALU.mult, ALU.add)
 
     def borders(buf, w, lo_, hi_, to_left, to_right, cast):
         mv_, lands = [], []
@@ -592,28 +629,33 @@ def rank_program(g, core, T, topo):
             remote(m1, "%s%d" % (rs, t), "%s%d" % (ls_, t), l1, sum(share(k) for k in nbs), HOP + (0 if t else FIRST))
 
     both = len(nbs) == 2
-    rot = 17 if both else 16
-    pieces = (((0, 16), (16, 48)), ((6, 24), (24, 48), (0, 6)), ((10, 28), (28, 48), (0, 10)),
-              ((16, 32), (32, 48), (0, 16)))[r]
+    rot = (16, 12, 8, 16)[r]
+    pieces = ((0, 20), (20, 34), (34, 48)) if both else ((0, 16), (16, 32), (32, 48)) if r == 0 else (
+        (16, 32), (32, 48), (0, 16))
+    if both and not DM:
+        rot, pieces = 17, (((6, 24), (24, 48), (0, 6)), ((10, 28), (28, 48), (0, 10)))[r - 1]
     if both:
-        quant("bq", 48 * (2 - r), 48 * (2 - r) + 128, "zer", 0)
+        quant("bq", 64 * (2 - r), 64 * (2 - r) + 128, "zer", 0)
 
     for b in range(4):
-        mm(b, "eq", 128 * b, "tn", 0, 384)
-        cp(vs, A("ft", b, 4 * S, 4), ps(b, 0, 384, 8))
+        mm(b, "eq", 128 * b, "tq", T0, 128)
+        cp(vs, A("ft", b, 4 * S, 4), ps(b, 0, S))
     quant("fq", 0, 128, "ft", 0)
     firsts(0, "fq", 0)
 
     for t in range(R):
         zq, cl = "zq%d" % t, "cl%d" % t
+        stage[0] = "round"
+        seen.clear()
         for l in range(L - 1, -1, -1):
             mm(l, "tq", T0 + 48 * l - sh, "uq", 0, 128)
         score(mo(1, 8), 0, kc("eb"))
         score(mo(11, 8), 7)
         for o, gr in ((0, 1), (1, 6), (2, 2), (3, 5), (4, 3), (5, 4), (6, 4), (10, 6)):
             score(odd("te", 10 * o + 1, 8), gr)
-        for o, gr in enumerate((5, 7, 4, 6)):
-            score(A("ee", 16 * o + 1, 16 * o + 9), gr)
+        for o in range(2):
+            score(A("ee", 16 * o + 1, 16 * o + 9), 4 + 2 * o)
+            score(A("c8", 64 * o + 7, 64 * o + 64, 8), 5 + 2 * o)
         for b in range(4):
             mm(b, "eq", 128 * b, "tq", T0, 384)
         for b in range(4):
@@ -629,22 +671,24 @@ def rank_program(g, core, T, topo):
         cost = [col(cl, 32 * k + 31) for k in range(N)]
         remote([(cost[r], cost[r], others)], "ak%d" % t, "sk%d" % t, [cost[k] for k in others],
                sum(len(topo.engines(T.cores[k], core)) for k in others), HOP + 300)
-        tt(A("ee", 64, 89), A("ee", 32, 57), A("ee", 33, 58), ALU.min)
-        weights(0, 128, A("ee", 32, 96, ind=A("lw", 0, 8)), A("ee", 0, 32, ind=A("lw", 8, 16)))
+        tt(A("ee", 32, 57), A("ee", 0, 25), A("ee", 1, 26), ALU.min)
+        cp(vs, A("ww"), A("ee", ind=A("lw", 0, 8)))
         twice(60, 100, 0)
-        twice(100, 120, 64, True)
+        twice(100, 120, 64)
+        scan(A("mc"), mo(121, 8), mo(121, 8), BIG, ALU.min, ALU.min)
         level(60, 80, 8)
         level(100, 110, 8)
-        for o in (80, 110):
-            tt(nb(o, 9), mo(o, 9), mo(o + 1, 9), ALU.min)
-        for o, w in ((2, 28), (42, 28), (82, 28), (112, 7)):
+        tt(nb(80, 9), mo(80, 9), mo(81, 9), ALU.min)
+        for o, w in ((2, 28), (42, 28), (82, 28)):
             back(o, w)
+        back_last(112)
         for o, w in ((22, 47), (102, 7)):
             back2(o, w)
-        act(A("dump", 56, 64), mo(121, 8), ACT.Sign, bias=mo(128, 1), scale=-1.0, accum=col("acc", 7))
+        act(A("dump", 56, 64), A("mc"), ACT.Sign, bias=col("mc", 7), scale=-1.0, accum=col("acc", 7))
         for gr, to in ((7, 6), (6, 4), (6, 5), (4, 2), (4, 3), (2, 0), (2, 1)):
             o = [2, 22, 42, 62, 82, 102, 112][gr - 1]
-            act(A("dump", 8 * to, 8 * to + 7), third("tau2" if gr - to == 2 else "tau", 2, o, 7), ACT.Sign,
+            act(A("dump", 8 * to, 8 * to + 7),
+                A("q2", 3, 28, 4) if gr == 7 else third("tau2" if gr - to == 2 else "tau", 2, o, 7), ACT.Sign,
                 bias=col("acc", gr), scale=1.0 if gr == 7 else 2.0, accum=col("acc", to))
         for gr in range(7, -1, -1):
             aff(vs, A("st", 64 * gr, 64 * gr + 64), A("sp"), col("acc", gr), 0.0)
@@ -654,7 +698,8 @@ def rank_program(g, core, T, topo):
             aff("v", col("lv", m_), ps(4, 48 + m_, 49 + m_), kc("al48"), col("w5", m_))
         mm(5, "sq", 0, "mq", 0, 128)
         act(A("oa", 0, 48), ps(5, 0, S), ACT.Sign, kc("ns"), kc("al"))
-        ts(A("oa", 48, 96), ps(4, 0, S), kc("at"), ALU.is_equal, kc("w2"), ALU.mult)
+        act(A("oa", 96, 144), ps(5, 0, S), ACT.Abs, kc("at"), kc("al"))
+        act(A("oa", 48, 96), A("oa", 96, 144), ACT.Relu, kc("w2"), kc("-w2"))
         if t == R - 1:
             aff("v", A("prow", 0, S), ps(4, 0, S), kc("al"), kc("be"))
         for b in range(4):
@@ -679,12 +724,12 @@ def rank_program(g, core, T, topo):
             aff(vs, A("inr", 64 * i, 64 * i + 64), A("kt", 64 * i, 64 * i + 64), cost[k], 0.0)
         keys = [r] + [k for k in others if (k > 0 if upper else k < N - 1)]
         for i, k in enumerate(keys):
-            aff(vs, col("key", i + 2), cost[k], col("km", k), col("key", i + 1) if i else 0.0)
+            aff(vs, col("key", i), cost[k], col("km", k), col("key", 0) if i == 1 else 0.0)
         for o, w in ((96, 32), (0, 96)):
             tr(A("row", o, o + w), A("inr", 2 * o, 2 * (o + w), 2))
             tr(A("row", 128 + o, 128 + o + w, 1, 64, 128), A("inr", 2 * o + 1, 2 * (o + w), 2, 0, 64))
             tr(A("row", 128 + o, 128 + o + w, 1, 0, 64), A("inr", 2 * o + 1, 2 * (o + w), 2, 64, 128))
-        ts(A("cmp", 0, 256), A("row"), col("key", 4), ALU.is_lt)
+        ts(A("cmp", 0, 256), A("row"), col("key", 1), ALU.subtract, col("key", 2), ALU.is_lt)
         scan(A("cnt"), A("cmp"), A("zer", 0, 288), 0.0, ALU.add, ALU.add)
         for a in range(4):
             o = 32 * blk[a] - kb
@@ -692,7 +737,7 @@ def rank_program(g, core, T, topo):
         o = S * r - kb
         for a in range(4):
             ts(A("lb", 0, 144, 3, 32 * a, 32 * a + 32), A("fone", o, o + S, 1, 0, 32), 96.0, ALU.is_ge, 48.0, ALU.mult)
-        for a in range(4):
+        for a in range(2):
             ts(A("fd", 0, 128, 1, 32 * a, 32 * a + 32), A("fone", 0, 128, 1, 0, 32), 96.0, ALU.is_ge, 0.25, ALU.mult)
         scan(A("lo_"), A("la"), A("lb"), 0.0, ALU.mult, ALU.add)
         cp("v", A("lz", 0, rot), third("lo_", 2, S - rot, rot))
@@ -700,17 +745,28 @@ def rank_program(g, core, T, topo):
         for a, b_ in pieces:
             for b in range(2):
                 cp(vs, A("zt", 32 * a + b, 32 * b_, 2), A("fb", PW * b, PW * (b + 3), ind=A("lz", a, b_)))
-        if both:
-            quant("bq", 88 - 8 * (rot - pieces[0][0]), 88 + 8 * (pieces[0][1] - rot), "zt", 32 * pieces[0][0])
-        quant(zq, Z0 + C - 8 * rot, Z0 + C, "zt", 0)
-        for a, b_ in ((0, 128), (128, 256)) if r == N - 1 else ((0, C - 8 * rot),):
-            quant(zq, Z0 + a, Z0 + b_, "zt", 32 * rot + 4 * a)
+        if both and not DM:
+            quant("bq", 96 - 8 * (rot - pieces[0][0]), 96 + 8 * (pieces[0][1] - rot), "zt", 32 * pieces[0][0])
+            quant(zq, Z0 + C - 8 * rot, Z0 + C, "zt", 0)
+            quant(zq, Z0, Z0 + C - 8 * rot, "zt", 32 * rot)
+        elif both:
+            low = 160 - 8 * rot
+            quant("bq", 96 - 8 * rot, 96 + low, "zt", 0)
+            quant(zq, Z0 + low, Z0 + C - 8 * rot, "zt", 640)
+            for nm, cast in (("", u8), ("s", None)):
+                dma("y", A(zq + nm, Z0 + C - 8 * rot, Z0 + C, cast=cast), A("bq" + nm, 96 - 8 * rot, 96, cast=cast),
+                    "dh%s%d" % (nm, t))
+                dma("y", A(zq + nm, Z0, Z0 + low, cast=cast), A("bq" + nm, 96, 96 + low, cast=cast), "dl%s%d" % (nm, t))
+        else:
+            quant(zq, Z0 + C - 8 * rot, Z0 + C, "zt", 0)
+            for a, b_ in ((0, 128), (128, 256)) if r == N - 1 else ((0, C - 8 * rot),):
+                quant(zq, Z0 + a, Z0 + b_, "zt", 32 * rot + 4 * a)
         for nm, cast, rs, ls_ in (("", u8, "ac", "sc"), ("s", None, "as", "ss")):
             if both:
-                m1, l1 = borders(("bq" + nm, zq + nm), [56, 88, 88, 56], 88, 88, Z0 + C, Z0, cast)
+                m1, l1 = borders(("bq" + nm, zq + nm), [56, 88, 88, 56], 96, 96, Z0 + C, Z0, cast)
             else:
                 m1, l1 = borders((zq + nm, zq + nm), [56, 88, 88, 56], Z0, Z0 + C, Z0 + C, Z0, cast)
-            remote(m1, "%s%d" % (rs, t), "%s%d" % (ls_, t), l1, sum(share(k) for k in nbs), HOP + 400)
+            remote(m1, "%s%d" % (rs, t), "%s%d" % (ls_, t), l1, sum(share(k) for k in nbs), HOP + (200 if nm else 450))
         e_ = 128 if upper else i0 + n
         scan(A("pos", 1, 1 + e_), A("c78", 0, e_), A("fd", 0, e_), 0.0, ALU.add, ALU.add)
         aff(vs, A("t7", 0, n), A("fd", i0, i0 + n), kc("ta"), kc("tb"))
@@ -727,8 +783,8 @@ def rank_program(g, core, T, topo):
         for m_ in range(6):
             act(A("cl", 68 * m_, 68 * m_ + n), A("th", 0, n), ACT.Relu, col(lo_, m_), kc("sc"), col("rs", m_))
         tt(A("sums", 0, 3), A("rs", 0, 3), A("rs", 3, 6), ALU.subtract)
-        for a, b in ((0, 64), (64, 0)):
-            tt(A("sums", 3, 6, 1, a, a + 64), A("rs", 0, 3, 1, b, b + 64), A("rs", 3, 6, 1, b, b + 64), ALU.subtract)
+        for a, b in ((0, 32), (32, 0)):
+            tt(A("sums", 3, 6, 1, a, a + 32), A("rs", 0, 3, 1, b, b + 32), A("rs", 3, 6, 1, b, b + 32), ALU.subtract)
         tt(A("xr"), A("sums", ind=A("ls")), A("dk", 0, 96), ALU.subtract)
         c1, c4, da, db = [A("xr", 24 * i, 24 * i + 24) for i in range(4)]
         tt(A("mm5", 0, 48, 2), da, db, ALU.subtract)
@@ -737,7 +793,8 @@ def rank_program(g, core, T, topo):
         scan(A("mm5", 96, 144), A("mm5", 48, 96), A("mm5", 0, 48), 0.0, ALU.mult, ALU.add)
         if t == R - 1:
             break
-        cp("v", A("lm"), A("mm5", 97, 144, 2))
+        for a in (0, 64):
+            cp("v", A("lm", 0, 24, 1, a, a + 64), A("mm5", 97, 144, 2, 0, 64))
         for c0, w in PARTS:
             pick("gq", c0, w, zq, ZC, A("lm", c0 // 16, (c0 + w) // 16))
         for c0, w in PARTS:
@@ -750,20 +807,22 @@ def rank_program(g, core, T, topo):
                 tt(A("xt", 4 * c0 + b, 4 * (c0 + w), 4), ps(3 - b, 0, w), A("tmp", o, o + w), ALU.add)
             quant("tq", T0 + c0, T0 + c0 + w, "xt", 4 * c0)
 
+    stage[0] = "end"
     for m_ in range(3):
         c0, c1 = 128 * m_, 128 * m_ + 128
-        cp("v", A("lm", 8 * m_, 8 * m_ + 8), A("mm5", 97 + 2 * m_, 144, 6))
+        for a in (0, 64):
+            cp("v", A("lm", 8 * m_, 8 * m_ + 8, 1, a, a + 64), A("mm5", 97 + 2 * m_, 144, 6, 0, 64))
         pick("gq", c0, 128, zq, ZC, A("lm", 8 * m_, 8 * m_ + 8))
+        cp("v", A("tl", c0, c1, cast=dt.uint32), A("gq", c0, c1, ind=A("lf"), cast=dt.uint32))
+        cp(vs, A("tls", c0, c1), A("gqs", c0, c1, ind=A("lf")))
         for b in range(4):
-            mm(7 - 2 * b, "wq", 128 * b, "gq", c0, 128)
-            mm(6 - 2 * b, "eq", 128 * b, "gq", c0, 128)
+            mm(7 - 2 * b, "wq", 128 * b, "tl", c0, 128)
+            mm(6 - 2 * b, "eq", 128 * b, "tl", c0, 128)
         for b in range(4):
             o = 384 * b + c0
             relu("s", A("tmp", o, o + 128), ps(7 - 2 * b, 0, 128), 0.015625)
             tt(A("xt", 4 * c0 + b, 4 * c1, 4), ps(6 - 2 * b, 0, 128), A("tmp", o, o + 128), ALU.add)
-        quant("tl", c0, c1, "xt", 4 * c0)
-        cp("v", A("tf", c0, c1, cast=dt.uint32), A("tl", c0, c1, ind=A("lf"), cast=dt.uint32))
-        cp("s", A("tfs", c0, c1), A("tls", c0, c1, ind=A("lf")))
+        quant("tf", c0, c1, "xt", 4 * c0)
         dma("y", T.oc[:, 4 * c0:4 * c1], A("tf", c0, c1, cast=u8), "doc")
     for m_ in range(3):
         c0, c1 = 128 * m_, 128 * m_ + 128
@@ -773,8 +832,22 @@ def rank_program(g, core, T, topo):
     for k in range(4):
         dma("sy"[k % 2], T.osc[4 * k:4 * k + 4, :], A("tfs", 0, 384, 1, 32 * k, 32 * k + 4), "dos")
 
+    return ops
+
+
+def rank_program(g, core, T, topo):
+    r = T.rank_of(core)
+    if r is None:
+        return
+    if not PLAN:
+        ranks, starts = [calls(k, T, topo) for k in range(N)], [[{} for k in range(N)] for seed in range(STARTS)]
+        for seed, found in enumerate(starts):
+            plan(ranks, ALONE, EARLY, found, SEED + seed)
+        PLAN.extend(plan(ranks, TRIES, EARLY, min(starts, key=lambda f: f[0]["best"]), SEED + STARTS))
+    eng = {"v": g.vector, "s": g.scalar, "p": g.tensor, "g": g, "y": g.sync}
+    ops = calls(r, T, topo)
     count, known, mark = {}, {q: {} for q in eng}, {}
-    for i, q in plan(ops):
+    for i, q in PLAN[r]:
         o = ops[i]
         sem = o["sem"] or COUNTER[q]
         count[sem] = count.get(sem, 0) + o["inc"]

import numpy as np
from concourse.bass import DstId, RemoteDMATransfer
from concourse.mybir import dt, AluOpType, AxisListType, ActivationFunctionType

ALU = AluOpType
ACT = ActivationFunctionType
C, S, L, R, N = 384, 48, 8, 3, 4
BIG = 1.0e29
FLOOR = 2.0 ** -100
MAGIC = 12582912.0
PW = 432
T0 = 16
Z0 = 96
B0 = 576
ZC = B0 + 3 * S
PARTS = ((256, 128), (128, 128), (0, 128))
F32, BF, I32, U16, CODE, PLANE = "float32", "bfloat16", "int32", "uint16", "float8_e4m3fn_x4", "uint8"
WIDTH = {F32: 4, BF: 2, I32: 4, U16: 2, CODE: 4, PLANE: 1}

SCRATCH = {"ps": ("psum", [128, 4096], F32)}


def _buf(dtype, **kw):
    for k, n in kw.items():
        SCRATCH[k] = ("sbuf", [128, n], dtype)


_buf(BF, xin=1536, uin=512, vin=512, xt=1536, fb=4 * PW, zt=1536, ft=512, vt=512, st=512, eb=516, mv=512, zer=512,
     cmp=288, cnt=288, fone=128, fd=128)
_buf(CODE, tn=384, tq=528, tf=384, uq=128, vq=128, wq=512, eq=512, mq=128, sq=128, vcq=128, fq=128, gq=384,
     zq0=ZC, zq1=ZC, zq2=ZC)
_buf(PLANE, tns=384, tqs=528, tfs=384, uqs=128, vqs=128, wqs=512, eqs=512, mqs=128, sqs=128, vcqs=128, fqs=128,
     gqs=384, zq0s=ZC, zq1s=ZC, zq2s=ZC)
_buf(F32, kc=64, te=244, mo=1048, mz=220, tc=24, ee=64, ww=128, wm=128, t3=330, u3=330, v3=330, tau=330,
     tau2=330, q0=28, q1=28, q2=28, c3=84, c8=128, flo=24, wb=24, mc=8, acc=8, dump=64,
     sp=64, prow=52, oa=144, la=144, lb=144, lo_=144, kt=256, kw=128, km=4, key=8, inr=256, row=256,
     c78=128, pos=132, t7=68, th=68, cl=408, rs=6, sums=8, lo=6, lu=6, dk=144, mm5=144, tmp=1536, ysb=384,
     olb=48, o8=48, io1=128, w0=24, w3=8, w4=8, w5=8, thp=4, cl0=128, cl1=128, cl2=128)
_buf(I32, pi=8, xr=96)
_buf(U16, l0=24, lf=8, lv=4, lz=48, ls=6, lm=24, l48=10, lw=20)
_buf(CODE, tl=384, bq=192)
_buf(PLANE, tls=384, bqs=192)

SEMAPHORES = ["cv", "cs", "cp", "cg", "dx", "dx2", "du", "dv", "dw", "dws", "dol", "dy", "doc", "dos"] + [
    "%s%d" % (k, t) for t in range(R) for k in ("ac", "as", "ak", "af", "ag", "sc", "ss", "sk", "sf", "sg", "dh", "dhs",
                                                "dl", "dls")]
COUNTER = {"v": "cv", "s": "cs", "p": "cp", "g": "cg"}
CY, GAT, WAKE, PE, HOP, DMA = 0.95, 1.4, 200.0, 0.6, 800.0, 1200.0
FINE = ("oa", "tq", "mo", "mz", "te", "cn", "cq", "tc", "gq", "gqs", "xt", "tmp", "ca", "cb", "tau",
        "th", "rr", "mm5", "cl", "fb", "zt")
FIRST, EARLY, ALIKE, SLACK, PLAN = 800.0, 0.03, 0.75, 60.0, []
DM, STARTS, MARKS, SEED = 1, 4, ("lm", "vcq", "tq"), 0
SPARE, ALONE, TRIES, SHAKE, SPAN = 150.0, 450, 1800, 200.0, 1500.0
AHEAD = dict([(k, 1000.0) for k in ("tc", "cl0", "cl1", "cl2")]
             + [(k, 600.0) for k in ("inr", "key", "row", "cmp", "cnt", "fone", "fd")]
             + [(k, 400.0) for k in ("pos", "t7", "th")])
VARIANTS = ((200.0, 1.0, 1.0, 1.0), (150.0, 1.15, 0.8, 0.7), (230.0, 1.2, 1.2, 1.6))


def A(name, c0=0, c1=None, step=1, p0=0, p1=128, ind=None, cast=None):
    if c1 is None:
        c1 = SCRATCH[name][1][1]
    return (name, c0, c1, step, p0, p1, ind, cast)


def col(name, c, p0=0, p1=128):
    return A(name, c, c + 1, 1, p0, p1)


def odd(buf, o, w):
    return A(buf, 2 * o + 1, 2 * (o + w), 2)


def size(a):
    return (a[2] - a[1] + a[3] - 1) // a[3]


def name(a):
    return a[0] + (str(a[1]) if a[0] in FINE else "")


def clash(a, b):
    if a[0] == "ps":
        return a[1] // 512 <= (b[2] - 1) // 512 and b[1] // 512 <= (a[2] - 1) // 512
    if a[5] <= b[4] or b[5] <= a[4] or a[2] <= b[1] or b[2] <= a[1]:
        return False
    return not (a[3] == b[3] and a[3] > 1 and (a[1] - b[1]) % a[3] != 0)


def plan(ranks, TRIES, EARLY, found, SEED):
    ops, pre, base, sent = [], [], [], {}
    for r, own in enumerate(ranks):
        base.append(len(ops))
        behind = []
        for i, o in enumerate(own):
            far = near = 0
            for j in o["hard"]:
                far |= behind[j]
                near |= 1 << j
            behind.append(far | near)
            pre.append([(base[r] + j, j in o["order"]) for j in sorted(o["deps"]) if not far >> j & 1])
            ops.append(dict(o, cost={q + str(r): c_ for q, c_ in o["cost"].items()}))
            sent[r, o["sem"]] = base[r] + i
    n = len(ops)
    for i in range(n):
        pre[i] += [(j, False) for j in sorted({sent[k % len(ranks), s_] for k, s_ in ops[i]["from"]})]
    after = [[] for o in ops]
    for i in range(n):
        for j, soft in pre[i]:
            after[j].append((i, soft))
    left, todo, way = [len(a) for a in after], [i for i in range(n) if not after[i]], [0.0] * n
    while todo:
        i = todo.pop()
        way[i] = min(ops[i]["cost"].values()) + max(
            [way[j] + (0.0 if soft else ops[i]["lat"] + WAKE) for j, soft in after[i]] + [ops[i]["lat"]])
        for j, soft in pre[i]:
            left[j] -= 1
            if not left[j]:
                todo.append(j)

    way = [way[i] + AHEAD.get(ops[i]["out"], 0.0) for i in range(n)]
    gap = [[(j, 0.0 if soft else ops[j]["lat"] + WAKE) for j, soft in pre[i]] for i in range(n)]
    pag = [[(j, 0.0 if soft else ops[i]["lat"] + WAKE) for j, soft in after[i]] + [(n, ops[i]["lat"])] for i in range(n)]

    cost = [list(o["cost"].items()) for o in ops]
    queues = {q for c_ in cost for q, x in c_}
    edges = [[[(j, 0.0 if soft else ops[j]["lat"] * fl + wake) for j, soft in pre[i]] for i in range(n)]
             for wake, fc, fp, fl in VARIANTS]

    def place(prio, spare, back=False):
        left = [len(p) for p in (after if back else pre)]
        ready = sorted((prio[i], i) for i in range(n) if not left[i])
        busy, start, end, where = {q: [] for q in queues}, [0.0] * n, [0.0] * (n + 1), [None] * n
        while ready:
            i = ready.pop()[1]
            at = 0.0
            for j, d in (pag if back else gap)[i]:
                if end[j] + d > at:
                    at = end[j] + d
            best = None
            for q, c_ in cost[i]:
                b, t = busy[q], at
                k = m_ = len(b)
                while k > 7 and b[k - 8][1] > at:
                    k -= 8
                while k and b[k - 1][1] > at:
                    k -= 1
                while k < m_ and b[k][0] < t + c_:
                    if b[k][1] > t:
                        t = b[k][1]
                    k += 1
                x = (t + c_ + (spare[i] if q[0] == "v" else 0.0), t, q, k, c_)
                if best is None or x < best:
                    best = x
            x, t, q, k, c_ = best
            busy[q].insert(k, (t, t + c_))
            start[i], end[i], where[i] = t, t + c_, q
            for j, soft in (pre if back else after)[i]:
                left[j] -= 1
                if not left[j]:
                    k, m_, x = 0, len(ready), prio[j]
                    while k < m_:
                        if ready[(k + m_) >> 1][0] > x:
                            m_ = (k + m_) >> 1
                        else:
                            k = ((k + m_) >> 1) + 1
                    ready.insert(k, (x, j))
        return end[:n] if back else (sorted(range(n), key=lambda k: (start[k], k)), where, start)

    def length(order, where):
        tot, held = 0.0, []
        before, at = [n] * n, {q: n for q in queues}
        for i in order:
            before[i], at[where[i]] = at[where[i]], i
        own = [ops[i]["cost"][where[i]] for i in range(n)]
        for (wake, fc, fp, fl), edge in zip(VARIANTS, edges):
            end = [0.0] * (n + 1)
            for i in order:
                t = end[before[i]]
                for j, d in edge[i]:
                    if end[j] + d > t:
                        t = end[j] + d
                end[i] = t + own[i] * (fp if where[i][0] == "p" else fc)
            i = max(last, key=lambda k: end[k] + ops[k]["lat"] * fl)
            tot += end[i] + ops[i]["lat"] * fl + EARLY * sum(end[k] for k in sends)
            while i < n:
                x, j = max([(end[j] + d, j) for j, d in edge[i]] + [(-1.0, n)])
                if end[before[i]] > x:
                    j = before[i]
                    if j < n:
                        held.append((i, j))
                i = j
        return tot, held

    sends = [i for i in range(n) if ops[i]["tag"] in ("sk", "sc", "dy") or ops[i]["out"] in MARKS]
    last = [i for i in range(n) if not after[i]]

    def rough(start):
        return max(start[i] + ops[i]["lat"] for i in last) + EARLY * sum(start[k] for k in sends)

    same = {}
    for i in range(n):
        same.setdefault(ops[i]["kind"], []).append(i)
    rng = np.random.default_rng(SEED)
    label, seen = [], {}
    for i in range(n):
        k = (ops[i]["kind"], int(list(ops[i]["cost"])[0][1:]))
        seen[k] = seen.get(k, 0) + 1
        label.append((found[k[1]], (k[0], seen[k])))
    prio = [way[i] + f.get(k, (0.0, SPARE))[0] for i, (f, k) in enumerate(label)]
    spare = [f.get(k, (0.0, SPARE))[1] for f, k in label]
    order, where, start = place(prio, spare)
    best, held = length(order, where)
    for it in range(TRIES):
        trial, lean = list(prio), spare
        if it % 50 < 2:
            trial = [x + AHEAD.get(o["out"], 0.0) * (it % 100 < 2) for x, o in zip(place(start, spare, True), ops)]
        elif it % 8 == 4:
            free = [k for pair in held for k in pair if len(ops[k]["cost"]) > 1] or [0]
            i, lean = free[int(rng.integers(len(free)))], list(spare)
            for j in same[ops[i]["kind"]] if it < TRIES * ALIKE else [i]:
                lean[j] = 1000.0 if where[i][0] == "v" else -1000.0
        elif it % 4 == 2:
            i, d = int(rng.integers(n)), float(rng.normal(0.0, 2 * SHAKE))
            cone, todo = {i}, [i]
            while todo:
                for j, soft in (pre if d > 0 else after)[todo.pop()]:
                    if j not in cone and abs(start[j] - start[i]) < SPAN / 2:
                        cone.add(j)
                        todo.append(j)
            for j in cone:
                trial[j] += d
        elif it % 4 == 0 or not held:
            at, z = rng.random() * max(start), rng.normal(0.0, SHAKE, n)
            for i in range(n):
                if abs(start[i] - at) < SPAN:
                    trial[i] += float(z[i])
        else:
            i, j = held[int(rng.integers(len(held)))]
            d = max(prio[j] - prio[i], 0.0) + rng.random() * 2 * SHAKE
            if it % 4 == 1:
                trial[j] -= d
            else:
                for k in [i] + [k for k, soft in pre[i]]:
                    trial[k] += d
        if it % 50 >= 2 and it < TRIES * ALIKE:
            for i in [i for i in range(n) if trial[i] != prio[i]]:
                for j in same[ops[i]["kind"]]:
                    trial[j] = prio[j] + trial[i] - prio[i]
        o2, w2, s2 = place(trial, lean)
        if rough(s2) > rough(start) + SLACK:
            continue
        x, h2 = length(o2, w2)
        if x <= best:
            best, held, prio, spare, order, where, start = x, h2, trial, lean, o2, w2, s2
    found[0]["best"] = (best, rough(start), max(start))
    for i, (f, k) in enumerate(label):
        f[k] = (prio[i] - way[i], spare[i])
    return [[(i - base[r], where[i][0]) for i in order if where[i][1:] == str(r)] for r in range(len(ranks))]


def calls(r, T, topo):
    core = T.cores[r]
    ops, touched, last_g, stage, seen = [], {}, [], ["set-up"], {}

    def X(a):
        if not isinstance(a, tuple):
            return a
        t = T[a[0]][a[4]:a[5], a[1]:a[2]:a[3]] if a[3] > 1 else T[a[0]][a[4]:a[5], a[1]:a[2]]
        if a[7] is not None:
            t = t.bitcast(a[7])
        if a[6] is not None:
            t = t.indirect(X(a[6]))
        return t

    def emit(fns, cost, outs, ins, sem=None, inc=1, chain=True, lat=0.0, soft=(), tag=None, senders=()):
        rd = [a for a in ins if isinstance(a, tuple)]
        rd += [a[6] for a in rd if a[6] is not None]
        i, hard = len(ops), set()
        for a, w in [(a, True) for a in outs] + [(a, False) for a in rd]:
            for j, b, wb in touched.get(a[0], []):
                if (w or wb or (a[0] == "ps" and (len(fns) > 1 or ops[j]["cost"].keys() != cost.keys()))) and clash(a, b):
                    hard.add(j)
        for a, w in [(a, True) for a in outs] + [(a, False) for a in rd]:
            touched.setdefault(a[0], []).append((i, a, w))
        soft = set(soft)
        if "g" in fns:
            if last_g and ops[last_g[-1]]["sem"] is None:
                hard.add(last_g[-1])
            soft |= set(last_g[-1:])
            last_g.append(i)
        kind = (stage[0],) + tuple(a[0].rstrip("012s") for a in list(outs[:1]) + rd[:1])
        seen[kind] = seen.get(kind, 0) + 1
        ops.append({"from": senders, "kind": kind + (seen[kind],), "fns": fns, "cost": cost, "hard": hard, "deps": hard | soft,
                    "order": set() if "x" in fns else soft - hard, "sem": sem, "inc": inc, "chain": chain,
                    "lat": lat, "tag": tag or (name(outs[0]) if outs else sem[:2]),
                    "out": outs[0][0] if outs else None})
        return i

    def price(out, in_, k=1.0):
        if in_[6] is not None:
            return 55.0 + GAT * size(out)
        if k == 1.0 and WIDTH[SCRATCH[out[0]][2]] == 2 and WIDTH[SCRATCH[in_[0]][2]] == 2:
            k = 0.5
        return CY * max(64.0, k * size(in_))

    def vec(fn, outs, ins, k=1.0):
        emit({"v": fn}, {"v": price(outs[0], ins[0], k)}, outs, ins)

    def either(q, fv, fs, out, ins):
        tag = name(out) + '<' + ins[0][0] + ('i' if ins[0][6] else '')
        cv, cs = price(out, ins[0]), max(price(out, ins[0]), CY * size(out))
        fns, cost = {"v": fv, "s": fs}, {"v": cv, "s": cs}
        emit({k: fns[k] for k in q}, {k: cost[k] for k in q}, [out], ins, tag=tag)

    def ts(out, in0, s1, op0, s2=None, op1=None):
        if op1 is None:
            vec(lambda e: e.tensor_scalar(X(out), X(in0), X(s1), None, op0), [out], [in0, s1])
        else:
            vec(lambda e: e.tensor_scalar(X(out), X(in0), X(s1), X(s2), op0, op1), [out], [in0, s1, s2])

    def tt(out, a, b, op):
        vec(lambda e: e.tensor_tensor(X(out), X(a), X(b), op), [out], [a, b], 1.0 if a[0] == "ps" else 2.0)

    def act(out, in_, func, bias=0.0, scale=1.0, accum=None):
        c_ = {"s": CY * max(64.0, size(in_)) + (20.0 if accum else 0.0)}
        if accum is None:
            emit({"s": lambda e: e.activation(X(out), X(in_), func, bias=X(bias), scale=X(scale))}, c_, [out],
                 [in_, bias, scale])
        else:
            emit({"s": lambda e: e.activation(X(out), X(in_), func, bias=X(bias), scale=X(scale), accum_out=X(accum))},
                 c_, [out, accum], [in_, bias, scale])

    def cp(q, out, in_):
        either(q, lambda e: e.tensor_copy(X(out), X(in_)), lambda e: e.activation(X(out), X(in_), ACT.Copy), out, [in_])

    def aff(q, out, in_, mul, add):
        either(q, lambda e: e.tensor_scalar(X(out), X(in_), X(mul), X(add), ALU.mult, ALU.add),
               lambda e: e.activation(X(out), X(in_), ACT.Identity, bias=X(add), scale=X(mul)), out, [in_, mul, add])

    def relu(q, out, in_, k):
        either(q, lambda e: e.tensor_scalar(X(out), X(in_), 0.0, k, ALU.max, ALU.mult),
               lambda e: e.activation(X(out), X(in_), ACT.Relu, scale=k), out, [in_])

    def fill(out, v):
        if out[0] == "zer" or size(out) > 256:
            emit({"v": lambda e: e.memset(X(out), v)}, {"v": price(out, out)}, [out], [])
            return
        z = A("zer", 0, size(out), 1, out[4], out[5])
        emit({"v": lambda e: e.memset(X(out), v), "s": lambda e: e.activation(X(out), X(z), ACT.Copy, bias=v)},
             {"v": price(out, out), "s": CY * max(64.0, size(out))}, [out], [z])

    def tr(out, in_):
        vec(lambda e: e.transpose(X(out), X(in_)), [out], [in_])

    def scan(out, d0, d1, init, op0, op1):
        vec(lambda e: e.tensor_tensor_scan(X(out), X(d0), X(d1), X(init), op0, op1), [out], [d0, d1, init])

    def red(out, in_, op):
        vec(lambda e: e.tensor_reduce(X(out), X(in_), AxisListType.X, op), [out], [in_])

    def iota(out, pat, base=0, cm=0):
        c_ = {"g": 130.0 + 2 * CY * size(out)}
        if SCRATCH[out[0]][2] == I32:
            emit({"g": lambda e: e.iota(X(out), pat, base, cm)}, c_, [out], [])
        else:
            emit({"g": lambda e: e.iota(X(out), pat, base, cm, allow_small_or_imprecise_dtypes=True)}, c_, [out], [])

    def quant(name_, c0, c1, src, e0):
        o, s_, i_ = A(name_, c0, c1), A(name_ + "s", c0, c1), A(src, e0, e0 + 4 * (c1 - c0))
        emit({"v": lambda e: e.quantize_mx(X(o), X(s_), X(i_))}, {"v": 14.0 + 0.25 * size(i_)}, [o, s_], [i_])

    def mm(bank, w, w0, x, x0, n, soft=()):
        o = A("ps", 512 * bank, 512 * bank + n)
        a, a_, b, b_ = A(w, w0, w0 + 128), A(w + "s", w0, w0 + 128), A(x, x0, x0 + n), A(x + "s", x0, x0 + n)
        return emit({"p": lambda e: e.matmul_mx(X(o), X(a), X(a_), X(b), X(b_), True, True)}, {"p": PE * (n + 16)},
                    [o], [a, a_, b, b_], soft=soft, tag=w + x[:2])

    def pick(dst, d0, n, src, w, lst):
        cp("v", A(dst, d0, d0 + n, cast=dt.uint32), A(src, 0, w, ind=lst, cast=dt.uint32))
        cp("vs" if dst == "gq" else "s", A(dst + "s", d0, d0 + n), A(src + "s", 0, w, ind=lst))

    def dma(q, out, in_, sem, lat=DMA, more=()):
        emit({q: lambda e: e.dma_start(X(out), X(in_))}, {q: 60.0}, [a for a in [out] if isinstance(a, tuple)],
             [in_] + list(more), sem, 16, True, lat)

    def remote(moves, rsem, lsem, lands, inc, hop=HOP):
        n_ = len(moves)
        trs, tot = [], 0
        for i, (src, dst, ranks) in enumerate(moves):
            es = [x for x in topo.engines(core, T.cores[ranks[0]])
                  if all(x in topo.engines(core, T.cores[k]) for k in ranks)]
            es = es[i::n_]
            ids = [DstId(rid=topo.addr(T.cores[k])[0], pnc=topo.addr(T.cores[k])[1]) for k in ranks]
            trs.append(RemoteDMATransfer(dst_ids=ids, dma_engine_mask=sum(1 << x for x in es), remote_sem=T.sem[rsem],
                                         srcs=[X(src)], dsts=[X(dst) for k in ranks]))
            tot += len(es)
        emit({"g": lambda e: e.remote_dma_fused(trs, local_sem=T.sem[lsem])}, {"g": 300.0}, [],
             [m_[0] for m_ in moves], lsem, tot, False, hop)
        emit({"x": None}, {"x": 0.0}, lands, [], rsem, inc, False,
             senders=[(k, lsem) for m_ in moves for k in m_[2]])

    def share(k):
        return len(topo.engines(T.cores[k], core)) // (2 if 0 < k < N - 1 else 1)

    def ps(bank, c0, c1, step=1):
        return A("ps", 512 * bank + c0, 512 * bank + c1, step)

    sent = [6, 12, 12, 6]
    uL, uR = [0, 6, 11, 6][r + 0], [7, 11, 6, 0][r]
    uL = [0, 6, 11, 7][r]
    n, w0 = uL + S + uR, S * r - uL
    upper = r >= N // 2
    kb = 64 if upper else 0
    blk = [2, 3, 5, 4] if upper else [0, 1, 3, 2]
    i0 = w0 - kb
    sh = 16 * (r % 2)
    nbs = [k for k in (r - 1, r + 1) if 0 <= k < N]
    others = [k for k in range(N) if k != r]
    u8 = dt.uint8
    vs = "vs"
    K = {}

    def kc(name_):
        if name_ not in K:
            K[name_] = len(K)
        return col("kc", K[name_])

    dma("y", A("xin", 0, 768), T.x[:, 0:768], "dx", DMA + 800.0)
    dma("s", A("xin", 768, 1536), T.x[:, 768:1536], "dx2", DMA + 1000.0)
    dma("s", A("uin"), T.u[:, :], "du", DMA + 1000.0)
    dma("y", A("wq", cast=u8), T.wc[:, :], "dw", DMA + 1200.0, [A("xin")])
    dma("y", A("wqs"), T.ws[:, :], "dws", DMA, [A("xin")])
    dma("y", A("vin"), T.v[:, :], "dv", DMA, [A("wq")])
    iota(col("pi", 0), [[0, 1]], 0, 1)
    iota(A("w0"), [[1, 8], [128, 3]])
    iota(A("io1"), [[1, 128]])
    iota(A("wb", 0, 8), [[16, 2], [2, 4]])
    iota(A("t3"), [[0, 11], [1, 10], [0, 3]], -6)
    for a in range(4):
        c_ = [-32 * blk[d] for d in (a, (a + 2) % 4)]
        iota(A("thp", 0, 2, 1, 32 * a, 32 * a + 32), [[c_[1] - c_[0], 2]], c_[0], 0)
    iota(A("dk", 24, 48), [[1, 8], [0, 3]])

    fill(A("zer"), 0.0)
    ts(col("pi", 1), col("pi", 0), 15, ALU.bitwise_and)
    ts(col("pi", 2), col("pi", 0), 4, ALU.arith_shift_right)
    ts(col("pi", 3), col("pi", 0), 7, ALU.bitwise_and)
    ts(col("pi", 4), col("pi", 0), 31, ALU.bitwise_and)
    ts(col("pi", 5), col("pi", 0), 3, ALU.arith_shift_right, 1, ALU.bitwise_and)
    ts(col("pi", 6), col("pi", 0), 1, ALU.bitwise_and)
    ts(col("pi", 7), col("pi", 0), 1, ALU.arith_shift_right, 7, ALU.bitwise_and)
    P, Q, G, Q7, LANE, QH, ODD, SLOT = [kc(k) for k in ("p", "q", "g", "q7", "lane", "qh", "odd", "slot")]
    cp("v", A("kc", 0, 8), A("pi", 0, 8))
    aff(vs, kc("q8"), Q, 8.0, 0.0)
    ts(A("l0"), A("w0"), kc("q8"), ALU.add)
    quant("tq", 0, 128, "zer", 0)
    quant("tq", 400, 528, "zer", 0)
    ts(kc("eb"), P, float(sh + 23.5), ALU.subtract)
    act(kc("eb"), kc("eb"), ACT.Abs)
    ts(kc("eb"), kc("eb"), 24.0, ALU.is_ge, BIG, ALU.mult)
    fill(A("mo", 7, 1048, 8), BIG)
    fill(A("te"), BIG)
    fill(A("mz"), 0.0)
    quant("uq", 0, 128, "uin", 0)
    quant("tn", 0, 192, "xin", 0)
    quant("tn", 192, 384, "xin", 768)
    for c0, w in PARTS:
        pick("tq", T0 + c0, w, "tn", 384, A("l0", c0 // 16, (c0 + w) // 16))
    quant("vq", 0, 128, "vin", 0)
    fill(A("eb"), 0.0)
    ts(A("eb", 3, 512, 4), A("io1"), P, ALU.is_equal)
    for b in range(4):
        quant("eq", 128 * b, 128 * b + 128, "eb", 3 - b)
    aff(vs, kc("fin"), Q7, 16.0, QH)
    ts(A("lf"), A("io1", 0, 16, 2), kc("fin"), ALU.add)
    aff(vs, A("q1", 3, 28, 4), A("io1", 0, 7), 1.0, -0.5)
    fill(A("q0"), 1.0)
    fill(A("q0", 0, 28, 4), 0.0)
    fill(A("v3", 0, 330, 3), 0.0)
    fill(A("sp"), 0.0)
    fill(A("mv"), 0.0)
    fill(A("sp", 0, 64, 4), 1.0)
    ts(A("sp", 1, 64, 4), A("io1", 0, 16), Q, ALU.is_equal)
    ts(A("mv", 0, 192, 4), A("io1", sh, sh + 48), P, ALU.is_equal)
    ts(A("mv", 193, 204, 4), A("io1", sh // 16, sh // 16 + 3), G, ALU.is_equal)
    quant("mq", 0, 128, "mv", 0)
    ts(kc("g7"), G, 7.0, ALU.is_equal)
    fill(A("vt", 4 * S, 512), 0.0)
    fill(A("ft", 4 * S, 512), 0.0)
    aff(vs, kc("al"), kc("g7"), -0.5, -0.5)
    aff(vs, kc("be"), kc("g7"), -3.5, 3.5)
    aff(vs, kc("al48"), kc("al"), 48.0, 0.0)
    aff(vs, kc("be48"), kc("be"), 48.0, Q)
    aff(vs, A("w3", 0, 6), A("io1", 0, 96, 16), 1.0, Q)
    aff(vs, A("w5", 0, 3), A("io1", 0, 48, 16), 1.0, kc("be48"))
    cp("v", A("l48", 0, 3), A("w3", 0, 3))
    ts(A("l48", 6, 9), A("w3", 0, 3), float(S), ALU.add)
    ts(kc("ns"), kc("be"), SLOT, ALU.subtract, -0.5, ALU.add)
    aff(vs, kc("at"), kc("ns"), 1.0, 0.5)
    aff(vs, kc("w2"), SLOT, -1.0, 8.0)
    aff(vs, kc("-w2"), SLOT, 1.0, -8.0)
    aff(vs, kc("sb"), SLOT, 48.0, 24.0)
    aff(vs, kc("sb"), ODD, 2.0 * PW, kc("sb"))
    cp(vs, A("lb", 2, 144, 3), A("io1", 0, 48))
    fill(A("la", 0, 144, 3), 0.0)
    fill(A("la", 2, 144, 3), 1.0)
    ts(kc("mid"), P, 63.5, ALU.subtract)
    act(kc("mid"), kc("mid"), ACT.Abs)
    ts(kc("mid"), kc("mid"), 32.0, ALU.is_lt)
    aff(vs, kc("h+"), kc("mid"), 32.0, LANE)
    aff(vs, kc("h-"), kc("mid"), -32.0, LANE)
    for i, k in enumerate(others + [r]):
        h, a_ = (("h+", 0), ("h-", 16), ("h-", 32), ("h+", -16))[k]
        ts(A("kw", 32 * i, 32 * i + 32), A("io1", 0, 32), kc(h), ALU.subtract, float(S * k + a_), ALU.subtract)
        ts(col("km", k), col("kw", 32 * i), LANE, ALU.add, col("thp", 0), ALU.is_equal)
        ts(col("km", k), col("kw", 32 * i), -S * (k + 1.0 - k % 2), ALU.is_le if k % 2 else ALU.is_gt, col("km", k),
           ALU.mult)
    for d in range(2):
        ts(A("kt", d, 256, 2), A("kw"), col("thp", d), ALU.is_gt, -2.0 ** -24, ALU.mult)
    aff(vs, A("kt"), A("kt"), 1.0, 1.0)
    for i in (1, 3, 5):
        ts(kc("g%d" % i), Q7, float(i), ALU.is_ge)
    ts(kc("l7"), Q7, 7.0, ALU.is_lt)
    ts(kc("c0"), kc("g3"), kc("g5"), ALU.add, QH, ALU.add)
    ts(kc("isn"), kc("g1"), kc("g5"), ALU.subtract, 32.0, ALU.mult)
    ts(kc("x"), Q7, kc("g3"), ALU.subtract, 4.0, ALU.min)
    ts(kc("x"), kc("x"), QH, ALU.add, 8.0, ALU.mult)
    aff(vs, kc("c0"), kc("c0"), 1.0, kc("isn"))
    ts(A("lw", 0, 8), A("wb", 0, 8), kc("c0"), ALU.add, kc("l7"), ALU.mult)
    ts(A("wb", 8, 12), A("io1", 0, 64, 16), kc("x"), ALU.add, 8.0, ALU.max)
    ts(A("lw", 16, 20), A("wb", 8, 12), 80.0, ALU.min, -1.0, ALU.add)
    fill(A("ee"), BIG)
    fill(A("c8"), 0.0)
    fill(A("c8", 0, 128, 8), BIG)
    fill(A("c3"), 1.0)
    fill(A("c3", 0, 84, 3), 0.0)
    fill(A("tau", 90, 126), 0.0)
    fill(A("flo"), FLOOR)
    cp(vs, A("cmp", 256, 288), A("zer", 0, 32))
    ts(kc("up"), P, 32.0, ALU.is_ge)
    fill(A("fd", 0, 128, 1, 64, 128), 0.0)
    far = N * C if upper else 0
    aff(vs, kc("ta"), kc("up"), -1024.0, 512.0)
    aff(vs, kc("tb"), kc("up"), 128.0 - 0.875, 0.875)
    aff(vs, kc("sc"), kc("up"), -1.0 / 9, 1.0)
    aff(vs, kc("-sc"), kc("sc"), -1.0, 0.0)
    aff(vs, kc("lo"), kc("up"), -0.125, float(S * r - far // 8))
    ts(A("lo", 0, 3), A("w3", 0, 3), kc("lo"), ALU.add, 1.0 if upper else kc("-sc"), ALU.mult)
    ts(A("lo", 3, 6), A("w3", 0, 3), float(S * r - far // 8 + 1), ALU.add, 1.0 if upper else kc("-sc"), ALU.mult)
    kj, kf = C * r - 8 * (S * r - Z0 // 8) + 8 * w0 - far, B0 + S - S * r + w0 + 2 * n - 1
    aff(vs, A("dk", 0, 24), A("w0"), 1.0, kc("q8"))
    aff(vs, A("dk", 48, 72), A("dk", 24, 48), 1.0 / 9, -3.0 / 9)
    aff(vs, A("dk", 72, 96), A("dk", 24, 48), 1.0 / 9, -4.0 / 9)
    aff(vs, A("dk", 96, 120), A("dk", 24, 48), 0.125, kj - 3.5 / 8)
    aff(vs, A("dk", 120, 144), A("dk", 24, 48), 1.0 / 9, kf - kj - 3.0 / 9)
    tt(A("dk", 96, 120), A("dk", 96, 120), A("dk", 0, 24), ALU.add)
    tt(A("dk", 120, 144), A("dk", 120, 144), A("dk", 0, 24), ALU.subtract)
    fill(A("mm5", 48, 96, 2), 0.0)
    aff(vs, A("w4", 0, 6), A("w3", 0, 6), 1.0 / 3, -1.0 / 3)
    ts(A("w4", 0, 6), A("w4", 0, 6), MAGIC, ALU.add, MAGIC, ALU.subtract)
    ts(A("dump", 0, 6), A("w3", 0, 6), 24.0, ALU.is_ge, kc("up"), ALU.not_equal)
    tt(A("w4", 0, 6), A("dump", 0, 6), A("w4", 0, 6), ALU.subtract)
    aff(vs, A("w4", 0, 6), A("w4", 0, 6), 3.0, 0.0)
    tt(A("w4", 0, 6), A("w4", 0, 6), A("w3", 0, 6), ALU.add)
    cp("v", A("ls"), A("w4", 0, 6))
    fill(A("c78"), 0.875)
    fill(col("pos", 0), 0.0)
    fill(A("sums"), 0.0)

    def score(out, gr, bias=0.0):
        act(out, A("ps", 16 * gr, 3585 + 16 * gr, 512), ACT.Abs, bias=bias)

    def mo(o, w):
        return A("mo", 8 * o + 7, 8 * (o + w), 8)

    def third(buf, k, o, w):
        return A(buf, 3 * o + k, 3 * (o + w), 3)

    def nb(o, w):
        return A("te", 2 * o + 2, 2 * (o + w) + 2, 2)

    def level(o, do, w):
        tt(nb(o, w + 1), mo(o, w + 1), mo(o + 1, w + 1), ALU.min)
        cp(vs, odd("mz", o + 1, w), mo(o + 2, w))
        scan(A("mo", 8 * do + 11, 8 * (do + w) + 8, 4), A("mz", 2 * o + 2, 2 * (o + w) + 2),
             A("te", 2 * o + 2, 2 * (o + w) + 2), 0.0, ALU.min, ALU.max)

    def twice(o, do, wo):
        tt(A("wm", wo, wo + 64), A("mo", 8 * o, 8 * o + 80, ind=A("lw", 16, 20)), A("ww", wo, wo + 64), ALU.max)
        scan(A("mo", 8 * do + 8, 8 * do + 72), A("c8", wo, wo + 64), A("wm", wo, wo + 64), 0.0, ALU.max, ALU.min)

    def back(o, w):
        tt(third("t3", 1, o, w), nb(o - 2, w), mo(o, w), ALU.is_le)
        tt(third("t3", 2, o, w), mo(o - 1, w), nb(o, w), ALU.is_le)
        scan(A("tau", 3 * o, 3 * (o + w)), A("c3", 0, 3 * w), A("t3", 3 * o, 3 * (o + w)), 0.0, ALU.mult, ALU.add)

    def back2(o, w):
        for k in range(2):
            cp(vs, third("v3", 2 - k, o, w), third("t3", 1 + k, o - 20, w))
            tt(third("u3", 1 - k, o, w), third("tau", 2, o + k, w), third("tau", 2, o + k - 1, w), ALU.subtract)
        cp(vs, third("u3", 2, o, w), third("tau", 2, o - 1, w))
        scan(A("tau2", 3 * o, 3 * (o + w)), A("v3", 3 * o, 3 * (o + w)), A("u3", 3 * o, 3 * (o + w)), 0.0, ALU.mult,
             ALU.add)

    def back_last(o):
        tt(A("q1", 0, 28, 4), mo(o - 1, 7), mo(o + 1, 7), ALU.is_le)
        tt(A("q1", 1, 28, 4), mo(o - 2, 7), mo(o, 7), ALU.is_gt)
        tt(A("q1", 2, 28, 4), mo(o - 2, 7), mo(o, 7), ALU.is_le)
        tt(A("q0", 2, 28, 4), mo(o - 1, 7), mo(o, 7), ALU.is_le)
        scan(A("q2"), A("q0"), A("q1"), 0.0, ALU.mult, ALU.add)

    def borders(buf, w, lo_, hi_, to_left, to_right, cast):
        mv_, lands = [], []
        for k in nbs:
            if k < r:
                mv_.append((A(buf[0], lo_, lo_ + w[r], cast=cast), A(buf[1], to_left, to_left + w[r], cast=cast), [k]))
                lands.append(A(buf[1], to_right - w[k], to_right))
            else:
                mv_.append((A(buf[0], hi_ - w[r], hi_, cast=cast), A(buf[1], to_right - w[r], to_right, cast=cast), [k]))
                lands.append(A(buf[1], to_left, to_left + w[k]))
        return mv_, lands

    def firsts(t, src, o):
        zq = "zq%d" % t
        pick(zq, B0 + S, S, src, 128, A("l48", 6, 9) if o else A("l48", 0, 3))
        for nm, cast, rs, ls_ in (("", u8, "af", "sf"), ("s", None, "ag", "sg")):
            m1, l1 = borders((src + nm, zq + nm), [8, 12, 12, 8], o, o + S, B0 + 2 * S, B0 + S, cast)
            remote(m1, "%s%d" % (rs, t), "%s%d" % (ls_, t), l1, sum(share(k) for k in nbs), HOP + (0 if t else FIRST))

    both = len(nbs) == 2
    rot = (16, 12, 8, 16)[r]
    pieces = ((0, 20), (20, 34), (34, 48)) if both else ((0, 16), (16, 32), (32, 48)) if r == 0 else (
        (16, 32), (32, 48), (0, 16))
    if both and not DM:
        rot, pieces = 17, (((6, 24), (24, 48), (0, 6)), ((10, 28), (28, 48), (0, 10)))[r - 1]
    if both:
        quant("bq", 64 * (2 - r), 64 * (2 - r) + 128, "zer", 0)

    for b in range(4):
        mm(b, "eq", 128 * b, "tq", T0, 128)
        cp(vs, A("ft", b, 4 * S, 4), ps(b, 0, S))
    quant("fq", 0, 128, "ft", 0)
    firsts(0, "fq", 0)

    for t in range(R):
        zq, cl = "zq%d" % t, "cl%d" % t
        stage[0] = "round"
        seen.clear()
        for l in range(L - 1, -1, -1):
            mm(l, "tq", T0 + 48 * l - sh, "uq", 0, 128)
        score(mo(1, 8), 0, kc("eb"))
        score(mo(11, 8), 7)
        for o, gr in ((0, 1), (1, 6), (2, 2), (3, 5), (4, 3), (5, 4), (6, 4), (10, 6)):
            score(odd("te", 10 * o + 1, 8), gr)
        for o in range(2):
            score(A("ee", 16 * o + 1, 16 * o + 9), 4 + 2 * o)
            score(A("c8", 64 * o + 7, 64 * o + 64, 8), 5 + 2 * o)
        for b in range(4):
            mm(b, "eq", 128 * b, "tq", T0, 384)
        for b in range(4):
            for c0 in (0, 192):
                cp("s", A("fb", PW * b + c0, PW * b + c0 + 192), ps(b, c0, c0 + 192))
        for o in (0, 20, 40):
            level(o, o + 20, 18)
        for x in range(3):
            tt(A("tc", 8 * x, 8 * x + 8), mo(60 + x, 8), mo(71, 8), ALU.max)
        for a, b, w in ((0, 0, 64), (64, 32, 32), (96, 0, 32)) if r in (0, 3) else ((0, 32, 32), (32, 0, 32), (64, 0, 64)):
            scan(A(cl, 32 * r + 8, 32 * r + 32, 1, a, a + w), A("tc", 0, 24, 1, b, b + w), A("flo", 0, 24, 1, b, b + w),
                 BIG, ALU.min, ALU.max)
        cost = [col(cl, 32 * k + 31) for k in range(N)]
        remote([(cost[r], cost[r], others)], "ak%d" % t, "sk%d" % t, [cost[k] for k in others],
               sum(len(topo.engines(T.cores[k], core)) for k in others), HOP + 300)
        tt(A("ee", 32, 57), A("ee", 0, 25), A("ee", 1, 26), ALU.min)
        cp(vs, A("ww"), A("ee", ind=A("lw", 0, 8)))
        twice(60, 100, 0)
        twice(100, 120, 64)
        scan(A("mc"), mo(121, 8), mo(121, 8), BIG, ALU.min, ALU.min)
        level(60, 80, 8)
        level(100, 110, 8)
        tt(nb(80, 9), mo(80, 9), mo(81, 9), ALU.min)
        for o, w in ((2, 28), (42, 28), (82, 28)):
            back(o, w)
        back_last(112)
        for o, w in ((22, 47), (102, 7)):
            back2(o, w)
        act(A("dump", 56, 64), A("mc"), ACT.Sign, bias=col("mc", 7), scale=-1.0, accum=col("acc", 7))
        for gr, to in ((7, 6), (6, 4), (6, 5), (4, 2), (4, 3), (2, 0), (2, 1)):
            o = [2, 22, 42, 62, 82, 102, 112][gr - 1]
            act(A("dump", 8 * to, 8 * to + 7),
                A("q2", 3, 28, 4) if gr == 7 else third("tau2" if gr - to == 2 else "tau", 2, o, 7), ACT.Sign,
                bias=col("acc", gr), scale=1.0 if gr == 7 else 2.0, accum=col("acc", to))
        for gr in range(7, -1, -1):
            aff(vs, A("st", 64 * gr, 64 * gr + 64), A("sp"), col("acc", gr), 0.0)
        quant("sq", 0, 128, "st", 0)
        mm(4, "sq", 0, "mq", 0, 128)
        for m_ in range(3):
            aff("v", col("lv", m_), ps(4, 48 + m_, 49 + m_), kc("al48"), col("w5", m_))
        mm(5, "sq", 0, "mq", 0, 128)
        act(A("oa", 0, 48), ps(5, 0, S), ACT.Sign, kc("ns"), kc("al"))
        act(A("oa", 96, 144), ps(5, 0, S), ACT.Abs, kc("at"), kc("al"))
        act(A("oa", 48, 96), A("oa", 96, 144), ACT.Relu, kc("w2"), kc("-w2"))
        if t == R - 1:
            aff("v", A("prow", 0, S), ps(4, 0, S), kc("al"), kc("be"))
        for b in range(4):
            cp(vs, A("vt", b, 192, 4), A("fb", PW * b, PW * b + 384, ind=A("lv", 0, 3)))
            if t:
                cp(vs, A("vt", 4 * S + b, 8 * S, 4), A("fb", PW * b, PW * b + S))
        quant("vcq", 0, 128, "vt", 0)
        if t:
            firsts(t, "vcq", S)
        for b in range(4):
            mm(4 + (b + 2) % 4, "wq", 128 * b, "vcq", 0, 128)
        for b in range(4):
            relu(vs, A("fb", PW * b + 384, PW * b + 432), ps(4 + (b + 2) % 4, 0, 48), 0.03125)
        tt(third("la", 1, 0, S), A("oa", 0, 48), A("oa", 48, 96), ALU.add)
        aff(vs, third("lb", 1, 0, S), A("oa", 0, 48), -24.0, kc("sb"))
        if t == R - 1:
            aff(vs, A("o8"), A("io1", 0, 48), 8.0, 0.0)
            tt(A("olb"), A("prow", 0, 48), A("o8"), ALU.add)
            for gr in range(8):
                dma("y", T.ol[gr:gr + 1, :], A("olb", 0, 48, 1, 16 * gr, 16 * gr + 1), "dol")
        for i, k in enumerate(others + [r]):
            aff(vs, A("inr", 64 * i, 64 * i + 64), A("kt", 64 * i, 64 * i + 64), cost[k], 0.0)
        keys = [r] + [k for k in others if (k > 0 if upper else k < N - 1)]
        for i, k in enumerate(keys):
            aff(vs, col("key", i), cost[k], col("km", k), col("key", 0) if i == 1 else 0.0)
        for o, w in ((96, 32), (0, 96)):
            tr(A("row", o, o + w), A("inr", 2 * o, 2 * (o + w), 2))
            tr(A("row", 128 + o, 128 + o + w, 1, 64, 128), A("inr", 2 * o + 1, 2 * (o + w), 2, 0, 64))
            tr(A("row", 128 + o, 128 + o + w, 1, 0, 64), A("inr", 2 * o + 1, 2 * (o + w), 2, 64, 128))
        ts(A("cmp", 0, 256), A("row"), col("key", 1), ALU.subtract, col("key", 2), ALU.is_lt)
        scan(A("cnt"), A("cmp"), A("zer", 0, 288), 0.0, ALU.add, ALU.add)
        for a in range(4):
            o = 32 * blk[a] - kb
            tr(A("fone", o, o + 32, 1, 0, 32), A("cnt", 256, 288, 1, 32 * a, 32 * a + 32))
        o = S * r - kb
        for a in range(4):
            ts(A("lb", 0, 144, 3, 32 * a, 32 * a + 32), A("fone", o, o + S, 1, 0, 32), 96.0, ALU.is_ge, 48.0, ALU.mult)
        for a in range(2):
            ts(A("fd", 0, 128, 1, 32 * a, 32 * a + 32), A("fone", 0, 128, 1, 0, 32), 96.0, ALU.is_ge, 0.25, ALU.mult)
        scan(A("lo_"), A("la"), A("lb"), 0.0, ALU.mult, ALU.add)
        cp("v", A("lz", 0, rot), third("lo_", 2, S - rot, rot))
        cp("v", A("lz", rot, S), third("lo_", 2, 0, S - rot))
        for a, b_ in pieces:
            for b in range(2):
                cp(vs, A("zt", 32 * a + b, 32 * b_, 2), A("fb", PW * b, PW * (b + 3), ind=A("lz", a, b_)))
        if both and not DM:
            quant("bq", 96 - 8 * (rot - pieces[0][0]), 96 + 8 * (pieces[0][1] - rot), "zt", 32 * pieces[0][0])
            quant(zq, Z0 + C - 8 * rot, Z0 + C, "zt", 0)
            quant(zq, Z0, Z0 + C - 8 * rot, "zt", 32 * rot)
        elif both:
            low = 160 - 8 * rot
            quant("bq", 96 - 8 * rot, 96 + low, "zt", 0)
            quant(zq, Z0 + low, Z0 + C - 8 * rot, "zt", 640)
            for nm, cast in (("", u8), ("s", None)):
                dma("y", A(zq + nm, Z0 + C - 8 * rot, Z0 + C, cast=cast), A("bq" + nm, 96 - 8 * rot, 96, cast=cast),
                    "dh%s%d" % (nm, t))
                dma("y", A(zq + nm, Z0, Z0 + low, cast=cast), A("bq" + nm, 96, 96 + low, cast=cast), "dl%s%d" % (nm, t))
        else:
            quant(zq, Z0 + C - 8 * rot, Z0 + C, "zt", 0)
            for a, b_ in ((0, 128), (128, 256)) if r == N - 1 else ((0, C - 8 * rot),):
                quant(zq, Z0 + a, Z0 + b_, "zt", 32 * rot + 4 * a)
        for nm, cast, rs, ls_ in (("", u8, "ac", "sc"), ("s", None, "as", "ss")):
            if both:
                m1, l1 = borders(("bq" + nm, zq + nm), [56, 88, 88, 56], 96, 96, Z0 + C, Z0, cast)
            else:
                m1, l1 = borders((zq + nm, zq + nm), [56, 88, 88, 56], Z0, Z0 + C, Z0 + C, Z0, cast)
            remote(m1, "%s%d" % (rs, t), "%s%d" % (ls_, t), l1, sum(share(k) for k in nbs), HOP + (200 if nm else 450))
        e_ = 128 if upper else i0 + n
        scan(A("pos", 1, 1 + e_), A("c78", 0, e_), A("fd", 0, e_), 0.0, ALU.add, ALU.add)
        aff(vs, A("t7", 0, n), A("fd", i0, i0 + n), kc("ta"), kc("tb"))
        tt(A("th", 0, n), A("pos", i0, i0 + n), A("t7", 0, n), ALU.add)
        lo_ = "lo"
        if upper:
            lo_ = "lu"
            ts(A("lu"), A("lo"), col("pos", 128), ALU.add, kc("-sc"), ALU.mult)
            ts(kc("p8"), col("pos", i0), col("pos", 128), ALU.subtract, -8.0, ALU.mult)
        else:
            aff(vs, kc("p8"), col("pos", i0), -8.0, 0.0)
        aff(vs, A("dk", 0, 24), A("dk", 96, 120), 1.0, kc("p8"))
        ts(A("dk", 24, 48), A("dk", 120, 144), kc("p8"), ALU.subtract)
        for m_ in range(6):
            act(A("cl", 68 * m_, 68 * m_ + n), A("th", 0, n), ACT.Relu, col(lo_, m_), kc("sc"), col("rs", m_))
        tt(A("sums", 0, 3), A("rs", 0, 3), A("rs", 3, 6), ALU.subtract)
        for a, b in ((0, 32), (32, 0)):
            tt(A("sums", 3, 6, 1, a, a + 32), A("rs", 0, 3, 1, b, b + 32), A("rs", 3, 6, 1, b, b + 32), ALU.subtract)
        tt(A("xr"), A("sums", ind=A("ls")), A("dk", 0, 96), ALU.subtract)
        c1, c4, da, db = [A("xr", 24 * i, 24 * i + 24) for i in range(4)]
        tt(A("mm5", 0, 48, 2), da, db, ALU.subtract)
        tt(A("mm5", 49, 96, 2), c4, da, ALU.add)
        tt(A("mm5", 1, 48, 2), da, c1, ALU.subtract)
        scan(A("mm5", 96, 144), A("mm5", 48, 96), A("mm5", 0, 48), 0.0, ALU.mult, ALU.add)
        if t == R - 1:
            break
        for a in (0, 64):
            cp("v", A("lm", 0, 24, 1, a, a + 64), A("mm5", 97, 144, 2, 0, 64))
        for c0, w in PARTS:
            pick("gq", c0, w, zq, ZC, A("lm", c0 // 16, (c0 + w) // 16))
        for c0, w in PARTS:
            for b in range(4):
                mm(7 - b, "wq", 128 * b, "gq", c0, w)
                mm(3 - b, "eq", 128 * b, "gq", c0, w)
            for b in range(4):
                o = 384 * b + c0
                relu("s", A("tmp", o, o + w), ps(7 - b, 0, w), 0.015625)
                tt(A("xt", 4 * c0 + b, 4 * (c0 + w), 4), ps(3 - b, 0, w), A("tmp", o, o + w), ALU.add)
            quant("tq", T0 + c0, T0 + c0 + w, "xt", 4 * c0)

    stage[0] = "end"
    for m_ in range(3):
        c0, c1 = 128 * m_, 128 * m_ + 128
        for a in (0, 64):
            cp("v", A("lm", 8 * m_, 8 * m_ + 8, 1, a, a + 64), A("mm5", 97 + 2 * m_, 144, 6, 0, 64))
        pick("gq", c0, 128, zq, ZC, A("lm", 8 * m_, 8 * m_ + 8))
        cp("v", A("tl", c0, c1, cast=dt.uint32), A("gq", c0, c1, ind=A("lf"), cast=dt.uint32))
        cp(vs, A("tls", c0, c1), A("gqs", c0, c1, ind=A("lf")))
        for b in range(4):
            mm(7 - 2 * b, "wq", 128 * b, "tl", c0, 128)
            mm(6 - 2 * b, "eq", 128 * b, "tl", c0, 128)
        for b in range(4):
            o = 384 * b + c0
            relu("s", A("tmp", o, o + 128), ps(7 - 2 * b, 0, 128), 0.015625)
            tt(A("xt", 4 * c0 + b, 4 * c1, 4), ps(6 - 2 * b, 0, 128), A("tmp", o, o + 128), ALU.add)
        quant("tf", c0, c1, "xt", 4 * c0)
        dma("y", T.oc[:, 4 * c0:4 * c1], A("tf", c0, c1, cast=u8), "doc")
    for m_ in range(3):
        c0, c1 = 128 * m_, 128 * m_ + 128
        mm(7 - 2 * m_, "vq", 0, "tf", c0, 128)
        cp(vs, A("ysb", c0, c1), ps(7 - 2 * m_, 0, 128))
        dma("y", T.y[:, c0:c1], A("ysb", c0, c1), "dy")
    for k in range(4):
        dma("sy"[k % 2], T.osc[4 * k:4 * k + 4, :], A("tfs", 0, 384, 1, 32 * k, 32 * k + 4), "dos")

    return ops


def rank_program(g, core, T, topo):
    r = T.rank_of(core)
    if r is None:
        return
    if not PLAN:
        ranks, starts = [calls(k, T, topo) for k in range(N)], [[{} for k in range(N)] for seed in range(STARTS)]
        for seed, found in enumerate(starts):
            plan(ranks, ALONE, EARLY, found, SEED + seed)
        PLAN.extend(plan(ranks, TRIES, EARLY, min(starts, key=lambda f: f[0]["best"]), SEED + STARTS))
    eng = {"v": g.vector, "s": g.scalar, "p": g.tensor, "g": g, "y": g.sync}
    ops = calls(r, T, topo)
    count, known, mark = {}, {q: {} for q in eng}, {}
    for i, q in PLAN[r]:
        o = ops[i]
        sem = o["sem"] or COUNTER[q]
        count[sem] = count.get(sem, 0) + o["inc"]
        if q == "x":
            mark[i] = (sem, count[sem], {sem: count[sem]}, len(mark))
            continue
        k = known[q]
        for s_, v_, clock, at in sorted((mark[j] for j in o["hard"]), key=lambda x: -x[3]):
            if k.get(s_, 0) < v_:
                eng[q].wait_ge(T.sem[s_], v_)
                for s2, v2 in clock.items():
                    k[s2] = max(k.get(s2, 0), v2)
        call = o["fns"][q](eng[q])
        if o["chain"]:
            call.then_inc(T.sem[sem], o["inc"])
        clock = dict(k)
        clock[sem] = count[sem]
        mark[i] = (sem, count[sem], clock, len(mark))
    for s_, v_ in count.items():
        g.wait_ge(T.sem[s_], v_)
